import numpy as np, ml_dtypes
CORES = [9,25,41,57]
N = 4
BF = ml_dtypes.bfloat16
def gentries(a):
    return np.ascontiguousarray(a.reshape(8, 16, -1).transpose(0, 2, 1)).reshape(8, -1)
def gtable(e):
    e = np.asarray(e); return np.ascontiguousarray(e.reshape(8, -1, 16).transpose(0, 2, 1)).reshape(128, -1).astype(np.int32)
V, R, L, ST, MF, SL, Q, TH = 4096, 1024, 256, 5, 6, 64, 2, 1330
def pairs(rng):
    a = rng.integers(0, R, (N, 8, L)); b = rng.integers(0, R, (N, 8, L))
    K = np.where(rng.random((N, 8, 1, L)) < 0.5, np.argsort(rng.random((N, 8, 16, L)), axis=2), rng.integers(0, 16, (N, 8, 16, L)))
    return a, b, K, rng.integers(0, 256, (N, 8, 16, L))
def pack(X, P, a, b, K, z, th):
    return {"ph": X.reshape(N, 128, V).astype(np.float32).astype(BF), "rp": np.ascontiguousarray(P.reshape(N, 128, R)).astype(np.int32),
            "av": np.stack([gtable(v) for v in a]), "bv": np.stack([gtable(v) for v in b]), "kc": np.ascontiguousarray(K.reshape(N, 128, L)).astype(np.int32),
            "zs": z.reshape(N, 128, L).astype(np.float32).astype(BF), "th": np.ascontiguousarray(th.reshape(N, 128, 1)).astype(np.int32)}
def camps(rng, M):
    h = V // 2; o = np.argsort(rng.random((N, 8, V)), axis=-1); side = np.zeros((N, 8, V), bool); np.put_along_axis(side, o[..., h:], True, 2)
    X = np.where(side[:, :, None], rng.integers(200, 256, (N, 8, 16, V)), rng.integers(0, 41, (N, 8, 16, V)))
    cl = np.broadcast_to(np.argsort(rng.random((M, 8, R)), axis=-1) & 3, (N, 8, R))
    up = np.argsort(rng.random((N, 8, 16, R)), axis=2) < np.array([0, 16, MF, MF + 1])[cl][:, :, None]
    pk = rng.integers(0, h, (N, 8, 16 * R))
    P = np.where(up, np.take_along_axis(o[..., h:2 * h], pk, 2).reshape(N, 8, 16, R), np.take_along_axis(o[..., :h], pk, 2).reshape(N, 8, 16, R))
    return X, P, np.argsort(cl, axis=-1, kind="stable")
def of(rng, birds, c):
    return np.take_along_axis(birds, c * (R // 4) + rng.integers(0, R // 4, c.shape), 2)
def setup_inputs(rng):
    a, b, K, z = pairs(rng)
    th = TH + 20 * rng.permutation(8)[None, :, None, None] + rng.integers(0, 40, (N, 8, 16, 1))
    return pack(rng.integers(0, 256, (N, 8, 16, V)), rng.integers(0, V, (N, 8, 16, R)), a, b, K, z, th)
def setup_inputs_spread(rng):
    a, b, K, z = pairs(rng)
    X = (np.exp2(8 * rng.random((N, 8, 1, V))) * rng.random((N, 8, 16, V))).astype(np.int64)
    z = (np.exp2(8 * rng.random((N, 8, 1, L))) * rng.random((N, 8, 16, L))).astype(np.int64)
    P = (V * rng.random((N, 8, 16, R)) ** 3).astype(np.int64); P[:, 1::2] = V - 1 - P[:, 1::2]
    a = (R * rng.random((N, 8, L)) ** 2).astype(np.int64); b = R - 1 - (R * rng.random((N, 8, L)) ** 3).astype(np.int64)
    K[:, ::2] = (16 * rng.random((N, 4, 16, L)) ** 2).astype(np.int64)
    th = np.minimum(4064, np.exp2(6 + 5 * rng.random((1, 8, 1, 1)) + rng.random((N, 8, 16, 1))).astype(np.int64))
    return pack(X, P, a, b, K, z, th)
def setup_inputs_ends(rng):
    s = 255 * rng.integers(0, 2, (N, 8, 1))
    kx = rng.integers(0, 3, (N, 8, 1, V)); X = np.where(kx < 2, 255 * kx, 255 * rng.integers(0, 2, (N, 8, 16, V))); X[..., 0] = s; X[..., V - 1] = 255 - s
    kz = rng.integers(0, 3, (N, 8, 1, L)); z = np.where(kz < 2, 255 * kz, 255 * rng.integers(0, 2, (N, 8, 16, L)))
    kp = rng.integers(0, 4, (N, 8, 1, R))
    P = np.where(kp < 2, (V - 1) * kp, np.where(kp == 2, (V - 1) * rng.integers(0, 2, (N, 8, 16, R)), rng.integers(0, V, (N, 8, 16, R))))
    P[..., 0] = (V - 1) * (np.argsort(rng.random((N, 8, 16)), axis=2) < rng.choice(np.array([MF, MF + 1, 3, 9]), (N, 8, 1)))
    P[..., 1] = V - 1; P[..., R - 1] = 0
    a, b = [np.where(rng.random((N, 8, L)) < 0.75, (R - 1) * rng.integers(0, 2, (N, 8, L)), rng.integers(0, R, (N, 8, L))) for i in range(2)]
    K = 15 * rng.integers(0, 2, (N, 8, 16, L)); th = 4064 * rng.integers(0, 2, (N, 8, 16, 1))
    e = np.array([0, 7, L - 1]); a[:, :, e] = R - 1; b[:, :, e] = R - 1; z[:, :, :, e] = (255 - s)[..., None]
    a[:, :, L - 2] = R - 1; b[:, :, L - 2] = 1
    return pack(X, P, a, b, K, z, th)
def setup_inputs_corners(rng):
    X, P, birds = camps(rng, N); a, b, K, z = pairs(rng); sh = int(rng.integers(0, 8))
    least = np.roll(np.array([SL, SL - 1, SL + 1, 0, L, 1, SL, L - 1]), sh); even = np.roll(np.arange(8) == 6, sh)
    C = least + ((L - least + 1) * rng.random((N, 8))).astype(np.int64); C[rng.integers(0, N, 8), np.arange(8)] = least; C = np.where(even, SL, C)
    kd = rng.integers(0, 3, (N, 8, 1)); ln = np.arange(L)
    div = np.argsort(np.argsort(np.where(kd == 0, rng.random((N, 8, L)), np.where(kd == 1, ln, -ln)), axis=-1), axis=-1) < C[..., None]
    s = rng.integers(0, 3, (N, 8, L))
    a = of(rng, birds, np.where(div, np.array([3, 1, 0])[s], np.array([0, 1, 2])[s])); b = of(rng, birds, np.where(div, np.array([0, 0, 1])[s], np.array([0, 1, 0])[s]))
    m = rng.integers(0, 6, (N, 8, 1, L)); row = np.arange(16)[:, None]
    K = np.where(m == 0, row, np.where(m == 1, 0, np.where(m == 2, 15, np.where(m == 3, 15 - row, K))))
    return pack(X, P, a, b, K, z, rng.integers(900, 2501, (N, 8, 16, 1)))
def setup_inputs_crowd(rng):
    X, P, birds = camps(rng, 1); a, b, K, z = pairs(rng); ln = np.arange(L)
    o = rng.permutation(np.array([0, 1, 2, 3, 6, 7])); p = int(rng.choice(np.array([0, 4, 6])))
    md = np.concatenate([o[:p], np.array([5, 4]), o[p:]])[None, :, None]
    two = np.take_along_axis(birds, (rng.integers(0, R // 4, (N, 8, 1)) + np.arange(2)) & (R // 4 - 1), 2)
    other = ((md == 1) & (ln == 0)) | ((md == 2) & (ln == L - 1)); same = (md < 3) | (md == 6)
    b = np.where(same, np.where(other, two[..., 1:], two[..., :1]), np.where(md == 3, np.take_along_axis(two, rng.integers(0, 2, (N, 8, L)), 2), np.where(md == 7, b, of(rng, birds, np.zeros((N, 8, L), np.int64)))))
    lone = ln == rng.integers(0, L, (N, 8, 1))
    high = (md == 4) | ((md == 5) & ~lone) | ((md == 6) & (ln < L // 2)) | ((md == 3) & (rng.random((N, 8, L)) < 0.5))
    a = np.where(md == 7, a, of(rng, birds, high.astype(np.int64)))
    K = np.where(same[:, :, None], rng.integers(0, 16, (N, 8, 1, 1)), K)
    th = np.where(md[:, :, None] < 3, 4064, rng.integers(900, 2501, (N, 8, 16, 1)))
    odd = (np.arange(N) & 1)[:, None, None] == 1; sure = (np.argsort(rng.random((N, 8, 16)), axis=2) < MF + 1)[..., None]
    near = ((md == 4) | ((md == 5) & odd))[:, :, None] & ~sure
    th = np.where(near, 4 * rng.integers(810, 851, (N, 8, 16, 1)) - rng.integers(0, 2, (N, 8, 16, 1)), th)
    return pack(X, P, a, b, K, z, th)
def setup_inputs_ties(rng):
    a, b, K, z = pairs(rng); pal = np.array([0, 60, 120, 120, 120, 120, 180, 180]); row = np.arange(16)[:, None]
    X = rng.choice(pal, (N, 8, 1, V)) + ((rng.random((N, 8, 1, V)) < 0.3) & (row == rng.integers(0, 16, (N, 8, 1, V))))
    z = rng.choice(pal, (N, 8, 1, L)) + ((rng.random((N, 8, 1, L)) < 0.3) & (row == rng.integers(0, 16, (N, 8, 1, L))))
    P = rng.integers(0, V, (N, 8, 16, R)); P[:, 1::2, 8:] = P[:, 1::2, :8]
    b = np.where(rng.random((N, 8, L)) < 0.3, a, b); a[:, :, 0] = 0; b[:, :, 0] = R - 1; a[:, :, L - 1] = R - 1; b[:, :, L - 1] = R - 1
    K = np.where(rng.random((N, 8, 1, L)) < 0.2, row, K); h = L // 2
    for v in (a, b, K, z): v[:, 2::3, ..., h:] = v[:, 2::3, ..., :h]
    th = 960 - rng.integers(-1, 33, (N, 8, 16, 1))
    Y, W, birds = camps(rng, 1); s = np.array([3, 4, 6]); lo = rng.integers(0, 156, (N, 8, 16, 1)); up = rng.integers(40, 100, (N, 8, 16, 1))
    rest = birds[0, 6, R // 4 + R // 128:]; W[:, 6][:, :, rest] = W[:, 6][:, :, birds[0, 6, rng.integers(0, R // 4, len(rest))]]
    cnt = (np.arange(N)[:, None] + rng.integers(0, 4, 3)) & 3; cnt[:, 1] = 1 + (np.arange(N) + int(rng.integers(0, 3))) % 3
    e = np.ones((N, 3), np.int64); e[:, 1] = cnt[:, 1] + rng.integers(0, 2, N); e[:, 2] = rng.integers(1, 4, N)
    hot = np.argsort(rng.random((N, 3, L)), axis=-1) < cnt[..., None]
    warm = np.take_along_axis(birds, R // 4 + rng.integers(0, R // 128, (N, 8, L)), 2); calm = of(rng, birds, np.zeros((N, 8, L), np.int64))
    X[:, s] = (lo + up * (Y[:, :, :1] >= 200))[:, s]; P[:, s] = W[:, s]; z[:, s] = rng.integers(0, 256, (N, 3, 16, L))
    a[:, s] = np.where(hot, warm[:, s], calm[:, s]); b[:, s] = of(rng, birds, np.zeros((N, 8, L), np.int64))[:, s]
    th[:, s] = np.add.reduce(up, axis=2, keepdims=True)[:, s] - e[:, :, None, None]
    return pack(X, P, a, b, K, z, th)
def check_inputs(d):
    bad = []
    for k, lo, hi in (("ph", 0, 255), ("rp", 0, V - 1), ("av", 0, R - 1), ("bv", 0, R - 1), ("kc", 0, 15), ("zs", 0, 255), ("th", 0, 4064)):
        v = np.asarray(d[k]).astype(np.float64)
        if not (np.min(v) >= lo and np.max(v) <= hi): bad.append("range of " + k)
        elif np.any(v != np.floor(v)): bad.append("whole numbers in " + k)
    return bad
def reference(ph, rp, av, bv, kc, zs, th):
    X = ph.astype(np.int32).reshape(N, 8, 16, V); P = rp.astype(np.int64).reshape(N, 8, 16, R); lim = th.astype(np.int64).reshape(N, 8, 16, 1)
    a = np.stack([gentries(v) for v in av]).astype(np.int64); b = np.stack([gentries(v) for v in bv]).astype(np.int64)
    K = kc.astype(np.int64).reshape(N, 8, 16, L); z = zs.astype(np.int32).reshape(N, 8, 16, L); A = np.zeros((N, 8), np.int64)
    wt = (2 * np.arange(16) + 1)[:, None]
    for t in range(ST):
        if t > 0: a, b, K, z = [np.roll(v, 1, axis=0) for v in (a, b, K, z)]
        ra = np.take_along_axis(P, a[:, :, None], 3); rb = np.take_along_axis(P, b[:, :, None], 3)
        x = np.take_along_axis(X, ra.reshape(N, 8, 1, 16 * L), 3).reshape(N, 8, 16, 16, L)
        y = np.take_along_axis(X, rb.reshape(N, 8, 1, 16 * L), 3).reshape(N, 8, 16, 16, L)
        w = np.take_along_axis(y, K[:, :, None], 3)
        d = np.add.reduce(np.abs(x - w), axis=2)
        mis = d > lim + (A & 31)[:, :, None, None]
        div = np.add.reduce(mis.astype(np.int64), axis=2) > MF
        k = np.argmin(np.add.reduce(np.abs(x - z[:, :, :, None]), axis=2), axis=2)
        xk = np.take_along_axis(x, k[:, :, None, None], 3)[:, :, :, 0]; wk = np.take_along_axis(w, k[:, :, None, None], 3)[:, :, :, 0]
        c = np.take_along_axis(rb, np.take_along_axis(K, k[:, :, None], 2), 2)[:, :, 0]
        half = (xk + wk) >> 1
        for h in range(N):
            for g in range(8):
                m = np.flatnonzero(~div[h, g]); col, first = np.unique(c[h, g, m], return_index=True)
                X[h, g][:, col] = half[h, g][:, m[first]]
        zn = np.where(div[:, :, None], (z + x[:, :, :, 0]) >> 1, np.abs(z - wk))
        an = np.where(div, a, (5 * a + np.add.reduce(zn * wt, axis=2)) & (R - 1))
        A = np.add.reduce(div.astype(np.int64), axis=2); n = np.minimum(SL, np.minimum.reduce(A, axis=0))
        bn = np.array(b); Kn = np.array(K)
        for h in range(N):
            q = (h + Q) % N
            for g in range(8):
                me = np.flatnonzero(div[h, g])[:n[g]]; mate = np.flatnonzero(div[q, g])[:n[g]]
                bn[h, g, me] = b[q, g, mate]; own = K[h, g][:, me]
                Kn[h, g][:, me] = np.where(mis[h, g][:, me], np.take_along_axis(K[q, g][:, mate], own, 0), own)
        a, b, K, z = an, bn, Kn, zn
    return {"yx": X.reshape(N, 128, V).astype(np.float32).astype(BF), "yk": K.reshape(N, 128, L).astype(np.float32).astype(BF),
            "ya": np.stack([gtable(v) for v in a]).astype(np.float32), "yb": np.stack([gtable(v) for v in b]).astype(np.float32), "yz": z.reshape(N, 128, L).astype(np.float32).astype(BF)}

@@ -1,0 +1,654 @@
+from concourse.bass import DstId, RemoteDMATransfer
+from concourse.mybir import dt, AluOpType, AxisListType, ActivationFunctionType
+
+ST = 5
+NR = 4
+KBW = 640
+PKW = 272
+BF, F32, I32, U16, F16 = "bfloat16", "float32", "int32", "uint16", "float16"
+
+SCRATCH = {}
+
+
+def _s(name, cols, d):
+    SCRATCH[name] = ("sbuf", [128, cols], d)
+
+
+for _n, _c, _d in [
+    ("X", 4112, BF), ("P", 1024, I32), ("XY", 8192, BF), ("DF", 4096, BF), ("AB", 4096, BF), ("MX", 4096, BF),
+    ("KB", KBW * ST, BF), ("aU", 16, U16), ("aS", 16 * ST, F32), ("zb", 256 * ST, BF), ("zS", 256 * ST, BF),
+    ("pkS", PKW * ST, BF), ("pkO", PKW * ST, BF), ("pkM", PKW * ST, BF), ("pkA", 8 * (ST + 2), BF),
+    ("avI", 16, I32), ("bvI", 16, I32), ("kcI", 256, I32), ("thI", 4, I32),
+    ("ra", 256, U16), ("rb", 256, U16), ("rb16", 256, F16), ("wo", 256, U16), ("bU", 16, U16), ("bF", 16, F32),
+    ("kT", 256, F32), ("kS", 256, F32), ("r16", 16, F32), ("low", 16, F32), ("ZT", 256, BF), ("ZB", 256, BF),
+    ("vF", 32, F32), ("vU", 32, U16), ("xw", 512, BF), ("T16", 256, F16), ("cS", 256, F32), ("cR", 256, F32),
+    ("eq", 256, BF), ("ZW", 512, BF), ("half", 256, BF), ("uS", 256, F32), ("a5", 16, F32), ("aF", 16 * ST, F32),
+    ("amI", 16, I32), ("amJ", 16, I32), ("da", 16, F32), ("mis", 272, BF), ("dvS", 256, BF), ("pref", 256, BF),
+    ("cm", 256, BF), ("bS", 256, F32), ("nS", 256, F32), ("f1", 16, F32), ("f2", 16, F32), ("offU", 32, U16),
+    ("dl", 16, F32), ("t2", 16, F32), ("aN", 16, F32), ("s1", 16, F32), ("s2", 16, F32), ("slU", 16, U16),
+    ("acc", 4, F32), ("posU", 4, U16), ("junk", 1024, BF), ("AI", 4, I32), ("AJ", 4, I32), ("nth", 4, F32), ("thF", 4, F32),
+    ("n1", 4, F32), ("n2", 4, F32), ("g1", 4, F32), ("g2", 4, F32), ("g3", 4, F32), ("spU", 4, U16),
+    ("CL", 1024, BF), ("k1", 64, F32), ("k2", 64, BF),
+    ("ZC", 128, BF), ("hJ", 32, I32), ("hl", 32, BF), ("hm", 512, BF),
+    ("io", 4, I32), ("ia", 4, I32), ("col", 16, F32), ("ones", 256, BF), ("Id", 128, BF), ("nId", 128, BF), ("hId", 128, BF),
+    ("sId", 128, BF), ("xId", 128, BF), ("mId", 128, BF), ("I16", 128, F16), ("BO", 128, BF), ("BO16", 128, F16), ("BOs", 128, BF),
+    ("Wu", 128, BF), ("WT", 128, BF), ("WC", 128, BF), ("U64", 144, BF), ("Un32", 144, BF), ("Vs", 640, BF),
+    ("SEL", 2048, BF), ("tri", 256, BF), ("cmk", 256, BF), ("R1", 256, BF), ("R2", 256, BF), ("R3", 256, BF), ("dg", 256, BF),
+    ("kc16", 256, F16), ("q25", 256, BF), ("wc", 256, BF), ("tI", 256, F32), ("tJ", 160, F32),
+    ("vC", 32, F32), ("lC", 16, F32), ("bcF", 48, F32), ("bcU", 48, U16), ("jC", 12, F32), ("pw", 16, F32),
+]:
+    _s(_n, _c, _d)
+for _b in range(8):
+    SCRATCH["B%d" % _b] = ("psum", [128, 512], F32)
+
+SEMAPHORES = ["sV", "sS", "sP", "sG", "sent", "out"] + ["ld%d" % i for i in range(8)]
+for _t in range(ST):
+    SEMAPHORES += ["rK%d" % _t, "ra%d" % _t, "rz%d" % _t, "rO%d" % _t, "rM%d" % _t, "rA%d" % _t]
+
+PAR = {"g": 1.56, "sc": 3.8, "pe": 0.7, "fix": 60, "hop": 110, "self": 60, "rem": 1200, "lat": 2600, "slack": 60, "any": True}
+PAR.update({
+    "relu": (0, 0, 0, 0), "kv": 8, "sub": 2,
+    "eng": {'x0': 'VS', 'x1': 'S', 'x2': 'VS', 'x3': 'S', 'y0': 'S', 'y1': 'S', 'y2': 'S', 'y3': 'S', 'x0@0': 'S', 'x1@0': 'VS', 'x2@0': 'S'},
+    "tpl": "Xm x0 y0 T16 pref eq x3 mx11 zS k2 km8 df1_1 df2_1 df0_1 df3_0 k1 mx14 vU K g2 mx10 n2 ra bU Bd ZT0 mx2 aU df1_0 mx8 mx9 x1 mx12 rb kx1 wo ZT1 km12 x2 mx4 posU uS mx3 junk3 kS nS junk2 km6 nth slU vF mx5 ab3 dl km2 cR topkA km0 mx7 cS mx6 g1 r16 km10 zd km4 kx3 kT CL0 spU mis kx0 df0_0 toaS zm dvS km14 pkM y1 ab0 y2 amI mx13 mx0 da f2 half aS amJ g3 df2_0 ZB kx2 t2 low ab1 CL1 junk0 xw cm offU bS pkA rb16 topkK n1 s2 pkK df3_1 pkB f1 junk1 a5 AJ AI mx1 toK ab2 tozS pkp mx15 y3",
+    "tplL": "kS x3 df2_1 mx2 df0_1 k2 y0 x1 ZT0 low km0 Bd df1_1 n2 km12 bU pref x0 x2 k1 mx9 mx10 wo vU mx11 mx5 mx12 km10 kT CL0 g2 mx0 K df3_0 aU kx1 CL1 f2 offU mx6 kx2 ra zd mx7 r16 df2_0 mx4 zm pkM g1 n1 nth junk0 df0_0 spU g3 km8 Xm mx14 toaS rb cS y1 kx3 dvS y2 uS mx3 km2 T16 ab0 ZB junk3 df1_0 aS cm mx8 df3_1 y3 ZT1 zS slU junk2 da kx0 km6 ab1 ab2 t2 amI toK rb16 dl pkA bS topkA mx13 topkK cR eq nS km4 mis posU pkp km14 xw pkB f1 s2 AJ mx1 ab3 mx15 tozS junk1 AI a5 half vF amJ pkK",
+})
+NCH = 4
+CH = 256 // NCH
+A = AluOpType
+AF = ActivationFunctionType
+
+
+def build(g, core, T, topo, par):
+    rank = T.rank_of(core)
+    ops = []
+    cur = [-1]
+    last_w, readers, bank_last = {}, {}, {}
+    V, S, PE, SY = g.vector, g.scalar, g.tensor, g.sync
+
+    def op(alts, reads, writes, banks=(), ext=(), after=(), lat=0, sem=None, semn=1):
+        i = len(ops)
+        deps = {}
+        for k in reads:
+            if k in last_w:
+                deps[last_w[k]] = "raw"
+        for k in writes:
+            if k in last_w:
+                deps.setdefault(last_w[k], "ww")
+            for r in readers.get(k, ()):
+                deps.setdefault(r, "ww")
+        for b in banks:
+            for r in bank_last.get(b, ()):
+                deps.setdefault(r, "bank")
+        for a in after:
+            deps.setdefault(a, "far")
+        for k in reads:
+            readers.setdefault(k, []).append(i)
+        for k in writes:
+            last_w[k] = i
+            readers[k] = []
+        for b in banks:
+            e = list(alts)[0]
+            prev = bank_last.get(b, [])
+            if prev and list(ops[prev[-1]]["alts"])[0] == e:
+                bank_last[b] = prev + [i]
+            else:
+                bank_last[b] = [i]
+        deps.pop(i, None)
+        ops.append({"alts": alts, "deps": deps, "ext": list(ext), "lat": lat, "sem": sem, "semn": semn,
+                    "nm": (list(writes) + ["to" + "".join(reads)[:4]])[0], "t": cur[0]})
+        return i
+
+    def cv(n, half=False):
+        return max(64, n * (0.5 if half else 1.0)) + par["fix"] * 0.5
+
+    def vts(out, in0, s1, s2, o0, o1, n, R, W, banks=(), half=False, ext=(), after=()):
+        if o1 is None:
+            f = lambda: V.tensor_scalar(out, in0, s1, None, o0)
+        else:
+            f = lambda: V.tensor_scalar(out, in0, s1, s2, o0, o1)
+        return op({"V": (cv(n, half), f)}, R, W, banks, ext, after)
+
+    def vtt(out, in0, in1, o, n, R, W, banks=(), ext=(), after=()):
+        return op({"V": (cv(n if banks else 2 * n), lambda: V.tensor_tensor(out, in0, in1, o))}, R, W, banks, ext, after)
+
+    def vcp(out, in_, n, R, W, banks=(), half=False, ext=(), after=()):
+        return op({"V": (cv(n, half), lambda: V.tensor_copy(out, in_))}, R, W, banks, ext, after)
+
+    def vscan(out, d0, d1, init, o0, o1, n, R, W, banks=(), half=False):
+        return op({"V": (cv(n, half), lambda: V.tensor_tensor_scan(out, d0, d1, init, o0, o1))}, R, W, banks)
+
+    def vset(ap, val, n, W):
+        return op({"V": (cv(n, True), lambda: V.memset(ap, val))}, [], W)
+
+    def act(out, in_, f, n, R, W, banks=(), bias=None, scale=None, accum=None, gather=False, ext=(), after=()):
+        kw = {}
+        if bias is not None:
+            kw["bias"] = bias
+        if scale is not None:
+            kw["scale"] = scale
+        if accum is not None:
+            kw["accum_out"] = accum
+        c = n * par["g"] + 80 if gather else cv(n) + 20
+        return op({"S": (c, lambda: S.activation(out, in_, f, **kw))}, R, W, banks, ext, after)
+
+    def gath(out, win, off, n, R, W, engs="VS", ext=(), after=()):
+        alts = {}
+        if "V" in engs:
+            alts["V"] = (n * par["g"] + 60, lambda: V.tensor_copy(out, win.indirect(off)))
+        if "S" in engs:
+            alts["S"] = (n * par["g"] + 80, lambda: S.activation(out, win.indirect(off), AF.Copy))
+        return op(alts, R, W, (), ext, after)
+
+    def gtt(out, win, off, in1, o, n, R, W):
+        return op({"V": (n * par["g"] + 60, lambda: V.tensor_tensor(out, win.indirect(off), in1, o))}, R, W)
+
+    def scat(win, off, in_, n, R, W, ext=(), after=()):
+        return op({"V": (n * par["sc"] + 60, lambda: V.tensor_copy(win.indirect(off), in_))}, R, W, (), ext, after)
+
+    def mm(lst, R, W, bank, start, stop, ext=(), after=(), nm=""):
+        c = sum(max(64, m[3]) for m in lst) * par["pe"] + 30
+
+        def f():
+            r = None
+            for j, m in enumerate(lst):
+                r = PE.matmul(m[0], m[1], m[2], start and j == 0, stop and j == len(lst) - 1)
+            return r
+        i = op({"P": (c, f)}, R, W, () if bank is None else (bank,), ext, after)
+        if bank is not None:
+            ops[i]["nm"] = W[0] + "<" + R[-1].rstrip("0123456789" if R[-1][0] in "KBzp" else "") + nm
+        return i
+
+    def pool(c, f, R, W):
+        return op({"G": (c, f)}, R, W)
+
+    def dma(q, out, in_, R, W, sem, lat):
+        e = {"Y": SY, "S": S}[q]
+        return op({q: (60, lambda: e.dma_start(out, in_))}, R, W, lat=lat, sem=sem, semn=16)
+
+    nsent = [0]
+
+    def send(items, R, lat):
+        def f():
+            if len(items) == 1:
+                o, src, dst, sem = items[0]
+                d = T.cores[(rank + o) % NR]
+                rid, pid, _ = topo.addr(d)
+                return g.remote_dma(dst, src, T.sem[sem], T.sem.sent, pid, rid, topo.mask(core, d))
+            tr = []
+            for j, (o, src, dst, sem) in enumerate(items):
+                d = T.cores[(rank + o) % NR]
+                rid, pid, _ = topo.addr(d)
+                en = topo.engines(core, d)
+                per = len(en) // len(items)
+                m = 0
+                for e in en[j * per:(j + 1) * per]:
+                    m |= 1 << e
+                tr.append(RemoteDMATransfer(dst_ids=[DstId(rid=rid, pnc=pid)], dma_engine_mask=m, remote_sem=T.sem[sem], src=src, dst=dst))
+            return g.remote_dma_fused(tr, local_sem=T.sem.sent)
+        nsent[0] += NE
+        return op({"G": (par["rem"], f)}, R, [], lat=lat, sem="none")
+
+    NE = len(topo.engines(core, T.cores[(rank + 1) % NR]))
+    B = [T["B%d" % i] for i in range(8)]
+    allx = ["x%d" % c for c in range(NCH)]
+    ally = ["y%d" % c for c in range(NCH)]
+
+    dma("Y", T.avI[:], T.av[:], [], ["avI"], "ld0", 2200)
+    dma("Y", T.P[:], T.rp[:], [], ["P"], "ld1", 4500)
+    dma("S", T.X[:, 0:4096], T.ph[:], [], ["Xm"], "ld2", 7000)
+    dma("Y", T.bvI[:], T.bv[:], [], ["bvI"], "ld3", 2500)
+    dma("Y", T.kcI[:], T.kc[:], [], ["kcI"], "ld4", 5000)
+    dma("Y", T.zb[:, 0:256], T.zs[:], [], ["z0"], "ld5", 5000)
+    op({"G": (300, lambda: g.dma_start(T.thI[:, 0:1], T.th[:], allow_slow_non_contiguous=True))}, [], ["thI"], lat=3000, sem="ld6", semn=16)
+
+    def iota(out, pat, base, cm, n, W, fl=True):
+        if fl:
+            return pool(160 + 2 * n, lambda: g.iota(out, pat, base, cm, allow_small_or_imprecise_dtypes=True), [], W)
+        return pool(160 + 2 * n, lambda: g.iota(out, pat, base, cm), [], W)
+
+    col = T.col
+    iota(T["io"][:, 0:1], [[0, 1]], 0, 1, 1, ["io"], False)
+    iota(T.tJ[:], [[1, 160]], -16, -1, 160, ["tJ"])
+    iota(T.tI[:], [[0, 16], [1, 16]], 0, 0, 256, ["tI"])
+    vts(T.ia[:, 0:1], T["io"][:, 0:1], 15, None, A.bitwise_and, None, 1, ["io"], ["ia0"])
+    vts(T.ia[:, 1:2], T["io"][:, 0:1], 16, None, A.bitwise_and, None, 1, ["io"], ["ia1"])
+    vcp(col[:, 0:2], T.ia[:, 0:2], 2, ["ia0", "ia1"], ["c0"])
+    r_ = col[:, 0:1]
+    vts(col[:, 2:3], r_, -1.0, -1.0, A.mult, A.add, 1, ["c0"], ["c2"])
+    vts(T.U64[:], T.tJ[:, 0:144], col[:, 2:3], 64.0, A.is_equal, A.mult, 144, ["tJ", "c2"], ["U64"])
+    vts(T.Un32[:], T.U64[:], -0.5, None, A.mult, None, 144, ["U64"], ["Un32"], half=True)
+    vts(T.Id[:], T.tJ[:, 16:144], 0.0, None, A.is_equal, None, 128, ["tJ"], ["Id"])
+    for nm, w in (("nId", -1.0), ("hId", 0.5), ("sId", 0.0625), ("xId", 16.0), ("mId", -16.0), ("I16", 1.0)):
+        vts(T[nm][:], T.Id[:], w, None, A.mult, None, 128, ["Id"], [nm], half=True)
+
+    def DG(U, k):
+        return T[U][:, 15 - k:143 - k]
+    vts(T.cS[:, 0:128], T.tJ[:, 16:144], r_, -7.5, A.add, A.add, 128, ["tJ", "c0"], ["cS"])
+    vtt(T.cR[:, 0:128], T.cS[:, 0:128], T.cS[:, 0:128], A.mult, 128, ["cS"], ["cR"])
+    vts(T.BO[:], T.cR[:, 0:128], 60.0, None, A.is_lt, None, 128, ["cR"], ["BO"])
+    vts(T.BO16[:], T.BO[:], 1.0, None, A.mult, None, 128, ["BO"], ["BO16"], half=True)
+    vts(T.BOs[:], T.BO[:], 0.0625, None, A.mult, None, 128, ["BO"], ["BOs"], half=True)
+    KV = par["kv"]
+    if KV > 0:
+        vts(T.kT[:, 0:128], T.tI[:, 0:128], float(KV), -32.0, A.is_lt, A.mult, 128, ["tI"], ["kT"])
+        vtt(T.ZC[:], T.kT[:, 0:128], T.BO[:], A.mult, 128, ["kT", "BO"], ["ZC"])
+    vts(col[:, 3:4], r_, 2.0, 1.0, A.mult, A.add, 1, ["c0"], ["c3"])
+    vts(T.Wu[:], T.BO[:], col[:, 3:4], None, A.mult, None, 128, ["BO", "c3"], ["Wu"], half=True)
+    vts(col[:, 4:5], r_, 1.0, 65536.0, A.is_equal, A.mult, 1, ["c0"], ["c4"])
+    vts(col[:, 5:6], r_, 2.0, 2048.0, A.is_equal, A.mult, 1, ["c0"], ["c5"])
+    vtt(col[:, 6:7], col[:, 4:5], col[:, 5:6], A.add, 1, ["c4", "c5"], ["c6"])
+    vts(T.WC[:], T.BO[:], col[:, 6:7], None, A.mult, None, 128, ["BO", "c6"], ["WC"], half=True)
+    vts(T.uS[:, 0:128], T.tI[:, 0:128], 2.0, -15.0, A.mult, A.add, 128, ["tI"], ["uS"])
+    vts(T.nS[:, 0:128], T.uS[:, 0:128], col[:, 5:6], col[:, 4:5], A.mult, A.subtract, 128, ["uS", "c5", "c4"], ["nS"])
+    vtt(T.WT[:], T.nS[:, 0:128], T.BO[:], A.mult, 128, ["nS", "BO"], ["WT"])
+    vts(col[:, 7:8], col[:, 1:2], 0.0, None, A.is_equal, None, 1, ["c0"], ["c7"])
+    vts(col[:, 8:9], col[:, 1:2], 0.0625, None, A.mult, None, 1, ["c0"], ["c8"])
+    vts(col[:, 9:11], col[:, 7:9], 16.0, None, A.mult, None, 2, ["c7", "c8"], ["c9"])
+    for j in range(4):
+        vts(T.Vs[:, 160 * j:160 * j + 160], T.tJ[:], 0.0, col[:, 7 + j:8 + j], A.is_equal, A.mult, 160, ["tJ", "c7", "c8", "c9"], ["Vs%d" % j])
+
+    def SW(h, g2, big):
+        o = 160 * (h + 2 * big) + 16 - 16 * (g2 - h)
+        return T.Vs[:, o:o + 128]
+    vts(T.tri[:], T.tI[:], r_, 8192.0, A.is_gt, A.mult, 256, ["tI", "c0"], ["tri"])
+    vts(T.cmk[:], T.tri[:], 1.1875, 16.0, A.max, A.min, 256, ["tri"], ["cmk"], half=True)
+    vts(T.R2[:], T.tI[:], r_, 1048576.0, A.is_le, A.mult, 256, ["tI", "c0"], ["R2"])
+    vts(T.R1[:], T.tI[:], 0.0, 1048576.0, A.is_equal, A.mult, 256, ["tI"], ["R1"])
+    vts(T.R3[:], T.tI[:], 0.0, 2.0, A.not_equal, A.mult, 256, ["tI"], ["R3"])
+    vts(T.dg[:], T.tI[:], r_, None, A.is_equal, None, 256, ["tI", "c0"], ["dg"])
+    vscan(T.pw[:], T.R3[:, 0:16], T.dg[:, 0:16], 0.0, A.mult, A.add, 16, ["R3", "dg"], ["pw"])
+    vset(T.ones[:], 1.0, 256, ["ones"])
+    vset(T.q25[:], -0.25, 256, ["q25"])
+    vts(col[:, 11:12], r_, -8.46875, None, A.add, None, 1, ["c0"], ["c11"])
+    vts(T.kc16[:], T.ones[:], col[:, 11:12], None, A.mult, None, 256, ["ones", "c11"], ["kc16"], half=True)
+    vts(col[:, 12:13], r_, 4096.0, None, A.add, None, 1, ["c0"], ["c12"])
+    NSUB = par["sub"]
+    DCH = CH // NSUB
+    iota(T.wc[:], [[0, 256 // DCH], [16, DCH]], 0, 0, 256, ["wc"])
+    iota(T.bcF[:, 0:16], [[16, 16]], 15, 0, 16, ["bc0"])
+    iota(T.bcF[:, 16:48], [[1, 32]], 0, 0, 32, ["bc1"])
+    vcp(T.bcU[:], T.bcF[:], 48, ["bc0", "bc1"], ["bcU"])
+    vts(T.lC[:], T.bcF[:, 0:16], r_, -15.0, A.add, A.add, 16, ["bc0", "c0"], ["lC"])
+    vts(T.vC[:, 0:16], T.lC[:], 16.0, 8.0, A.mult, A.add, 16, ["lC"], ["vC0"])
+    vts(T.vC[:, 16:32], T.lC[:], 16.0, 4103.5, A.mult, A.add, 16, ["lC"], ["vC1"])
+    vts(T.jC[:, 0:4], T.lC[:, 0:4], 2.0, 1.0, A.mult, A.add, 4, ["lC"], ["jC0"])
+    vts(T.jC[:, 4:8], T.lC[:, 0:4], -2.0, -1.0, A.mult, A.add, 4, ["lC"], ["jC1"])
+    vts(T.jC[:, 8:12], T.lC[:, 0:4], 256.0, None, A.add, None, 4, ["lC"], ["jC2"])
+    vset(T.ZT[:], 0.0, 256, ["ZT0", "ZT1", "ZT2"])
+    vset(T.ZT[:, 2:256:16], 1.0, 16, ["ZT2"])
+    vset(T.X[:, 4096:4112], 0.0, 16, ["Xd"])
+    vset(T.mis[:, 256:272], 0.0, 16, ["misd"])
+    for t in range(ST):
+        vset(T.pkS[:, PKW * t + 128:PKW * t + 136], 0.0, 8, ["pkp%d" % t])
+    vts(col[:, 15:16], r_, 16.0, None, A.mult, None, 1, ["c0"], ["c15"])
+    vset(T.KB[:, 256:320], 0.0, 64, ["Kd0"])
+    for t in range(ST):
+        vset(T.KB[:, KBW * t + 576:KBW * t + 640], 0.0, 64, ["Be%d" % t])
+    vset(T.SEL[:], 1.0, 2048, ["SEL"])
+    pool(4300, lambda: g.affine_select(T.SEL[:], T.SEL[:], [[1, 16], [16, 8], [0, 16]], A.is_equal, 0.0, 0, -1), ["SEL"], ["SEL"])
+
+    vcp(T.aF[:, 0:16], T.avI[:], 16, ["avI"], ["a0"])
+    vts(T.s1[:], T.lC[:], 2.0, None, A.mult, None, 16, ["lC"], ["s1"])
+    vcp(T.bU[:], T.bvI[:], 16, ["bvI"], ["bU"])
+    vcp(T.KB[:, 0:256], T.kcI[:], 256, ["kcI"], ["K0"])
+    vts(T.thF[:, 0:1], T.thI[:, 0:1], -1.0, -0.5, A.mult, A.add, 1, ["thI"], ["thF"])
+    vcp(T.nth[:, 0:1], T.thF[:, 0:1], 1, ["thF"], ["nth"])
+    vts(T.hJ[:, 0:16], T.bvI[:], 992, None, A.bitwise_and, None, 16, ["bvI"], ["hJ0"])
+    vts(T.hJ[:, 16:32], T.bvI[:], 31, None, A.bitwise_and, None, 16, ["bvI"], ["hJ1"])
+    vcp(T.hl[:], T.hJ[:], 32, ["hJ0", "hJ1"], ["hl"])
+    for j in range(2):
+        gtt(T.hm[:, 256 * j:256 * j + 256], T.hl[:, 0:32], T.bcU[:, 16 + 16 * j:32 + 16 * j], T.dg[:], A.mult, 256, ["hl", "bcU", "dg"], ["hm%d" % j])
+    mm([(B[7][:, 0:256], DG("U64", 0), T.hm[:, 0:256], 256), (B[7][:, 0:256], DG("U64", 1), T.hm[:, 256:512], 256)],
+       ["hm0", "hm1", "U64"], ["b7"], 7, True, True)
+    act(T.KB[:, 320:576], B[7][:, 0:256], AF.Copy, 256, ["b7"], ["Bd0"], (7,), scale=1.0 / 64)
+
+    M32 = 1.5 * 2 ** 28
+    M1 = 1.5 * 2 ** 23
+    snd = {}
+
+    def patch(t, tk, last):
+        ko = KBW * tk
+        own = PKW * t
+        if last:
+            o, m = T.pkS, T.pkM
+            oR = lambda a: ["pk%s%d" % (a, t)]
+            oE, oA = [], []
+            mE, mA = [("rM%d" % t, NE)], [snd["P", t]]
+            aE, aA = [("rA%d" % t, NE // 2), ("rO%d" % t, NE // 2)], [snd["A", t]]
+            c1, c2 = T.pkA[:, 8 * t + 7:8 * t + 8], T.pkA[:, 8 * t + 15:8 * t + 16]
+            kE, kA = [], []
+        else:
+            o, m = T.pkO, T.pkM
+            oR = lambda a: []
+            oE, oA = [("rO%d" % t, NE // 2)], [snd["P", t]]
+            mE, mA = [("rM%d" % t, NE // 2)], [snd["P", t]]
+            aE, aA = [("rA%d" % t, NE)] + oE, [snd["A", t]] + oA
+            c1, c2 = T.pkA[:, 8 * t + 7:8 * t + 8], T.pkO[:, own + 143:own + 144]
+            kE, kA = [("rK%d" % tk, NE)], [snd["K", t]]
+        vts(T.n1[:, 0:1], T.pkS[:, own + 143:own + 144], c1, c2, A.min, A.min, 1, ["pkA%d" % t], ["n1"], ext=aE, after=aA)
+        vts(T.n2[:, 0:1], T.n1[:, 0:1], m[:, own + 143:own + 144], 128.0, A.min, A.min, 1, ["n1"], ["n2"], ext=mE, after=mA)
+        vts(T.g1[:], T.jC[:, 0:4], T.n2[:, 0:1], 512.0, A.is_gt, A.mult, 4, ["jC0", "n2"], ["g1"])
+        vtt(T.g2[:], T.g1[:], o[:, own + 128:own + 132], A.add, 4, ["g1"] + oR("p"), ["g2"], ext=oE, after=oA)
+        vtt(T.g3[:], T.g2[:], T.jC[:, 8:12], A.min, 4, ["g2", "jC2"], ["g3"])
+        vcp(T.spU[:], T.g3[:], 4, ["g3"], ["spU"])
+        Ko, Km = o[:, own + 64:own + 128], m[:, own + 208:own + 272]
+        for hb in range(2):
+            bk = 3 + hb
+            lst = []
+            for j in range(8):
+                lst.append((B[bk][:, 64 * j:64 * j + 64], T.mId[:], Ko, 64))
+                mi = 8 * hb + j
+                lst.append((B[bk][:, 64 * j:64 * j + 64], T.SEL[:, 128 * mi:128 * mi + 128], Km, 64))
+            mm(lst, ["mId", "SEL"] + oR("K"), ["b%d" % bk], bk, True, True, ext=oE + mE, after=oA + mA)
+            vts(T.CL[:, 512 * hb:512 * hb + 512], B[bk][:], 0.0, 16.0, A.max, A.min, 512, ["b%d" % bk], ["CL%d" % hb], (bk,))
+        mm([(B[6][:, 0:64], T.xId[:], Ko, 64), (B[6][:, 0:64], T.nId[:], Ko, 64)] +
+           [(B[6][:, 0:64], T.Id[:], T.CL[:, 64 * j:64 * j + 64], 64) for j in range(8)],
+           ["xId", "nId", "Id", "CL0"] + oR("K"), ["b6"], 6, True, False, ext=oE, after=oA)
+        mm([(B[6][:, 0:64], T.Id[:], T.CL[:, 64 * j:64 * j + 64], 64) for j in range(8, 16)], ["CL1"], ["b6"], 6, False, True)
+        act(T.k1[:], B[6][:, 0:64], AF.Identity, 64, ["b6", "c13"], ["k1"], (6,), bias=col[:, 13:14])
+        vtt(T.k1[:], T.k1[:], o[:, own:own + 64], A.mult, 64, ["k1"] + oR("M"), ["k1"], ext=oE, after=oA)
+        vtt(T.k2[:], T.k1[:], Ko, A.add, 64, ["k1"] + oR("K"), ["k2"])
+        scat(T.KB[:, ko + 320:ko + 640], T.spU[:], m[:, own + 144:own + 208], 64, ["spU", "Be%d" % tk], ["Bd%d" % tk, "Be%d" % tk], ext=kE + mE, after=kA + mA)
+        scat(T.KB[:, ko:ko + 320], T.spU[:], T.k2[:], 64, ["spU", "k2"], ["K%d" % tk, "Kd%d" % tk], ext=kE, after=kA)
+        mm([(B[6][:, 64:80], DG("U64", j), T.KB[:, ko + 320 + j:ko + 576:16], 16) for j in range(16)], ["U64", "Bd%d" % tk], ["b6b"], 6, True, True)
+
+    vset(col[:, 13:14], -240.0, 1, ["c13"])
+
+    for t in range(ST):
+        last = t == ST - 1
+        cur[0] = t
+        ko = KBW * t
+        K = T.KB[:, ko:ko + 256]
+        z = T.zb[:, 256 * t:256 * t + 256]
+        aF = T.aF[:, 16 * t:16 * t + 16]
+        aR, zR = (["a0"], ["z0"]) if t == 0 else ([], [])
+        aE, aA = ([], []) if t == 0 else ([("ra%d" % t, NE)], [snd["a", t - 1]])
+        zE, zA = ([], []) if t == 0 else ([("rz%d" % t, NE)], [snd["z", t - 1]])
+        Xr = ["Xm", "Xd"]
+        vcp(T.aU[:], aF, 16, aR, ["aU"], ext=aE, after=aA)
+        gath(T.ra[:], T.P[:], T.aU[:], 256, ["P", "aU"], ["ra"], "V")
+        act(T.a5[:], aF, AF.Copy, 16, aR, ["a5"], scale=5.0, ext=aE, after=aA)
+        for c in range(NCH):
+            gath(T.XY[:, 16 * CH * c:16 * CH * (c + 1)], T.X[:, 0:4096], T.ra[:, CH * c:CH * (c + 1)], 16 * CH, ["ra"] + Xr, ["x%d" % c])
+        mm([(B[1][:, 0:256], T.I16[:], T.kc16[:], 256)], ["I16", "kc16"], ["b1", "b1s"], 1, True, False)
+        parts = []
+        if KV > 0:
+            mm([(B[2][:, 0:256], T.Id[:], z, 256)], ["Id"] + zR, ["b2"], 2, True, True, zE, zA)
+            mm([(B[1][:, 0:256], T.ZC[:], z, 256)], ["ZC", "b1s"] + zR, ["kz"], None, False, False, zE, zA)
+            parts.append("kz")
+            for c in range(NCH):
+                mm([(B[1][:, CH * c:CH * (c + 1)], DG("Un32", j), T.XY[:, 16 * CH * c + j:16 * CH * (c + 1):16], CH) for j in range(KV)],
+                   ["Un32", "b1s", "x%d" % c], ["kx%d" % c], None, False, False)
+                parts.append("kx%d" % c)
+        for k in range(0, 16, 2):
+            if k < KV:
+                for j in (k, k + 1):
+                    vtt(T.MX[:, 256 * j:256 * j + 256], T.XY[:, j:4096:16], B[2][:, 0:256], A.max, 256, allx + ["b2"], ["mx%d" % j], (2,))
+            else:
+                bk = (0, 7, 2)[(k // 2) % (2 if KV else 3)]
+                mm([m for j in (0, 1) for m in ((B[bk][:, 256 * j:256 * j + 256], T.nId[:], z, 256),
+                                                (B[bk][:, 256 * j:256 * j + 256], T.Id[:], T.XY[:, k + j:4096:16], 256))],
+                   zR + allx + ["Id", "nId"], ["b%d" % bk, "b%db" % bk], bk, True, True, zE, zA, nm=str(k))
+                act(T.MX[:, 256 * k:256 * k + 512], B[bk][:], AF.Abs, 512, ["b%d" % bk, "b%db" % bk], ["mx%d" % k, "mx%d" % (k + 1)], (bk,), scale=0.5)
+            mm([(B[1][:, 0:256], DG("U64", j), T.MX[:, 256 * j:256 * j + 256], 256) for j in (k, k + 1)],
+               ["U64", "b1s", "mx%d" % k, "mx%d" % (k + 1)], ["km%d" % k], None, False, False)
+            parts.append("km%d" % k)
+        mm([(B[5][:, 0:256], T.Id[:], T.q25[:], 256), (B[5][:, 0:256], T.hId[:], z, 256), (B[5][:, 0:256], T.hId[:], T.XY[:, 0:4096:16], 256)],
+           ["Id", "hId", "q25"] + allx + zR, ["b5"], 5, True, True, zE, zA)
+        vts(T.ZW[:, 1:512:2], B[5][:, 0:256], M1, M1, A.add, A.subtract, 256, ["b5"], ["zd"], (5,))
+        if t > 0:
+            patch(t - 1, t, False)
+            vts(T.bU[:], B[6][:, 64:80], 1.0 / 64, None, A.mult, None, 16, ["b6b"], ["bU"], (6,))
+        Kt, Bt = "K%d" % t, "Bd%d" % t
+        if not last:
+            snd["K", t] = send([(1, T.KB[:, ko:ko + 576], T.KB[:, ko + KBW:ko + KBW + 576], "rK%d" % (t + 1))], [Kt, Bt, "Kd%d" % t], par["lat"] + 2500)
+        gath(T.rb[:], T.P[:], T.bU[:], 256, ["P", "bU"], ["rb"], "V")
+        mm([(B[6][:, 256:512], T.Id[:], T.wc[:], 256), (B[6][:, 256:512], T.Id[:], K, 256)], ["Id", "wc", Kt], ["b6c"], 6, True, True)
+        vcp(T.wo[:], B[6][:, 256:512], 256, ["b6c"], ["wo"], (6,))
+        vts(T.rb16[:], T.rb[:], -2048.0, None, A.add, None, 256, ["rb"], ["rb16"], half=True)
+        for c in range(NCH):
+            gath(T.XY[:, 4096 + 16 * CH * c:4096 + 16 * CH * (c + 1)], T.X[:, 0:4096], T.rb[:, CH * c:CH * (c + 1)], 16 * CH, ["rb"] + Xr, ["y%d" % c])
+        mm([(B[1][:, 0:256], T.sId[:], K, 256)], ["sId", Kt] + parts, ["b1"], 1, False, True)
+        op({"V": (cv(256), lambda: V.transpose(T.kT[:], B[1][:, 0:256]))}, ["b1"], ["kT"], (1,))
+        vscan(T.kS[:], T.R1[:], T.kT[:], 0.0, A.add, A.min, 256, ["R1", "kT"], ["kS"])
+        k16 = T.kS[:, 15:256:16]
+        vts(T.r16[:], k16, M32, M32, A.add, A.subtract, 16, ["kS"], ["r16"])
+        vtt(T.low[:], k16, T.r16[:], A.subtract, 16, ["kS", "r16"], ["low"])
+        vts(T.ZT[:, 0:256:16], T.low[:], M1, M1, A.add, A.subtract, 16, ["low"], ["ZT0"])
+        vtt(T.ZT[:, 1:256:16], T.low[:], T.ZT[:, 0:256:16], A.subtract, 16, ["low", "ZT0"], ["ZT1"])
+        mm([(B[5][:, 256 + 16 * big + h:272 + 16 * big:2], SW(h, g2, big), T.ZT[:, 16 * g2 + big:256:32], 8)
+            for big in range(2) for h in range(2) for g2 in range(2)], ["ZT0", "ZT1", "Vs0", "Vs1", "Vs2", "Vs3"], ["b5v"], 5, True, True)
+        vtt(T.vF[:], B[5][:, 256:288], T.vC[:], A.add, 32, ["b5v", "vC0", "vC1"], ["vF"], (5,))
+        vcp(T.vU[:], T.vF[:], 32, ["vF"], ["vU"])
+        op({"V": (cv(256, True), lambda: V.transpose(T.ZB[:], T.ZT[:]))}, ["ZT0", "ZT1", "ZT2"], ["ZB"])
+        mm([(B[3][:, 0:256], T.I16[:], T.rb16[:], 256), (B[3][:, 0:256], T.WT[:], T.ZB[:], 256)], ["I16", "rb16", "WT", "ZB"], ["b3"], 3, True, True)
+        vts(T.T16[:], B[3][:, 0:256], -2048.0, 2048.0, A.max, A.min, 256, ["b3"], ["T16"], (3,))
+        mm([(B[4][:, 0:256], T.Id[:], T.tri[:], 256), (B[4][:, 0:256], T.WC[:], T.ZB[:], 256), (B[4][:, 0:256], T.BO16[:], T.T16[:], 256)],
+           ["Id", "tri", "WC", "ZB", "BO16", "T16"], ["b4"], 4, True, True)
+        vscan(T.cS[:], T.R2[:], B[4][:, 0:256], 0.0, A.add, A.min, 256, ["R2", "b4"], ["cS"], (4,))
+        act(T.cR[:], B[4][:, 0:256], AF.Copy, 256, ["b4"], ["cR"], (4,))
+        gtt(T.eq[:], T.cS[:], T.bcU[:, 0:16], T.cR[:], A.is_equal, 256, ["cS", "cR", "bcU"], ["eq"])
+        gath(T.xw[:], T.XY[:], T.vU[:], 512, ["vU"] + allx + ally, ["xw"], "S")
+        mm([(B[5][:, 0:256], T.Id[:], z, 256), (B[5][:, 0:256], T.nId[:], T.xw[:, 256:512], 256)], ["Id", "nId", "xw"] + zR, ["b5"], 5, True, True)
+        act(T.ZW[:, 0:512:2], B[5][:, 0:256], AF.Abs, 256, ["b5"], ["zm"], (5,))
+        mm([(B[6][:, 0:256], T.Id[:], T.q25[:], 256), (B[6][:, 0:256], T.hId[:], T.xw[:, 0:256], 256), (B[6][:, 0:256], T.hId[:], T.xw[:, 256:512], 256)],
+           ["Id", "hId", "q25", "xw"], ["b6", "b6b"], 6, True, True)
+        mm([(B[3][:, 256:512], T.xId[:], T.tri[:], 256), (B[3][:, 256:512], T.Wu[:], T.ZW[:, 0:512:2], 256)], ["xId", "tri", "Wu", "zm"], ["b3u"], 3, True, True)
+        vscan(T.uS[:], T.R2[:], B[3][:, 256:512], 0.0, A.add, A.min, 256, ["R2", "b3u"], ["uS"], (3,))
+        vtt(T.amI[:], T.uS[:, 15:256:16], T.a5[:], A.add, 16, ["uS", "a5"], ["amI"])
+        vts(T.amJ[:], T.amI[:], 1023, None, A.bitwise_and, None, 16, ["amI"], ["amJ"])
+        vtt(T.da[:], aF, T.amJ[:], A.subtract, 16, ["aU", "amJ"], ["da"])
+        vts(T.half[:], B[6][:, 0:256], M1, M1, A.add, A.subtract, 256, ["b6"], ["half"], (6,))
+        for c in range(NCH):
+            lo, hi = 16 * CH * c, 16 * CH * (c + 1)
+            for j in range(NSUB):
+                l0, l1 = CH * c + DCH * j, CH * c + DCH * (j + 1)
+                gtt(T.DF[:, 16 * l0:16 * l1], T.XY[:, 4096 + 16 * l0:4096 + 16 * l1], T.wo[:, l0:l1], T.XY[:, 16 * l0:16 * l1], A.subtract, 16 * DCH,
+                    ["x%d" % c, "y%d" % c, "wo"], ["df%d_%d" % (c, j)])
+            dfs = ["df%d_%d" % (c, j) for j in range(NSUB)]
+            out = B[0][:, CH * c:CH * (c + 1)]
+            if par["relu"][c]:
+                vts(T.AB[:, lo:hi], T.DF[:, lo:hi], 0.0, None, A.max, None, 16 * CH, dfs, ["ab%d" % c], half=True)
+                mm([(out, DG("Un32", k), T.DF[:, lo + k:hi:16], CH) for k in range(16)], ["Un32"] + dfs, ["b0"], 0, c == 0, False)
+                mm([(out, DG("U64", k), T.AB[:, lo + k:hi:16], CH) for k in range(16)], ["U64", "ab%d" % c], ["b0"], 0, False, c == NCH - 1)
+            else:
+                act(T.AB[:, lo:hi], T.DF[:, lo:hi], AF.Abs, 16 * CH, dfs, ["ab%d" % c], scale=0.5)
+                mm([(out, DG("U64", k), T.AB[:, lo + k:hi:16], CH) for k in range(16)], ["U64", "ab%d" % c], ["b0"], 0, c == 0, c == NCH - 1)
+        mm([(B[7][:, 0:256], T.Id[:], T.cmk[:], 256)], ["Id", "cmk"], ["b7"], 7, True, False)
+        act(T.mis[:, 0:256], B[0][:, 0:256], AF.Sign, 256, ["b0", "nth"], ["mis"], (0,), bias=T.nth[:, 0:1], scale=1.0 / 32)
+        mm([(B[7][:, 0:256], T.BOs[:], T.mis[:, 0:256], 256)], ["BOs", "mis"], ["b7"], 7, False, True)
+        mm([(B[0][:, 256:512], T.BOs[:], T.mis[:, 0:256], 256)], ["BOs", "mis"], ["b0b"], 0, True, True)
+        vscan(T.nS[:], T.R2[:], B[7][:, 0:256], 0.0, A.add, A.min, 256, ["R2", "b7"], ["nS"], (7,))
+        vts(T.dl[:], T.nS[:, 15:256:16], 1.0, None, A.is_gt, None, 16, ["nS"], ["dl"])
+        vtt(T.t2[:], T.dl[:], T.da[:], A.mult, 16, ["dl", "da"], ["t2"])
+        aS = T.aS[:, 16 * t:16 * t + 16]
+        vtt(aS, T.t2[:], T.amJ[:], A.add, 16, ["t2", "amJ"], ["aS%d" % t])
+        if not last:
+            snd["a", t] = send([(1, aS, T.aF[:, 16 * t + 16:16 * t + 32], "ra%d" % (t + 1))], ["aS%d" % t], par["lat"])
+        else:
+            dma("Y", T.ya[:], aS, ["aS%d" % t], [], "out", 2500)
+        act(T.dvS[:], B[0][:, 256:512], AF.Sign, 256, ["b0b", "c14"], ["dvS"], (0,), bias=col[:, 14:15])
+        vtt(T.cm[:], T.eq[:], B[7][:, 0:256], A.is_gt, 256, ["eq", "b7"], ["cm"], (7,))
+        vscan(T.bS[:], T.R3[:], T.cm[:], 0.0, A.mult, A.add, 256, ["R3", "cm"], ["bS"])
+        vts(T.f1[:], T.bS[:, 15:256:16], T.pw[:, 15:16], col[:, 12:13], A.not_equal, A.mult, 16, ["bS", "pw", "c12"], ["f1"])
+        vtt(T.f2[:], T.f1[:], T.cS[:, 15:256:16], A.max, 16, ["f1", "cS"], ["f2"])
+        vcp(T.offU[:, 0:32:2], T.f2[:], 16, ["f2"], ["offU"])
+        own = PKW * t
+        vscan(T.pref[:], T.ones[:], T.dvS[:], 0.0, A.add, A.add, 256, ["ones", "dvS"], ["pref"], half=True)
+        act(T.pkS[:, own + 136:own + 144], T.pref[:, 248:256], AF.Copy, 8, ["pref"], ["pkA%d" % t])
+        src = T.pkS[:, own + 136:own + 144]
+        if not last:
+            snd["A", t] = send([(2, src, T.pkA[:, 8 * t:8 * t + 8], "rA%d" % t)], ["pkA%d" % t], par["lat"])
+        else:
+            snd["A", t] = send([(1, src, T.pkA[:, 8 * t:8 * t + 8], "rA%d" % t), (3, src, T.pkA[:, 8 * t + 8:8 * t + 16], "rO%d" % t)], ["pkA%d" % t], par["lat"] + 600)
+        for j in range(4):
+            act(T.junk[:, 256 * j:256 * j + 256], T.pref[:], AF.Sign, 256, ["pref", "jC1"], ["junk%d" % j, "acc%d" % j], bias=T.jC[:, 4 + j:5 + j], accum=T.acc[:, j:j + 1])
+        accs = ["acc%d" % j for j in range(4)]
+        vts(T.posU[:], T.acc[:], -0.5, 128.0, A.mult, A.add, 4, accs, ["posU"])
+        act(T.pkS[:, own + 128:own + 132], T.acc[:], AF.Copy, 4, accs, ["pkp%d" % t], bias=128.0, scale=-0.5)
+        gath(T.pkS[:, own + 64:own + 128], T.KB[:, ko:ko + 320], T.posU[:], 64, ["posU", Kt, "Kd%d" % t], ["pkK%d" % t], "S")
+        gath(T.pkS[:, own + 144:own + 208], T.KB[:, ko + 320:ko + 640], T.posU[:], 64, ["posU", Bt, "Be%d" % t], ["pkB%d" % t], "S")
+        act(T.pkS[:, own + 208:own + 272], T.KB[:, ko:ko + 320].indirect(T.posU[:]), AF.Identity, 64, ["posU", Kt, "Kd%d" % t, "c15"], ["pkL%d" % t],
+            bias=col[:, 15:16], gather=True)
+        act(T.pkS[:, own:own + 64], T.mis[:].indirect(T.posU[:]), AF.Copy, 64, ["posU", "mis", "misd"], ["pkM%d" % t], bias=0.5, scale=0.5, gather=True)
+        sO, sM = T.pkS[:, own:own + 144], T.pkS[:, own + 128:own + 272]
+        pkR = ["pk%s%d" % (a, t) for a in ("BLpA" if last else "KMBLpA")]
+        if not last:
+            snd["P", t] = send([(1, sO, T.pkO[:, own:own + 144], "rO%d" % t), (3, sM, T.pkM[:, own + 128:own + 272], "rM%d" % t)], pkR, par["lat"] + 800)
+        else:
+            snd["P", t] = send([(2, sM, T.pkM[:, own + 128:own + 272], "rM%d" % t)], ["pkK"] + pkR, par["lat"] + 300)
+        vtt(T.s2[:], T.s1[:], T.dl[:], A.add, 16, ["s1", "dl"], ["s2"])
+        vcp(T.slU[:], T.s2[:], 16, ["s2"], ["slU"])
+        zS = T.zS[:, 256 * t:256 * t + 256]
+        gath(zS, T.ZW[:], T.slU[:], 256, ["slU", "zm", "zd"], ["zS%d" % t], "S")
+        if not last:
+            snd["z", t] = send([(1, zS, T.zb[:, 256 * t + 256:256 * t + 512], "rz%d" % (t + 1))], ["zS%d" % t], par["lat"] + 600)
+        else:
+            dma("Y", T.yz[:], zS, ["zS%d" % t], [], "out", 2500)
+        for lh in range(15, -1, -1):
+            scat(T.X[:], T.offU[:, 2 * lh:2 * lh + 1], T.half[:, 16 * lh:16 * lh + 16], 16, ["offU", "half"], Xr)
+        if not last:
+            vts(T.AI[:, 0:1], T.pref[:, 255:256], 0.5, None, A.mult, None, 1, ["pref"], ["AI"])
+            vts(T.AJ[:, 0:1], T.AI[:, 0:1], 31, None, A.bitwise_and, None, 1, ["AI"], ["AJ"])
+            vtt(T.nth[:, 0:1], T.thF[:, 0:1], T.AJ[:, 0:1], A.subtract, 1, ["thF", "AJ"], ["nth"])
+        else:
+            dma("Y", T.yx[:], T.X[:, 0:4096], Xr, [], "out", 7000)
+            patch(t, t, True)
+            act(T.bF[:], B[6][:, 64:80], AF.Copy, 16, ["b6b"], ["bF"], (6,), scale=1.0 / 64)
+            dma("S", T.yk[:], K, [Kt], [], "out", 2500)
+            dma("S", T.yb[:], T.bF[:], ["bF"], [], "out", 2500)
+    return ops, nsent[0]
+
+
+def schedule(ops, par):
+    n = len(ops)
+    succ = [[] for _ in range(n)]
+    for i, o in enumerate(ops):
+        for d in o["deps"]:
+            succ[d].append(i)
+    pr = [0.0] * n
+    for i in range(n - 1, -1, -1):
+        c = min(a[0] for a in ops[i]["alts"].values())
+        pr[i] = c + ops[i]["lat"] + max([pr[s] + par["hop"] for s in succ[i]] + [0.0])
+    kind_of = [o["nm"].rstrip("0123456789") if o["nm"][:2] in ("K0", "K1", "K2", "K3", "K4", "Bd", "aS", "zS", "pk", "to") else o["nm"] for o in ops]
+    rank_of = {k: j for j, k in enumerate(par["tpl"].split())}
+    rank_last = {k: j for j, k in enumerate(par["tplL"].split())}
+    for i in range(n - 1, -1, -1):
+        if ops[i]["t"] >= 0 and kind_of[i] in rank_of:
+            pr[i] = -(1000.0 * ops[i]["t"] + (rank_last if ops[i]["t"] == ST - 1 else rank_of)[kind_of[i]])
+        else:
+            pr[i] = max([pr[s] for s in succ[i]] + [-1e9]) + 0.001
+    left = [len(o["deps"]) for o in ops]
+    cand = [i for i in range(n) if left[i] == 0]
+    free = {}
+    eng, end, start = [None] * n, [0.0] * n, [0.0] * n
+    order = []
+    rdy = {}
+
+    def ready(i, e):
+        r = 0.0
+        for d, kind in ops[i]["deps"].items():
+            if eng[d] == e and ops[d]["lat"] == 0:
+                w = par["self"] if (kind != "bank" and e != "P") else 0.0
+            else:
+                w = par["hop"]
+            r = max(r, end[d] + w)
+        return r
+
+    while cand:
+        opts = []
+        for i in cand:
+            if i not in rdy:
+                es = list(ops[i]["alts"])
+                if len(es) > 1:
+                    es = par["eng"].get(kind_of[i] + "@%d" % ops[i]["t"], par["eng"].get(kind_of[i], "VS"))
+                rdy[i] = [(e, ready(i, e)) for e in es]
+            for e, r in rdy[i]:
+                opts.append((max(r, free[e][-1][1] if free.get(e) else 0.0), e, i))
+        s0, e0, _ = min(opts)
+        i = max((b[2] for b in opts if (b[1] == e0 or par["any"]) and b[0] <= s0 + par["slack"]), key=lambda c: (pr[c], -c))
+        alts = ops[i]["alts"]
+        es = [e for e, r in rdy[i]]
+        best = None
+        for e in es:
+            s, c = ready(i, e), alts[e][0]
+            busy = free.setdefault(e, [])
+            lo, hi = 0, len(busy)
+            while lo < hi:
+                mid = (lo + hi) // 2
+                if busy[mid][1] <= s:
+                    lo = mid + 1
+                else:
+                    hi = mid
+            while lo < len(busy) and busy[lo][0] < s + c:
+                s = max(s, busy[lo][1])
+                lo += 1
+            if best is None or s + c < best[0]:
+                best = (s + c, s, e, lo)
+        fin, s, e, lo = best
+        free[e].insert(lo, (s, fin))
+        eng[i], start[i] = e, s
+        end[i] = fin + ops[i]["lat"]
+        order.append(i)
+        cand.remove(i)
+        for j in succ[i]:
+            left[j] -= 1
+            if left[j] == 0:
+                cand.append(j)
+    order.sort(key=lambda c: (start[c], c))
+    return order, eng, start, end
+
+
+def rank_program(g, core, T, topo):
+    if T.rank_of(core) is None:
+        return
+    par = PAR
+    g.vector.memset(T.col[:, 14:15], 0.1875).then_inc(T.sem.sV, 1)
+    ops, nsent = build(g, core, T, topo, par)
+    order, eng, start, end = schedule(ops, par)
+    Q = {"V": g.vector, "S": g.scalar, "P": g.tensor, "G": g, "Y": g.sync}
+    cnt = {"sV": 1, "out": 0}
+    mark = {}
+    seen = {e: {} for e in Q}
+    allw = {}
+    need = set()
+    for i, o in enumerate(ops):
+        for d, kind in o["deps"].items():
+            if kind == "far" or ops[d]["sem"] == "none":
+                continue
+            if eng[d] == eng[i] and ops[d]["sem"] is None and (kind == "bank" or eng[i] == "P"):
+                continue
+            need.add((d, i))
+    raises = set(d for d, i in need)
+    g.scalar.wait_ge(T.sem.sV, 1)
+    seen["S"]["sV"] = 1
+    for i in order:
+        o, e = ops[i], eng[i]
+        waits = {}
+        for d in o["deps"]:
+            if (d, i) in need:
+                s, v = mark[d]
+                waits[s] = max(waits.get(s, 0), v)
+        for s, v in o["ext"]:
+            waits[s] = max(waits.get(s, 0), v)
+        for s, v in waits.items():
+            if seen[e].get(s, 0) < v:
+                Q[e].wait_ge(T.sem[s], v)
+                seen[e][s] = v
+                allw[s] = max(allw.get(s, 0), v)
+        r = o["alts"][e][1]()
+        if o["sem"] == "none":
+            continue
+        if o["sem"] is not None:
+            s = o["sem"]
+        elif i in raises:
+            s = "s" + e
+        else:
+            continue
+        r.then_inc(T.sem[s], o["semn"])
+        cnt[s] = cnt.get(s, 0) + o["semn"]
+        mark[i] = (s, cnt[s])
+    g.wait_ge(T.sem.sent, nsent)
+    for s, v in cnt.items():
+        if allw.get(s, 0) < v:
+            g.wait_ge(T.sem[s], v)

@@ -25,7 +25,7 @@ for _n, _c, _d in [
     ("eq", 256, BF), ("ZW", 512, BF), ("half", 256, BF), ("uS", 256, F32), ("a5", 16, F32), ("aF", 16 * ST, F32),
     ("amI", 16, I32), ("amJ", 16, I32), ("da", 16, F32), ("mis", 272, BF), ("dvS", 256, BF), ("pref", 256, BF),
     ("cm", 256, BF), ("bS", 256, F32), ("nS", 256, F32), ("f1", 16, F32), ("f2", 16, F32), ("offU", 32, U16),
-    ("dl", 16, F32), ("t2", 16, F32), ("aN", 16, F32), ("s1", 16, F32), ("s2", 16, F32), ("slU", 16, U16),
+    ("dl", 16, F32), ("t2", 16, F32), ("n240", 128, BF), ("s1", 16, F32), ("s2", 16, F32), ("slU", 16, U16),
     ("acc", 4, F32), ("posU", 4, U16), ("junk", 1024, BF), ("AI", 4, I32), ("AJ", 4, I32), ("nth", 4, F32), ("thF", 4, F32),
     ("n1", 4, F32), ("n2", 4, F32), ("g1", 4, F32), ("g2", 4, F32), ("g3", 4, F32), ("spU", 4, U16),
     ("CL", 1024, BF), ("k1", 64, F32), ("k2", 64, BF),
@@ -47,11 +47,15 @@ for _t in range(ST):
 
 PAR = {"g": 1.56, "sc": 3.8, "pe": 0.7, "fix": 60, "hop": 110, "self": 60, "rem": 1200, "lat": 2600, "slack": 60, "any": True}
 PAR.update({
-    "relu": (0, 0, 0, 0), "kv": 8, "sub": 2,
+    "relu": (0, 0, 0, 0), "kv": 12, "sub": 2,
     "eng": {'x0': 'VS', 'x1': 'S', 'x2': 'VS', 'x3': 'S', 'y0': 'S', 'y1': 'S', 'y2': 'S', 'y3': 'S', 'x0@0': 'S', 'x1@0': 'VS', 'x2@0': 'S'},
     "tpl": "Xm x0 y0 T16 pref eq x3 mx11 zS k2 km8 df1_1 df2_1 df0_1 df3_0 k1 mx14 vU K g2 mx10 n2 ra bU Bd ZT0 mx2 aU df1_0 mx8 mx9 x1 mx12 rb kx1 wo ZT1 km12 x2 mx4 posU uS mx3 junk3 kS nS junk2 km6 nth slU vF mx5 ab3 dl km2 cR topkA km0 mx7 cS mx6 g1 r16 km10 zd km4 kx3 kT CL0 spU mis kx0 df0_0 toaS zm dvS km14 pkM y1 ab0 y2 amI mx13 mx0 da f2 half aS amJ g3 df2_0 ZB kx2 t2 low ab1 CL1 junk0 xw cm offU bS pkA rb16 topkK n1 s2 pkK df3_1 pkB f1 junk1 a5 AJ AI mx1 toK ab2 tozS pkp mx15 y3",
     "tplL": "kS x3 df2_1 mx2 df0_1 k2 y0 x1 ZT0 low km0 Bd df1_1 n2 km12 bU pref x0 x2 k1 mx9 mx10 wo vU mx11 mx5 mx12 km10 kT CL0 g2 mx0 K df3_0 aU kx1 CL1 f2 offU mx6 kx2 ra zd mx7 r16 df2_0 mx4 zm pkM g1 n1 nth junk0 df0_0 spU g3 km8 Xm mx14 toaS rb cS y1 kx3 dvS y2 uS mx3 km2 T16 ab0 ZB junk3 df1_0 aS cm mx8 df3_1 y3 ZT1 zS slU junk2 da kx0 km6 ab1 ab2 t2 amI toK rb16 dl pkA bS topkA mx13 topkK cR eq nS km4 mis posU pkp km14 xw pkB f1 s2 AJ mx1 ab3 mx15 tozS junk1 AI a5 half vF amJ pkK",
 })
+ORDER = {'V': '070c0b0d1x0y1k0h1r0p150o0z0f0q1f181c2s1b132l0r2n192y1h1q1d0u2z1a140v1e2r2o2t431l342v2p102u1g48453c1w3d3f563g57523i0s533j5a3l5b3m3o3p3r3s5e5f4c1i4d414e2q4f1m4g4h464l4j4k4n5m5n6b4p5x6c6v6w4r6x5s515t5u5v4x4y5w4z64506f5o5p6g6h6i6j6k6l6m6n6o6p6q6r6s6t6u6y6z7382838485898b86878g8e8f7c7d7f8h7g8j7i8l7j7l7m7o7p8n7r7s9k9l9s9t8u9o8v9p8w818x8y9x8z9w938o91929597a4a599ataa9faf9g9h9ia6a7abbdauac9jbeadbfaeamaxayazb0b1b2b3b4b5b6b7b8b9babbbgbcbhblckclcmcncocrcpctcybubvcwbxcxbyczc0d1c1d3c3c4d5c6c7c9cae3e2ebeae6dcdde7decjdfeedgdhefd6dldjdkdndpemendrfbesdxexdydze0eofvepfwetfxeufcevewe1f4fffgfhfifjfkflfmfnfofpfqfrfsftfyfufzg3h2h3h4h5h9h6hbh7hggchegdgfhfgghhhjgihlgjglgmgogpgrhngsh1ilikisithuiphviohwhxhyixhziwi3hoi1i2i5i7j4j5i9jtjaifjfigihkdiij6juj7jbijkejmjcjdjejxjykfjzk0k1k2k3k4k5k6k7k8k9kakbkgkckhkllklllmlnlrloltlplykukvlwkxkylxl0lzm1l1m2l3l4l6l7l9m4lan2n1n5n6ndmbm5mcljmdn9menamfmgmknemmmimjmomqnlnrnwnmnsntn0oao3numwnvmxoemyobmzofnnognoohoiojokolomonooopoqorosotovowoxoyozp2p4p0p9p7p8pa',
+         'S': '021j201z27160e1y0w17280l0g1s0k1t121v0i0j262m21300n0m291u220x0t2a232b242c253332312x47113y3v4958544a5c5g5j4s5r4q4u6d6362605y616569686766707274717v7y8p8r8q8s9m9q9u9y9aa1989ca9akagaialajanavaraqapaobibkbmbjcdcgd7d9d8dae4e8ecegdsejdqduerf1f3f2f0eyf5fdf8f7f9f6g0g1g2g4gvhpgyhrhqhsimiqiuiyiaj1i8icj9jijljjjkjgjvjnjpjojrjqkikjkkkmlgldm6m7m9m8n3n7nbnfmrmpninqmtnxo0o1o2nzo4o6o7o8o5ocpdpcpe',
+         'P': '353637443a3b2w393u3x40383w3z3k5i3e55593n3q3h3t4b5d755h4i4m5k5l4o4t4v4w7677888a798c8d7a8i7u7x8m7b7w7e7za0807n7q7k787h7t8t9nbn9r909v949z96a29ba39e9dbscqcsbocucvccd0cfd4cebpeichbwc5btc8bqcibrc2bzcbdbe5e9g5dieddmehdoekdteldwdvgah8hag6hcg7hdguhighg9gxhmh0gbgegkgwgtgzgngqg8htj0kniniri0ivi4izi6j2ibj3ieidkslqlslukolvkplfm0lclhnhm3lekwktl5l8likql2krlbkzman4n8mlmhncmnngmunjnkmsmvp1p3p5p6pb',
+         'G': '081p091o0a1n062d2e2f2g2h2i2j2k426e5z5q6a8ka8ahasawd2eqezfafehkj8jsjhjwnyo9', 'Y': '0001030405npodou'}
 NCH = 4
 CH = 256 // NCH
 A = AluOpType
@@ -106,7 +110,10 @@ def build(g, core, T, topo, par):
             f = lambda: V.tensor_scalar(out, in0, s1, None, o0)
         else:
             f = lambda: V.tensor_scalar(out, in0, s1, s2, o0, o1)
-        return op({"V": (cv(n, half), f)}, R, W, banks, ext, after)
+        alts = {"V": (cv(n, half), f)}
+        if cur[0] < 0 and o0 == A.mult and W[0] not in ("I16", "BO16", "kc16", "thF") and (o1 is None or (o1 == A.add and isinstance(s2, float))):
+            alts["S"] = (cv(n) + 20, lambda: S.activation(out, in0, AF.Copy, bias=s2 or 0.0, scale=s1))
+        return op(alts, R, W, banks, ext, after)
 
     def vtt(out, in0, in1, o, n, R, W, banks=(), ext=(), after=()):
         return op({"V": (cv(n if banks else 2 * n), lambda: V.tensor_tensor(out, in0, in1, o))}, R, W, banks, ext, after)
@@ -118,7 +125,10 @@ def build(g, core, T, topo, par):
         return op({"V": (cv(n, half), lambda: V.tensor_tensor_scan(out, d0, d1, init, o0, o1))}, R, W, banks)
 
     def vset(ap, val, n, W):
-        return op({"V": (cv(n, True), lambda: V.memset(ap, val))}, [], W)
+        if W[0] == "ones":
+            return op({"V": (cv(n, True), lambda: V.memset(ap, val))}, [], W)
+        return op({"V": (cv(n, True), lambda: V.memset(ap, val)),
+                   "S": (cv(n) + 20, lambda: S.activation(ap, T.ones[:, 0:n], AF.Copy, scale=val))}, ["ones"], W)
 
     def act(out, in_, f, n, R, W, banks=(), bias=None, scale=None, accum=None, gather=False, ext=(), after=()):
         kw = {}
@@ -207,6 +217,7 @@ def build(g, core, T, topo, par):
         return pool(160 + 2 * n, lambda: g.iota(out, pat, base, cm), [], W)
 
     col = T.col
+    vset(T.ones[:], 1.0, 256, ["ones"])
     iota(T["io"][:, 0:1], [[0, 1]], 0, 1, 1, ["io"], False)
     iota(T.tJ[:], [[1, 160]], -16, -1, 160, ["tJ"])
     iota(T.tI[:], [[0, 16], [1, 16]], 0, 0, 256, ["tI"])
@@ -218,7 +229,7 @@ def build(g, core, T, topo, par):
     vts(T.U64[:], T.tJ[:, 0:144], col[:, 2:3], 64.0, A.is_equal, A.mult, 144, ["tJ", "c2"], ["U64"])
     vts(T.Un32[:], T.U64[:], -0.5, None, A.mult, None, 144, ["U64"], ["Un32"], half=True)
     vts(T.Id[:], T.tJ[:, 16:144], 0.0, None, A.is_equal, None, 128, ["tJ"], ["Id"])
-    for nm, w in (("nId", -1.0), ("hId", 0.5), ("sId", 0.0625), ("xId", 16.0), ("mId", -16.0), ("I16", 1.0)):
+    for nm, w in (("nId", -1.0), ("hId", 0.5), ("sId", 0.0625), ("xId", 16.0), ("mId", -16.0), ("n240", -240.0), ("I16", 1.0)):
         vts(T[nm][:], T.Id[:], w, None, A.mult, None, 128, ["Id"], [nm], half=True)
 
     def DG(U, k):
@@ -257,7 +268,6 @@ def build(g, core, T, topo, par):
     vts(T.R3[:], T.tI[:], 0.0, 2.0, A.not_equal, A.mult, 256, ["tI"], ["R3"])
     vts(T.dg[:], T.tI[:], r_, None, A.is_equal, None, 256, ["tI", "c0"], ["dg"])
     vscan(T.pw[:], T.R3[:, 0:16], T.dg[:, 0:16], 0.0, A.mult, A.add, 16, ["R3", "dg"], ["pw"])
-    vset(T.ones[:], 1.0, 256, ["ones"])
     vset(T.q25[:], -0.25, 256, ["q25"])
     vts(col[:, 11:12], r_, -8.46875, None, A.add, None, 1, ["c0"], ["c11"])
     vts(T.kc16[:], T.ones[:], col[:, 11:12], None, A.mult, None, 256, ["ones", "c11"], ["kc16"], half=True)
@@ -284,8 +294,9 @@ def build(g, core, T, topo, par):
     vset(T.KB[:, 256:320], 0.0, 64, ["Kd0"])
     for t in range(ST):
         vset(T.KB[:, KBW * t + 576:KBW * t + 640], 0.0, 64, ["Be%d" % t])
-    vset(T.SEL[:], 1.0, 2048, ["SEL"])
-    pool(4300, lambda: g.affine_select(T.SEL[:], T.SEL[:], [[1, 16], [16, 8], [0, 16]], A.is_equal, 0.0, 0, -1), ["SEL"], ["SEL"])
+    for j in range(8):
+        pool(720, lambda j=j: g.affine_select(T.SEL[:, 256 * j:256 * j + 256], T.ones[:], [[1, 2], [16, 8], [0, 16]], A.is_equal, 0.0, 2 * j, -1),
+             ["ones"], ["SEL%d" % j])
 
     vcp(T.aF[:, 0:16], T.avI[:], 16, ["avI"], ["a0"])
     vts(T.s1[:], T.lC[:], 2.0, None, A.mult, None, 16, ["lC"], ["s1"])
@@ -339,20 +350,18 @@ def build(g, core, T, topo, par):
                 lst.append((B[bk][:, 64 * j:64 * j + 64], T.mId[:], Ko, 64))
                 mi = 8 * hb + j
                 lst.append((B[bk][:, 64 * j:64 * j + 64], T.SEL[:, 128 * mi:128 * mi + 128], Km, 64))
-            mm(lst, ["mId", "SEL"] + oR("K"), ["b%d" % bk], bk, True, True, ext=oE + mE, after=oA + mA)
+            mm(lst, ["SEL%d" % j for j in range(8)] + ["mId"] + oR("K"), ["b%d" % bk], bk, True, True, ext=oE + mE, after=oA + mA)
             vts(T.CL[:, 512 * hb:512 * hb + 512], B[bk][:], 0.0, 16.0, A.max, A.min, 512, ["b%d" % bk], ["CL%d" % hb], (bk,))
-        mm([(B[6][:, 0:64], T.xId[:], Ko, 64), (B[6][:, 0:64], T.nId[:], Ko, 64)] +
+        mm([(B[6][:, 0:64], T.xId[:], Ko, 64), (B[6][:, 0:64], T.nId[:], Ko, 64), (B[6][:, 0:64], T.n240[:], T.ones[:, 0:64], 64)] +
            [(B[6][:, 0:64], T.Id[:], T.CL[:, 64 * j:64 * j + 64], 64) for j in range(8)],
-           ["xId", "nId", "Id", "CL0"] + oR("K"), ["b6"], 6, True, False, ext=oE, after=oA)
+           ["xId", "nId", "n240", "Id", "CL0"] + oR("K"), ["b6"], 6, True, False, ext=oE, after=oA)
         mm([(B[6][:, 0:64], T.Id[:], T.CL[:, 64 * j:64 * j + 64], 64) for j in range(8, 16)], ["CL1"], ["b6"], 6, False, True)
-        act(T.k1[:], B[6][:, 0:64], AF.Identity, 64, ["b6", "c13"], ["k1"], (6,), bias=col[:, 13:14])
-        vtt(T.k1[:], T.k1[:], o[:, own:own + 64], A.mult, 64, ["k1"] + oR("M"), ["k1"], ext=oE, after=oA)
+        vtt(T.k1[:], B[6][:, 0:64], o[:, own:own + 64], A.mult, 64, ["b6"] + oR("M"), ["k1"], (6,), ext=oE, after=oA)
         vtt(T.k2[:], T.k1[:], Ko, A.add, 64, ["k1"] + oR("K"), ["k2"])
         scat(T.KB[:, ko + 320:ko + 640], T.spU[:], m[:, own + 144:own + 208], 64, ["spU", "Be%d" % tk], ["Bd%d" % tk, "Be%d" % tk], ext=kE + mE, after=kA + mA)
         scat(T.KB[:, ko:ko + 320], T.spU[:], T.k2[:], 64, ["spU", "k2"], ["K%d" % tk, "Kd%d" % tk], ext=kE, after=kA)
         mm([(B[6][:, 64:80], DG("U64", j), T.KB[:, ko + 320 + j:ko + 576:16], 16) for j in range(16)], ["U64", "Bd%d" % tk], ["b6b"], 6, True, True)
 
-    vset(col[:, 13:14], -240.0, 1, ["c13"])
 
     for t in range(ST):
         last = t == ST - 1
@@ -599,13 +608,30 @@ def schedule(ops, par):
     return order, eng, start, end
 
 
+def merge(ops, table):
+    dig = "0123456789abcdefghijklmnopqrstuvwxyz"
+    seq = {e: [dig.index(s[j]) * 36 + dig.index(s[j + 1]) for j in range(0, len(s), 2)] for e, s in table.items()}
+    eng = [None] * len(ops)
+    pos = {e: 0 for e in seq}
+    order = []
+    while len(order) < len(ops):
+        before = len(order)
+        for e, s in seq.items():
+            while pos[e] < len(s) and all(eng[d] is not None for d in ops[s[pos[e]]]["deps"]):
+                eng[s[pos[e]]] = e
+                order.append(s[pos[e]])
+                pos[e] += 1
+        assert len(order) > before
+    return order, eng
+
+
 def rank_program(g, core, T, topo):
     if T.rank_of(core) is None:
         return
     par = PAR
     g.vector.memset(T.col[:, 14:15], 0.1875).then_inc(T.sem.sV, 1)
     ops, nsent = build(g, core, T, topo, par)
-    order, eng, start, end = schedule(ops, par)
+    order, eng = merge(ops, ORDER) if ORDER else schedule(ops, par)[:2]
     Q = {"V": g.vector, "S": g.scalar, "P": g.tensor, "G": g, "Y": g.sync}
     cnt = {"sV": 1, "out": 0}
     mark = {}

@@ -17,7 +17,7 @@ def _s(name, cols, d):
 for _n, _c, _d in [
     ("X", 4112, BF), ("P", 1024, I32), ("XY", 8192, BF), ("DF", 4096, BF), ("AB", 4096, BF), ("MX", 4096, BF),
     ("KB", KBW * ST, BF), ("aU", 16, U16), ("aS", 16 * ST, F32), ("zb", 256 * ST, BF), ("zS", 256 * ST, BF),
-    ("pkS", PKW * ST, BF), ("pkO", PKW * ST, BF), ("pkM", PKW * ST, BF), ("pkA", 8 * (ST + 2), BF),
+    ("pkS", PKW * ST, BF), ("pkO", PKW * ST, BF), ("pkM", PKW * ST, BF), ("pkA", 32 * ST, BF),
     ("avI", 16, I32), ("bvI", 16, I32), ("kcI", 256, I32), ("thI", 4, I32),
     ("ra", 256, U16), ("rb", 256, U16), ("rb16", 256, F16), ("wo", 256, U16), ("bU", 16, U16), ("bF", 16, F32),
     ("kT", 256, F32), ("kS", 256, F32), ("r16", 16, F32), ("low", 16, F32), ("ZT", 256, BF), ("ZB", 256, BF),
@@ -47,7 +47,7 @@ for _t in range(ST):
 
 PAR = {"g": 1.56, "sc": 3.8, "pe": 0.7, "fix": 60, "hop": 110, "self": 60, "rem": 1200, "lat": 2600, "slack": 60, "any": True}
 PAR.update({
-    "relu": (0, 0, 0, 0), "kv": 12, "sub": 2,
+    "parts": ((3, 2), (1, 0)), "kv": 8, "sub": 2,
     "eng": {'x0': 'VS', 'x1': 'S', 'x2': 'VS', 'x3': 'S', 'y0': 'S', 'y1': 'S', 'y2': 'S', 'y3': 'S', 'x0@0': 'S', 'x1@0': 'VS', 'x2@0': 'S'},
     "tpl": "Xm x0 y0 T16 pref eq x3 mx11 zS k2 km8 df1_1 df2_1 df0_1 df3_0 k1 mx14 vU K g2 mx10 n2 ra bU Bd ZT0 mx2 aU df1_0 mx8 mx9 x1 mx12 rb kx1 wo ZT1 km12 x2 mx4 posU uS mx3 junk3 kS nS junk2 km6 nth slU vF mx5 ab3 dl km2 cR topkA km0 mx7 cS mx6 g1 r16 km10 zd km4 kx3 kT CL0 spU mis kx0 df0_0 toaS zm dvS km14 pkM y1 ab0 y2 amI mx13 mx0 da f2 half aS amJ g3 df2_0 ZB kx2 t2 low ab1 CL1 junk0 xw cm offU bS pkA rb16 topkK n1 s2 pkK df3_1 pkB f1 junk1 a5 AJ AI mx1 toK ab2 tozS pkp mx15 y3",
     "tplL": "kS x3 df2_1 mx2 df0_1 k2 y0 x1 ZT0 low km0 Bd df1_1 n2 km12 bU pref x0 x2 k1 mx9 mx10 wo vU mx11 mx5 mx12 km10 kT CL0 g2 mx0 K df3_0 aU kx1 CL1 f2 offU mx6 kx2 ra zd mx7 r16 df2_0 mx4 zm pkM g1 n1 nth junk0 df0_0 spU g3 km8 Xm mx14 toaS rb cS y1 kx3 dvS y2 uS mx3 km2 T16 ab0 ZB junk3 df1_0 aS cm mx8 df3_1 y3 ZT1 zS slU junk2 da kx0 km6 ab1 ab2 t2 amI toK rb16 dl pkA bS topkA mx13 topkK cR eq nS km4 mis posU pkp km14 xw pkB f1 s2 AJ mx1 ab3 mx15 tozS junk1 AI a5 half vF amJ pkK",
@@ -56,6 +56,10 @@ ORDER = {'V': '070c0b0d1x0y1k0h1r0p150o0z0f0q1f181c2s1b132l0r2n192y1h1q1d0u2z1a1
          'S': '021j201z27160e1y0w17280l0g1s0k1t121v0i0j262m21300n0m291u220x0t2a232b242c253332312x47113y3v4958544a5c5g5j4s5r4q4u6d6362605y616569686766707274717v7y8p8r8q8s9m9q9u9y9aa1989ca9akagaialajanavaraqapaobibkbmbjcdcgd7d9d8dae4e8ecegdsejdqduerf1f3f2f0eyf5fdf8f7f9f6g0g1g2g4gvhpgyhrhqhsimiqiuiyiaj1i8icj9jijljjjkjgjvjnjpjojrjqkikjkkkmlgldm6m7m9m8n3n7nbnfmrmpninqmtnxo0o1o2nzo4o6o7o8o5ocpdpcpe',
          'P': '353637443a3b2w393u3x40383w3z3k5i3e55593n3q3h3t4b5d755h4i4m5k5l4o4t4v4w7677888a798c8d7a8i7u7x8m7b7w7e7za0807n7q7k787h7t8t9nbn9r909v949z96a29ba39e9dbscqcsbocucvccd0cfd4cebpeichbwc5btc8bqcibrc2bzcbdbe5e9g5dieddmehdoekdteldwdvgah8hag6hcg7hdguhighg9gxhmh0gbgegkgwgtgzgngqg8htj0kniniri0ivi4izi6j2ibj3ieidkslqlslukolvkplfm0lclhnhm3lekwktl5l8likql2krlbkzman4n8mlmhncmnngmunjnkmsmvp1p3p5p6pb',
          'G': '081p091o0a1n062d2e2f2g2h2i2j2k426e5z5q6a8ka8ahasawd2eqezfafehkj8jsjhjwnyo9', 'Y': '0001030405npodou'}
+ORDER = {'V': '070b0c1j0d0h1k0p0z0y1l0u1g15101e0q0o1h0r2s2n2r1r1q0f2t2l132u0s2y2v182z2p2o191c431u33320v453c1a1b1d3d1f3f1m533g3i143j3l1i3m52565q57464c2q4d5r4e5v4f5u4g414h1w4l4j4k4n4p4r515d6l5e4x5f614y664z5g62505h6z635i6s64735j675k68705l74695m756a5n5o5p6b6c8a6d6e6f6g767h776i7b8b8j8c8h8d8e8f8o8m8n8p7k7l7n7o8r7q8t7r8z897t8v7u9t9w9xag9s92ah93ak94al958w96979b999a9d9f9hbba39ra49na59oar9pas9qa6biatbpa7auawbta8a9axaabqayabbuazacbvb0adaeafb1b2d0b3b4b5b6bwb7bxb8c1d1d9d2d7d3d4d5dedcdddfcacbdhcddjcecgdpdlchcjckejeiemf7endsf6dtfadudvfbdwczdxdme1dze0e3e5ehe7etg1euedeveefhefewfiegexfjeyfkg8gffmezgjfnf0ggfof1gkfpf2glfqf3f4f5frfshqftfufvfwgmfxgnfygrhrhzhshxhthuhvi4i2i3i5h0h1h3i7h4h6i9h7h9ibifhajcj9j8jdiijxijjwikk0ilk1imhpiniciripiqitivixkrjjj3jkj7j4k7jlj5k8jmj6l5jnk9kcl6jokakyjpkdjql9kejrlakfjslbkgjtjujvkhkikjmgkkklkmlcknldkolhmhmnmimpmjmkmlmsmumtmvlqlrltmxlumylwlxn4n0lznyo2nxm0ommfo1n7oln8opn9oqnanbn1ncngnenfninknmpgo8nso9nwoantowobnuoxocpnpuodp1oenvp2ofpvp3ogoyp4ohp5oiozojokp6p7p8p9pzpapbpcpdq0q1q2q6q3q8q4qdqbqcqe'.replace('6g767h77', '6g766h77'),
+         'S': '02291z1x272028220i1y210j0l0e0n0k120w16260m2a230g2b241s172c1v30252x0t0x34314a3s3p49483y3v4754585s1t5b5w112m4s5z4q4u6k6q6m6p6o6r6t6v6w6x6u7178797c7a807x9086838y8x9y9uaiama19iap9gba9kbfbcbhbebgbnbmbkblbjbrbybzc2c0cqcndqdoctcwdnekeof8erfce8ffe6eag0g6g2g4g5g7g9gdgagcgbghgogpgsgqhdhgighjhmieidjajejyjhk2iyk5iwj0kqkskvkwkxkukzl7l0l2l1l3lelilglfm6n5m3n3mcm9n2nzo3ono6ornnounlnppfphplpmpkpjpoprpqpspppwqhqgqi',
+         'P': '352w36443a3r3o3839403u3b3x3t3e3h3k3q3n373w3z4b5a7d55595t4i4m5x4o4t6j4v5c4w5y608i8g7e7g7i8k8l7f7j8q7z7w8885828u7h7m817p7s877y847v91a0c39v9zaj989can9ea2b99j9l9maoaqd8d6c5c4c6dadbc8dgcpcmc9dkcscvcocrcycicfcucccxclc7dreqgtelepf9dye2esfde4ebe9fzecfefghyhwgugygwi0i1gvgzi6hchfiagxhihlh5hhh2hkhbhejgh8hnihholjjbjfjzioisk3iujiizkpj1j2k4k6mmmolklpmqmrlnlomwm5llm2mzmblvmelslmm8m7mdo5lym1mam4n6o0o4oondnhosnjnopenqo7nrotovq5q7q9qaqf',
+         'G': '08090a1o1p1n062d2e2f2g2h422i2j2k6n656y728sbdavbobsdig3flgegii8ktkbl4l8pipt', 'Y': '0001030405p0pxpy'}
 NCH = 4
 CH = 256 // NCH
 A = AluOpType
@@ -326,7 +330,7 @@ def build(g, core, T, topo, par):
             oE, oA = [], []
             mE, mA = [("rM%d" % t, NE)], [snd["P", t]]
             aE, aA = [("rA%d" % t, NE // 2), ("rO%d" % t, NE // 2)], [snd["A", t]]
-            c1, c2 = T.pkA[:, 8 * t + 7:8 * t + 8], T.pkA[:, 8 * t + 15:8 * t + 16]
+            c1, c2 = T.pkA[:, 32 * t + 7:32 * t + 8], T.pkA[:, 32 * t + 15:32 * t + 16]
             kE, kA = [], []
         else:
             o, m = T.pkO, T.pkM
@@ -334,10 +338,10 @@ def build(g, core, T, topo, par):
             oE, oA = [("rO%d" % t, NE // 2)], [snd["P", t]]
             mE, mA = [("rM%d" % t, NE // 2)], [snd["P", t]]
             aE, aA = [("rA%d" % t, NE)] + oE, [snd["A", t]] + oA
-            c1, c2 = T.pkA[:, 8 * t + 7:8 * t + 8], T.pkO[:, own + 143:own + 144]
+            c1, c2 = T.pkA[:, 32 * t + 7:32 * t + 8], T.pkO[:, own + 143:own + 144]
             kE, kA = [("rK%d" % tk, NE)], [snd["K", t]]
-        vts(T.n1[:, 0:1], T.pkS[:, own + 143:own + 144], c1, c2, A.min, A.min, 1, ["pkA%d" % t], ["n1"], ext=aE, after=aA)
-        vts(T.n2[:, 0:1], T.n1[:, 0:1], m[:, own + 143:own + 144], 128.0, A.min, A.min, 1, ["n1"], ["n2"], ext=mE, after=mA)
+        vts(T.n1[:, 0:1], T.pkS[:, own + 143:own + 144], c1, None, A.min, None, 1, ["pkA%d" % t], ["n1"], ext=aE[:1], after=aA[:1])
+        vts(T.n2[:, 0:1], T.n1[:, 0:1], m[:, own + 143:own + 144], c2, A.min, A.min, 1, ["n1"], ["n2"], ext=mE + aE, after=mA + aA)
         vts(T.g1[:], T.jC[:, 0:4], T.n2[:, 0:1], 512.0, A.is_gt, A.mult, 4, ["jC0", "n2"], ["g1"])
         vtt(T.g2[:], T.g1[:], o[:, own + 128:own + 132], A.add, 4, ["g1"] + oR("p"), ["g2"], ext=oE, after=oA)
         vtt(T.g3[:], T.g2[:], T.jC[:, 8:12], A.min, 4, ["g2", "jC2"], ["g3"])
@@ -448,48 +452,55 @@ def build(g, core, T, topo, par):
         vts(T.amJ[:], T.amI[:], 1023, None, A.bitwise_and, None, 16, ["amI"], ["amJ"])
         vtt(T.da[:], aF, T.amJ[:], A.subtract, 16, ["aU", "amJ"], ["da"])
         vts(T.half[:], B[6][:, 0:256], M1, M1, A.add, A.subtract, 256, ["b6"], ["half"], (6,))
-        for c in range(NCH):
-            lo, hi = 16 * CH * c, 16 * CH * (c + 1)
-            for j in range(NSUB):
-                l0, l1 = CH * c + DCH * j, CH * c + DCH * (j + 1)
-                gtt(T.DF[:, 16 * l0:16 * l1], T.XY[:, 4096 + 16 * l0:4096 + 16 * l1], T.wo[:, l0:l1], T.XY[:, 16 * l0:16 * l1], A.subtract, 16 * DCH,
-                    ["x%d" % c, "y%d" % c, "wo"], ["df%d_%d" % (c, j)])
-            dfs = ["df%d_%d" % (c, j) for j in range(NSUB)]
-            out = B[0][:, CH * c:CH * (c + 1)]
-            if par["relu"][c]:
-                vts(T.AB[:, lo:hi], T.DF[:, lo:hi], 0.0, None, A.max, None, 16 * CH, dfs, ["ab%d" % c], half=True)
-                mm([(out, DG("Un32", k), T.DF[:, lo + k:hi:16], CH) for k in range(16)], ["Un32"] + dfs, ["b0"], 0, c == 0, False)
-                mm([(out, DG("U64", k), T.AB[:, lo + k:hi:16], CH) for k in range(16)], ["U64", "ab%d" % c], ["b0"], 0, False, c == NCH - 1)
+        def new_a():
+            vscan(T.nS[:], T.R2[:], B[7][:, 0:256], 0.0, A.add, A.min, 256, ["R2", "b7"], ["nS"], (7,))
+            vts(T.dl[:], T.nS[:, 15:256:16], 1.0, None, A.is_gt, None, 16, ["nS"], ["dl"])
+            vtt(T.t2[:], T.dl[:], T.da[:], A.mult, 16, ["dl", "da"], ["t2"])
+            aS = T.aS[:, 16 * t:16 * t + 16]
+            vtt(aS, T.t2[:], T.amJ[:], A.add, 16, ["t2", "amJ"], ["aS%d" % t])
+            if not last:
+                snd["a", t] = send([(1, aS, T.aF[:, 16 * t + 16:16 * t + 32], "ra%d" % (t + 1))], ["aS%d" % t], par["lat"])
             else:
+                dma("Y", T.ya[:], aS, ["aS%d" % t], [], "out", 2500)
+
+        miss = ["mis%d" % pi for pi in range(len(par["parts"]))]
+        for pi, cs in enumerate(par["parts"]):
+            bk, off, key = (0, 0, "b0") if pi % 2 == 0 else (2, 256, "b2b")
+            a0, a1 = CH * min(cs), CH * (max(cs) + 1)
+            n, nl, s = a1 - a0, (a1 - a0) // 16, "_%d" % pi
+            for c in cs:
+                lo, hi = 16 * CH * c, 16 * CH * (c + 1)
+                for j in range(NSUB):
+                    l0, l1 = CH * c + DCH * j, CH * c + DCH * (j + 1)
+                    gtt(T.DF[:, 16 * l0:16 * l1], T.XY[:, 4096 + 16 * l0:4096 + 16 * l1], T.wo[:, l0:l1], T.XY[:, 16 * l0:16 * l1], A.subtract, 16 * DCH,
+                        ["x%d" % c, "y%d" % c, "wo"], ["df%d_%d" % (c, j)])
+                dfs = ["df%d_%d" % (c, j) for j in range(NSUB)]
+                out = B[bk][:, off + CH * c:off + CH * (c + 1)]
                 act(T.AB[:, lo:hi], T.DF[:, lo:hi], AF.Abs, 16 * CH, dfs, ["ab%d" % c], scale=0.5)
-                mm([(out, DG("U64", k), T.AB[:, lo + k:hi:16], CH) for k in range(16)], ["U64", "ab%d" % c], ["b0"], 0, c == 0, c == NCH - 1)
-        mm([(B[7][:, 0:256], T.Id[:], T.cmk[:], 256)], ["Id", "cmk"], ["b7"], 7, True, False)
-        act(T.mis[:, 0:256], B[0][:, 0:256], AF.Sign, 256, ["b0", "nth"], ["mis"], (0,), bias=T.nth[:, 0:1], scale=1.0 / 32)
-        mm([(B[7][:, 0:256], T.BOs[:], T.mis[:, 0:256], 256)], ["BOs", "mis"], ["b7"], 7, False, True)
-        mm([(B[0][:, 256:512], T.BOs[:], T.mis[:, 0:256], 256)], ["BOs", "mis"], ["b0b"], 0, True, True)
-        vscan(T.nS[:], T.R2[:], B[7][:, 0:256], 0.0, A.add, A.min, 256, ["R2", "b7"], ["nS"], (7,))
-        vts(T.dl[:], T.nS[:, 15:256:16], 1.0, None, A.is_gt, None, 16, ["nS"], ["dl"])
-        vtt(T.t2[:], T.dl[:], T.da[:], A.mult, 16, ["dl", "da"], ["t2"])
-        aS = T.aS[:, 16 * t:16 * t + 16]
-        vtt(aS, T.t2[:], T.amJ[:], A.add, 16, ["t2", "amJ"], ["aS%d" % t])
-        if not last:
-            snd["a", t] = send([(1, aS, T.aF[:, 16 * t + 16:16 * t + 32], "ra%d" % (t + 1))], ["aS%d" % t], par["lat"])
-        else:
-            dma("Y", T.ya[:], aS, ["aS%d" % t], [], "out", 2500)
+                mm([(out, DG("U64", k), T.AB[:, lo + k:hi:16], CH) for k in range(16)], ["U64", "ab%d" % c], [key], bk, c == cs[0], c == cs[-1])
+            mm([(B[7][:, a0:a1], T.Id[:], T.cmk[:, a0:a1], n)], ["Id", "cmk"], ["b7"], 7, True, False, nm=s)
+            act(T.mis[:, a0:a1], B[bk][:, off + a0:off + a1], AF.Sign, n, [key, "nth"], [miss[pi]], (bk,), bias=T.nth[:, 0:1], scale=1.0 / 32)
+            mm([(B[7][:, a0:a1], T.BOs[:], T.mis[:, a0:a1], n)], ["BOs", miss[pi]], ["b7"], 7, False, True)
+            if cs is par["parts"][-1]:
+                new_a()
+            vtt(T.cm[:, a0:a1], T.eq[:, a0:a1], B[7][:, a0:a1], A.is_gt, n, ["eq", "b7"], ["cm" + s], (7,))
+            vscan(T.bS[:, a0:a1], T.R3[:, a0:a1], T.cm[:, a0:a1], 0.0, A.mult, A.add, n, ["R3", "cm" + s], ["bS" + s])
+            q0, q1 = a0 // 16, a1 // 16
+            vts(T.f1[:, q0:q1], T.bS[:, a0 + 15:a1:16], T.pw[:, 15:16], col[:, 12:13], A.not_equal, A.mult, nl, ["bS" + s, "pw", "c12"], ["f1" + s])
+            vtt(T.f2[:, q0:q1], T.f1[:, q0:q1], T.cS[:, a0 + 15:a1:16], A.max, nl, ["f1" + s, "cS"], ["f2" + s])
+            vcp(T.offU[:, 2 * q0:2 * q1:2], T.f2[:, q0:q1], nl, ["f2" + s], ["offU" + s])
+            for lh in range(q1 - 1, q0 - 1, -1):
+                scat(T.X[:], T.offU[:, 2 * lh:2 * lh + 1], T.half[:, 16 * lh:16 * lh + 16], 16, ["offU" + s, "half"], Xr)
+        mm([(B[0][:, 256:512], T.BOs[:], T.mis[:, 0:256], 256)], ["BOs"] + miss, ["b0b"], 0, True, True)
         act(T.dvS[:], B[0][:, 256:512], AF.Sign, 256, ["b0b", "c14"], ["dvS"], (0,), bias=col[:, 14:15])
-        vtt(T.cm[:], T.eq[:], B[7][:, 0:256], A.is_gt, 256, ["eq", "b7"], ["cm"], (7,))
-        vscan(T.bS[:], T.R3[:], T.cm[:], 0.0, A.mult, A.add, 256, ["R3", "cm"], ["bS"])
-        vts(T.f1[:], T.bS[:, 15:256:16], T.pw[:, 15:16], col[:, 12:13], A.not_equal, A.mult, 16, ["bS", "pw", "c12"], ["f1"])
-        vtt(T.f2[:], T.f1[:], T.cS[:, 15:256:16], A.max, 16, ["f1", "cS"], ["f2"])
-        vcp(T.offU[:, 0:32:2], T.f2[:], 16, ["f2"], ["offU"])
         own = PKW * t
         vscan(T.pref[:], T.ones[:], T.dvS[:], 0.0, A.add, A.add, 256, ["ones", "dvS"], ["pref"], half=True)
         act(T.pkS[:, own + 136:own + 144], T.pref[:, 248:256], AF.Copy, 8, ["pref"], ["pkA%d" % t])
         src = T.pkS[:, own + 136:own + 144]
         if not last:
-            snd["A", t] = send([(2, src, T.pkA[:, 8 * t:8 * t + 8], "rA%d" % t)], ["pkA%d" % t], par["lat"])
+            snd["A", t] = send([(2, src, T.pkA[:, 32 * t:32 * t + 8], "rA%d" % t)], ["pkA%d" % t], par["lat"])
         else:
-            snd["A", t] = send([(1, src, T.pkA[:, 8 * t:8 * t + 8], "rA%d" % t), (3, src, T.pkA[:, 8 * t + 8:8 * t + 16], "rO%d" % t)], ["pkA%d" % t], par["lat"] + 600)
+            snd["A", t] = send([(1, src, T.pkA[:, 32 * t:32 * t + 8], "rA%d" % t), (3, src, T.pkA[:, 32 * t + 8:32 * t + 16], "rO%d" % t)], ["pkA%d" % t], par["lat"] + 600)
         for j in range(4):
             act(T.junk[:, 256 * j:256 * j + 256], T.pref[:], AF.Sign, 256, ["pref", "jC1"], ["junk%d" % j, "acc%d" % j], bias=T.jC[:, 4 + j:5 + j], accum=T.acc[:, j:j + 1])
         accs = ["acc%d" % j for j in range(4)]
@@ -499,7 +510,7 @@ def build(g, core, T, topo, par):
         gath(T.pkS[:, own + 144:own + 208], T.KB[:, ko + 320:ko + 640], T.posU[:], 64, ["posU", Bt, "Be%d" % t], ["pkB%d" % t], "S")
         act(T.pkS[:, own + 208:own + 272], T.KB[:, ko:ko + 320].indirect(T.posU[:]), AF.Identity, 64, ["posU", Kt, "Kd%d" % t, "c15"], ["pkL%d" % t],
             bias=col[:, 15:16], gather=True)
-        act(T.pkS[:, own:own + 64], T.mis[:].indirect(T.posU[:]), AF.Copy, 64, ["posU", "mis", "misd"], ["pkM%d" % t], bias=0.5, scale=0.5, gather=True)
+        act(T.pkS[:, own:own + 64], T.mis[:].indirect(T.posU[:]), AF.Copy, 64, ["posU", "misd"] + miss, ["pkM%d" % t], bias=0.5, scale=0.5, gather=True)
         sO, sM = T.pkS[:, own:own + 144], T.pkS[:, own + 128:own + 272]
         pkR = ["pk%s%d" % (a, t) for a in ("BLpA" if last else "KMBLpA")]
         if not last:
@@ -514,8 +525,6 @@ def build(g, core, T, topo, par):
             snd["z", t] = send([(1, zS, T.zb[:, 256 * t + 256:256 * t + 512], "rz%d" % (t + 1))], ["zS%d" % t], par["lat"] + 600)
         else:
             dma("Y", T.yz[:], zS, ["zS%d" % t], [], "out", 2500)
-        for lh in range(15, -1, -1):
-            scat(T.X[:], T.offU[:, 2 * lh:2 * lh + 1], T.half[:, 16 * lh:16 * lh + 16], 16, ["offU", "half"], Xr)
         if not last:
             vts(T.AI[:, 0:1], T.pref[:, 255:256], 0.5, None, A.mult, None, 1, ["pref"], ["AI"])
             vts(T.AJ[:, 0:1], T.AI[:, 0:1], 31, None, A.bitwise_and, None, 1, ["AI"], ["AJ"])

@@ -8,12 +8,6 @@ PKW = 272
 BF, F32, I32, U16, F16 = "bfloat16", "float32", "int32", "uint16", "float16"
 
 SCRATCH = {}
-
-
-def _s(name, cols, d):
-    SCRATCH[name] = ("sbuf", [128, cols], d)
-
-
 for _n, _c, _d in [
     ("X", 4112, BF), ("P", 1024, I32), ("XY", 8192, BF), ("DF", 4096, BF), ("AB", 4096, BF), ("MX", 4096, BF),
     ("KB", KBW * ST, BF), ("aU", 16, U16), ("aS", 16 * ST, F32), ("zb", 256 * ST, BF), ("zS", 256 * ST, BF),
@@ -25,19 +19,27 @@ for _n, _c, _d in [
     ("eq", 256, BF), ("ZW", 512, BF), ("half", 256, BF), ("uS", 256, F32), ("a5", 16, F32), ("aF", 16 * ST, F32),
     ("amI", 16, I32), ("amJ", 16, I32), ("da", 16, F32), ("mis", 272, BF), ("dvS", 256, BF), ("pref", 256, BF),
     ("cm", 256, BF), ("bS", 256, F32), ("nS", 256, F32), ("f1", 16, F32), ("f2", 16, F32), ("offU", 32, U16),
-    ("dl", 16, F32), ("t2", 16, F32), ("n240", 128, BF), ("s1", 16, F32), ("s2", 16, F32), ("slU", 16, U16),
-    ("acc", 4, F32), ("posU", 4, U16), ("junk", 1024, BF), ("AI", 4, I32), ("AJ", 4, I32), ("nth", 4, F32), ("thF", 4, F32),
+    ("dl", 16, F32), ("t2", 16, F32), ("s1", 16, F32), ("s2", 16, F32), ("slU", 16, U16),
+    ("acc", 16, F32), ("accS", 16, F32), ("posU", 4, U16), ("junk", 1024, BF), ("AI", 4, I32), ("AJ", 4, I32), ("nth", 4, F32), ("thF", 4, F32),
     ("n1", 4, F32), ("n2", 4, F32), ("g1", 4, F32), ("g2", 4, F32), ("g3", 4, F32), ("spU", 4, U16),
-    ("CL", 1024, BF), ("k1", 64, F32), ("k2", 64, BF),
+    ("CL", 1024, BF), ("k1", 64, BF),
     ("ZC", 128, BF), ("hJ", 32, I32), ("hl", 32, BF), ("hm", 512, BF),
-    ("io", 4, I32), ("ia", 4, I32), ("col", 16, F32), ("ones", 256, BF), ("Id", 128, BF), ("nId", 128, BF), ("hId", 128, BF),
+    ("io", 4, I32), ("ia", 4, I32), ("col", 16, F32), ("ones", 256, BF), ("Id", 128, BF), ("nId", 128, BF), ("hId", 128, F16),
     ("sId", 128, BF), ("xId", 128, BF), ("mId", 128, BF), ("I16", 128, F16), ("BO", 128, BF), ("BO16", 128, F16), ("BOs", 128, BF),
-    ("Wu", 128, BF), ("WT", 128, BF), ("WC", 128, BF), ("U64", 144, BF), ("Un32", 144, BF), ("Vs", 640, BF),
+    ("Wu", 144, BF), ("WT", 128, BF), ("WC", 128, BF), ("U64", 144, BF), ("Un32", 144, BF), ("Vs", 640, BF),
     ("SEL", 2048, BF), ("tri", 256, BF), ("cmk", 256, BF), ("R1", 256, BF), ("R2", 256, BF), ("R3", 256, BF), ("dg", 256, BF),
-    ("kc16", 256, F16), ("q25", 256, BF), ("wc", 256, BF), ("tI", 256, F32), ("tJ", 160, F32),
-    ("vC", 32, F32), ("lC", 16, F32), ("bcF", 48, F32), ("bcU", 48, U16), ("jC", 12, F32), ("pw", 16, F32),
+    ("tId", 128, BF), ("wc", 256, BF), ("tI", 256, F32), ("tJ", 160, F32),
+    ("vC", 32, F16), ("lC", 16, F32), ("bcF", 48, F32), ("bcU", 48, U16), ("jC", 12, F32), ("pw", 16, F32),
 ]:
-    _s(_n, _c, _d)
+    SCRATCH[_n] = ("sbuf", [128, _c], _d)
+for _n, _c, _d in (("ZB", 32, BF), ("T16", 32, F16)):
+    SCRATCH[_n] = ("sbuf", [128, 8, _c], _d)
+for _n, _c, _d in (("X", 4128, BF), ("cR", 384, F32), ("eq", 384, BF), ("cm", 384, BF), ("bS", 384, F32), ("cmk", 384, BF), ("R3", 384, BF), ("R2", 384, BF),
+                   ("bcF", 72, F32), ("bcU", 72, U16), ("tI", 384, F32), ("cS", 384, F32), ("ZT", 48, BF), ("SK", 32, BF), ("skU", 4, U16), ("skW", 32, BF),
+                   ("vC", 32, F32), ("vD", 32, F16), ("Id2", 256, BF), ("ia", 16, I32), ("col", 20, F32), ("Vs", 16, BF), ("f3", 16, F32)):
+    SCRATCH[_n] = ("sbuf", [128, _c], _d)
+for _n in ("Vs", "accS", "uS"):
+    del SCRATCH[_n]
 for _b in range(8):
     SCRATCH["B%d" % _b] = ("psum", [128, 512], F32)
 
@@ -45,22 +47,33 @@ SEMAPHORES = ["sV", "sS", "sP", "sG", "sent", "out"] + ["ld%d" % i for i in rang
 for _t in range(ST):
     SEMAPHORES += ["rK%d" % _t, "ra%d" % _t, "rz%d" % _t, "rO%d" % _t, "rM%d" % _t, "rA%d" % _t]
 
-PAR = {"g": 1.56, "sc": 3.8, "pe": 0.7, "fix": 60, "hop": 110, "self": 60, "rem": 1200, "lat": 2600, "slack": 60, "any": True}
-PAR.update({
-    "parts": ((3, 2), (1, 0)), "kv": 8, "sub": 2,
-    "eng": {'x0': 'VS', 'x1': 'S', 'x2': 'VS', 'x3': 'S', 'y0': 'S', 'y1': 'S', 'y2': 'S', 'y3': 'S', 'x0@0': 'S', 'x1@0': 'VS', 'x2@0': 'S'},
-    "tpl": "Xm x0 y0 T16 pref eq x3 mx11 zS k2 km8 df1_1 df2_1 df0_1 df3_0 k1 mx14 vU K g2 mx10 n2 ra bU Bd ZT0 mx2 aU df1_0 mx8 mx9 x1 mx12 rb kx1 wo ZT1 km12 x2 mx4 posU uS mx3 junk3 kS nS junk2 km6 nth slU vF mx5 ab3 dl km2 cR topkA km0 mx7 cS mx6 g1 r16 km10 zd km4 kx3 kT CL0 spU mis kx0 df0_0 toaS zm dvS km14 pkM y1 ab0 y2 amI mx13 mx0 da f2 half aS amJ g3 df2_0 ZB kx2 t2 low ab1 CL1 junk0 xw cm offU bS pkA rb16 topkK n1 s2 pkK df3_1 pkB f1 junk1 a5 AJ AI mx1 toK ab2 tozS pkp mx15 y3",
-    "tplL": "kS x3 df2_1 mx2 df0_1 k2 y0 x1 ZT0 low km0 Bd df1_1 n2 km12 bU pref x0 x2 k1 mx9 mx10 wo vU mx11 mx5 mx12 km10 kT CL0 g2 mx0 K df3_0 aU kx1 CL1 f2 offU mx6 kx2 ra zd mx7 r16 df2_0 mx4 zm pkM g1 n1 nth junk0 df0_0 spU g3 km8 Xm mx14 toaS rb cS y1 kx3 dvS y2 uS mx3 km2 T16 ab0 ZB junk3 df1_0 aS cm mx8 df3_1 y3 ZT1 zS slU junk2 da kx0 km6 ab1 ab2 t2 amI toK rb16 dl pkA bS topkA mx13 topkK cR eq nS km4 mis posU pkp km14 xw pkB f1 s2 AJ mx1 ab3 mx15 tozS junk1 AI a5 half vF amJ pkK",
-})
-ORDER = {'V': '070c0b0d1x0y1k0h1r0p150o0z0f0q1f181c2s1b132l0r2n192y1h1q1d0u2z1a140v1e2r2o2t431l342v2p102u1g48453c1w3d3f563g57523i0s533j5a3l5b3m3o3p3r3s5e5f4c1i4d414e2q4f1m4g4h464l4j4k4n5m5n6b4p5x6c6v6w4r6x5s515t5u5v4x4y5w4z64506f5o5p6g6h6i6j6k6l6m6n6o6p6q6r6s6t6u6y6z7382838485898b86878g8e8f7c7d7f8h7g8j7i8l7j7l7m7o7p8n7r7s9k9l9s9t8u9o8v9p8w818x8y9x8z9w938o91929597a4a599ataa9faf9g9h9ia6a7abbdauac9jbeadbfaeamaxayazb0b1b2b3b4b5b6b7b8b9babbbgbcbhblckclcmcncocrcpctcybubvcwbxcxbyczc0d1c1d3c3c4d5c6c7c9cae3e2ebeae6dcdde7decjdfeedgdhefd6dldjdkdndpemendrfbesdxexdydze0eofvepfwetfxeufcevewe1f4fffgfhfifjfkflfmfnfofpfqfrfsftfyfufzg3h2h3h4h5h9h6hbh7hggchegdgfhfgghhhjgihlgjglgmgogpgrhngsh1ilikisithuiphviohwhxhyixhziwi3hoi1i2i5i7j4j5i9jtjaifjfigihkdiij6juj7jbijkejmjcjdjejxjykfjzk0k1k2k3k4k5k6k7k8k9kakbkgkckhkllklllmlnlrloltlplykukvlwkxkylxl0lzm1l1m2l3l4l6l7l9m4lan2n1n5n6ndmbm5mcljmdn9menamfmgmknemmmimjmomqnlnrnwnmnsntn0oao3numwnvmxoemyobmzofnnognoohoiojokolomonooopoqorosotovowoxoyozp2p4p0p9p7p8pa',
-         'S': '021j201z27160e1y0w17280l0g1s0k1t121v0i0j262m21300n0m291u220x0t2a232b242c253332312x47113y3v4958544a5c5g5j4s5r4q4u6d6362605y616569686766707274717v7y8p8r8q8s9m9q9u9y9aa1989ca9akagaialajanavaraqapaobibkbmbjcdcgd7d9d8dae4e8ecegdsejdqduerf1f3f2f0eyf5fdf8f7f9f6g0g1g2g4gvhpgyhrhqhsimiqiuiyiaj1i8icj9jijljjjkjgjvjnjpjojrjqkikjkkkmlgldm6m7m9m8n3n7nbnfmrmpninqmtnxo0o1o2nzo4o6o7o8o5ocpdpcpe',
-         'P': '353637443a3b2w393u3x40383w3z3k5i3e55593n3q3h3t4b5d755h4i4m5k5l4o4t4v4w7677888a798c8d7a8i7u7x8m7b7w7e7za0807n7q7k787h7t8t9nbn9r909v949z96a29ba39e9dbscqcsbocucvccd0cfd4cebpeichbwc5btc8bqcibrc2bzcbdbe5e9g5dieddmehdoekdteldwdvgah8hag6hcg7hdguhighg9gxhmh0gbgegkgwgtgzgngqg8htj0kniniri0ivi4izi6j2ibj3ieidkslqlslukolvkplfm0lclhnhm3lekwktl5l8likql2krlbkzman4n8mlmhncmnngmunjnkmsmvp1p3p5p6pb',
-         'G': '081p091o0a1n062d2e2f2g2h2i2j2k426e5z5q6a8ka8ahasawd2eqezfafehkj8jsjhjwnyo9', 'Y': '0001030405npodou'}
-ORDER = {'V': '070b0c1j0d0h1k0p0z0y1l0u1g15101e0q0o1h0r2s2n2r1r1q0f2t2l132u0s2y2v182z2p2o191c431u33320v453c1a1b1d3d1f3f1m533g3i143j3l1i3m52565q57464c2q4d5r4e5v4f5u4g414h1w4l4j4k4n4p4r515d6l5e4x5f614y664z5g62505h6z635i6s64735j675k68705l74695m756a5n5o5p6b6c8a6d6e6f6g767h776i7b8b8j8c8h8d8e8f8o8m8n8p7k7l7n7o8r7q8t7r8z897t8v7u9t9w9xag9s92ah93ak94al958w96979b999a9d9f9hbba39ra49na59oar9pas9qa6biatbpa7auawbta8a9axaabqayabbuazacbvb0adaeafb1b2d0b3b4b5b6bwb7bxb8c1d1d9d2d7d3d4d5dedcdddfcacbdhcddjcecgdpdlchcjckejeiemf7endsf6dtfadudvfbdwczdxdme1dze0e3e5ehe7etg1euedeveefhefewfiegexfjeyfkg8gffmezgjfnf0ggfof1gkfpf2glfqf3f4f5frfshqftfufvfwgmfxgnfygrhrhzhshxhthuhvi4i2i3i5h0h1h3i7h4h6i9h7h9ibifhajcj9j8jdiijxijjwikk0ilk1imhpiniciripiqitivixkrjjj3jkj7j4k7jlj5k8jmj6l5jnk9kcl6jokakyjpkdjql9kejrlakfjslbkgjtjujvkhkikjmgkkklkmlcknldkolhmhmnmimpmjmkmlmsmumtmvlqlrltmxlumylwlxn4n0lznyo2nxm0ommfo1n7oln8opn9oqnanbn1ncngnenfninknmpgo8nso9nwoantowobnuoxocpnpuodp1oenvp2ofpvp3ogoyp4ohp5oiozojokp6p7p8p9pzpapbpcpdq0q1q2q6q3q8q4qdqbqcqe'.replace('6g767h77', '6g766h77'),
-         'S': '02291z1x272028220i1y210j0l0e0n0k120w16260m2a230g2b241s172c1v30252x0t0x34314a3s3p49483y3v4754585s1t5b5w112m4s5z4q4u6k6q6m6p6o6r6t6v6w6x6u7178797c7a807x9086838y8x9y9uaiama19iap9gba9kbfbcbhbebgbnbmbkblbjbrbybzc2c0cqcndqdoctcwdnekeof8erfce8ffe6eag0g6g2g4g5g7g9gdgagcgbghgogpgsgqhdhgighjhmieidjajejyjhk2iyk5iwj0kqkskvkwkxkukzl7l0l2l1l3lelilglfm6n5m3n3mcm9n2nzo3ono6ornnounlnppfphplpmpkpjpoprpqpspppwqhqgqi',
-         'P': '352w36443a3r3o3839403u3b3x3t3e3h3k3q3n373w3z4b5a7d55595t4i4m5x4o4t6j4v5c4w5y608i8g7e7g7i8k8l7f7j8q7z7w8885828u7h7m817p7s877y847v91a0c39v9zaj989can9ea2b99j9l9maoaqd8d6c5c4c6dadbc8dgcpcmc9dkcscvcocrcycicfcucccxclc7dreqgtelepf9dye2esfde4ebe9fzecfefghyhwgugygwi0i1gvgzi6hchfiagxhihlh5hhh2hkhbhejgh8hnihholjjbjfjzioisk3iujiizkpj1j2k4k6mmmolklpmqmrlnlomwm5llm2mzmblvmelslmm8m7mdo5lym1mam4n6o0o4oondnhosnjnopenqo7nrotovq5q7q9qaqf',
-         'G': '08090a1o1p1n062d2e2f2g2h422i2j2k6n656y728sbdavbobsdig3flgegii8ktkbl4l8pipt', 'Y': '0001030405p0pxpy'}
+PAR = {"g": 1.3, "sc": 3.15, "pe": 0.5, "hop": 200, "rem": 540, "lat": 2400,
+       "parts": ((0, 1, 2), (3,)), "kv": 10, "sub": 2, "rv": (3,), "asc": True, "split": True, "zd": "S", "pu": "V", "pb": "P", "dg": ((0, 1), (2,), (3,)),
+       "xs": ((0, 1, "V"), (1, 1, "V"), (2, 1, "V"), (3, 1, "V"), (4, 4, "S"), (8, 4, "S"), (12, 4, "S")), "ys": ((0, 4, "S"), (4, 4, "S"), (8, 4, "S"), (12, 4, "S")),
+       "eng": {"xk": "S", "wk0": "S", "wk1": "S", "zS": "S", "pkB": "S", "pkK": "S", "rb": "V"}}
+PAR["queues"] = {
+    "V": "+sx2 aU +sx1 ra +sx0 n1 x0 n2 g1 g2 g3 spU scB CL1 CL0 bU rb mx0 mx1 k1 mx2 scK mx3 mx4 mx5 mx6 wo mx7 df0_1 mx8 +nth df0_0 df1_0 mx9 df1_1 df2_0 df2_1 kT kS r16 rb16 low ZT0 ZT1 ZB df3_0 vF T16 vU df3_1 cS ab3 eq nS0 pref0 uS cm_0 amI bS_0 amJ f1_0 da nS1 pref1 dl cm_1 t2 bS_1 aS sum1 f1_1 posU f2_1 half offU_1 f2_0 sx15 sx14 s2 sx13 offU_0 sx12 AI sx11 sx10 sx9 sx8 slU sx7 sx6 sx5 AJ sx4 sx3".split(),
+    "S": "+pkA +pkp +pkL +pkB +pkM +pkK +zc +zd +zS x6 x4 x2 y0 y2 mx10 mx12 y4 mx14 ab0 ab1 y6 ab2 a5 bF xw mis0 ob cR zm dvS0 junk0_1 junk0_3 mis1 junk0_0 dvS1 junk0_2 junk1_0 junk1_3 +oz junk1_2 junk1_1".split(),
+    "P": "+ph +pd pc1 pc0 pb pz ps0 kz ps1 pm10 kx8 pw pm12 km2 kx6 km6 km4 pm14 kx0 km12 kx2 km10 km14 km8 kx4 km0 kB da1_0 da1_1 pv pt n0_0 da2_0 pc da2_1 pe pn n1_0 pq0 dl3_0 dl3_1 pu da3_0 da3_1 n0_1 pq1 n1_1".split(),
+    "G": "toK toa toA toP toz".split(),
+    "Y": "ok oa ox".split(),
+}
+del PAR["queues"]
+PAR.update({"kv": 8, "rv": (3, 0), "pb": "P", "pu": "P", "asc": False, "split": False, "parts": ((3, 2, 1), (0,)), "dg": ((3,), (2,), (1,), (0,)), "zd": "V", "sub": 4,
+            "xs": ((0, 1, "V"), (1, 1, "V"), (2, 1, "V"), (3, 1, "V"), (12, 4, "S"), (8, 4, "S"), (4, 4, "S")), "ys": ((12, 4, "S"), (8, 4, "S"), (4, 4, "S"), (0, 4, "S")),
+            "first": ("aU", "ra", "rb", "x0", "x1", "x2", "x3", "x4", "x8", "x12"), "zb": "S", "rows": (0, 7, 3, 4), "slack": 200.0, "near": 300.0})
+PAR["order"] = "mx5 +sx5 df3_0 +mx1 mx6 df3_2 +pd kz k1 +a5 ps1 pc1 +mx4 scB +sx4 scK ra n1 rb kx4 pb kx6 g3 CL0 aU +sx0 +rb16 ps0 wo spU x4 +toA x1 x0 pc0 +g2 mx0 bU vU x3 km12 pw CL1 x12 pm8 df0_1 mx3 n2 mx2 x2 x8 pz pm12 da2_1 toK mx7 df3_1 +df1_3 kS kx0 pm10 df3_3 km0 kx2 km8 ZT1 pv wk1 kT km4 df1_0 ZT0 low +df0_0 +g1 km6 km2 zd ZB pm14 mx8 y12 mx14 wk0 ab2 km10 mx12 dl3_0 y8 mx10 pt y4 df2_0 df2_3 T16 dl3_1 df0_3 da1_1 zm ab1 da1_0 df2_1 pkB da0_0 kB n1_0 da0_1 r16 y0 pkL dl0_1 dl0_0 pA mis0 xk da2_0 dvS0 pc ab3 +df0_2 n1_1 cR km14 n0_0 +ph0 pn df2_2 ab0 da3_1 da3_0 cS pq0 df1_2 pkK df1_1 amJ pu junk0_2 cm_0 +bS_0 n0_1 cm_1 ph1 posU da pref0 sx1 pkM half0 dl nS1 bS_1 f0_0 sx6 junk0_1 eq nS0 junk0_3 amI junk0_0 aS f1_0 t2 toa f0_1 toz pkA sx3 f2_0 f1_1 pkp sx2 AI slU offU_0 toP s2 zS half1 offU_1 mis1 f2_1 sx7 nth +AJ".split()
+PAR["order"] = "x8 x12 dl0_1 kS +pkM g2 +sx7 +pz +toa +cR +dl3_1 +dl0_0 x4 ps1 scB ps0 +df2_1 n2 AJ x2 ra pb aU x0 spU g1 CL0 x3 kz g3 offU_0 pc1 mx10 x1 mx8 posU pm12 k1 bU CL1 pm14 mx12 wo y12 mx1 pc0 rb pw mx0 kx0 km2 mx14 n1 kx4 y8 scK km12 ab3 toK kx6 pm8 pm10 kx2 km4 r16 df1_2 rb16 low mx6 ZT1 ZT0 df1_1 mx4 km0 mx3 km8 df3_3 mx5 df3_0 df3_2 pt y4 km6 mx2 df2_0 df0_0 df3_1 kB mx7 ZB wk0 xk pA pv y0 df2_2 eq vU da2_0 kT df1_0 df2_3 da2_1 km14 da3_0 ab1 a5 ab0 km10 cm_0 half0 df0_3 pc dl3_0 ab2 cS nS0 T16 cm_1 df1_3 da3_1 n0_1 df0_1 amI amJ mis0 df0_2 offU_1 sx4 n0_0 dl s2 nS1 zm n1_0 bS_0 pref0 pkB bS_1 dvS0 ph0 pn sx5 sx3 pd toP f3_0 t2 f4_0 pq0 da f0_0 pkA sx1 f3_1 f1_0 da0_1 slU f1_1 mis1 wk1 da0_0 junk0_2 pkL pkp nth da1_1 ph1 da1_0 n1_1 pu half1 zS +aS junk0_0 sx0 sx6 f2_1 zd toz pkK junk0_1 toA sx2 +f2_0 +AI f0_1 f4_1 junk0_3".split()
+PAR.update({"zd": "S", "zb": "V", "eng": {"xk": "S", "wk0": "S", "wk1": "S", "zS": "S", "pkB": "S", "pkK": "S", "rb": "S"}})
+PAR["queues"] = {
+    "V": "aU +sx0 ra n1 x1 x2 x0 n2 g1 +AJ g2 g3 +nth spU x3 scB CL0 CL1 bU mx0 mx1 k1 mx2 scK mx3 mx4 mx5 wo mx6 df3_2 df3_3 df3_0 df3_1 mx7 df2_0 df2_2 df2_3 df2_1 ab3 kS rb16 low r16 ZT1 ZT0 df1_1 SK ZB df1_3 df1_0 vF T16 vU df0_2 df1_2 df0_0 df0_3 df0_1 cS0 half0 cS1 ab0 eq nS0 cm_0 nS1 pref0 amI bS_0 amJ cm_1 dl da f4_0 f3_0 f0_0 t2 f1_0 half1 aS bS_1 f2_0 posU offU_0 AI f3_1 f4_1 f0_1 sx7 s2 f1_1 sx6 slU f2_1 sx5 sx4 offU_1 sx3 sx2 sx1".split(),
+    "S": "a5 x4 x8 x12 rb y12 y8 bF mx12 mx8 mx14 mx10 y4 y0 ab2 wk0 wk1 xk ab1 cR mis0 mis1 zm dvS0 pkA junk0_2 ob junk0_1 junk0_0 junk0_3 pkp pkB pkL pkM pkK zc ok zd zS".split(),
+    "P": "+pq0 +n0_1 +n1_1 +pu +pd pc0 pc1 pz pb kz ps0 ps1 kx0 pm8 pw pm12 pm10 pm14 km0 km2 km12 km8 kx2 km6 km4 kx4 km14 kx6 km10 kB dl3_0 dl3_1 da3_0 n0_0 pZ da3_1 pv pt pA da2_0 pc da2_1 pn ph0 dl0_0 dl0_1 da1_0 da1_1 da0_0 da0_1 n1_0 ph1".split(),
+    "G": "+toa +toP +toz toK toA".split(),
+    "Y": "+oz oa ox".split(),
+}
 NCH = 4
+HALF = 0.5 - 2.0 ** -11
 CH = 256 // NCH
 A = AluOpType
 AF = ActivationFunctionType
@@ -73,7 +86,7 @@ def build(g, core, T, topo, par):
     last_w, readers, bank_last = {}, {}, {}
     V, S, PE, SY = g.vector, g.scalar, g.tensor, g.sync
 
-    def op(alts, reads, writes, banks=(), ext=(), after=(), lat=0, sem=None, semn=1):
+    def op(alts, reads, writes, banks=(), ext=(), after=(), lat=0, sem=None, semn=1, nm=None):
         i = len(ops)
         deps = {}
         for k in reads:
@@ -102,31 +115,34 @@ def build(g, core, T, topo, par):
             else:
                 bank_last[b] = [i]
         deps.pop(i, None)
-        ops.append({"alts": alts, "deps": deps, "ext": list(ext), "lat": lat, "sem": sem, "semn": semn,
-                    "nm": (list(writes) + ["to" + "".join(reads)[:4]])[0], "t": cur[0]})
+        nm = nm or writes[0]
+        e = par["eng"].get(nm)
+        if e in alts:
+            alts = {e: alts[e]}
+        ops.append({"alts": alts, "deps": deps, "ext": list(ext), "lat": lat, "sem": sem, "semn": semn, "nm": nm, "t": cur[0]})
         return i
 
     def cv(n, half=False):
-        return max(64, n * (0.5 if half else 1.0)) + par["fix"] * 0.5
+        return max(64, n * (0.5 if half else 1.0))
 
-    def vts(out, in0, s1, s2, o0, o1, n, R, W, banks=(), half=False, ext=(), after=()):
+    def vts(out, in0, s1, s2, o0, o1, n, R, W, banks=(), half=False, ext=(), after=(), nm=None):
         if o1 is None:
             f = lambda: V.tensor_scalar(out, in0, s1, None, o0)
         else:
             f = lambda: V.tensor_scalar(out, in0, s1, s2, o0, o1)
         alts = {"V": (cv(n, half), f)}
-        if cur[0] < 0 and o0 == A.mult and W[0] not in ("I16", "BO16", "kc16", "thF") and (o1 is None or (o1 == A.add and isinstance(s2, float))):
+        if cur[0] < 0 and o0 == A.mult and W[0] not in ("I16", "BO16", "hId", "thF") and (o1 is None or (o1 == A.add and isinstance(s2, float))):
             alts["S"] = (cv(n) + 20, lambda: S.activation(out, in0, AF.Copy, bias=s2 or 0.0, scale=s1))
-        return op(alts, R, W, banks, ext, after)
+        return op(alts, R, W, banks, ext, after, nm=nm)
 
-    def vtt(out, in0, in1, o, n, R, W, banks=(), ext=(), after=()):
-        return op({"V": (cv(n if banks else 2 * n), lambda: V.tensor_tensor(out, in0, in1, o))}, R, W, banks, ext, after)
+    def vtt(out, in0, in1, o, n, R, W, banks=(), ext=(), after=(), nm=None):
+        return op({"V": (cv(n if banks else 2 * n), lambda: V.tensor_tensor(out, in0, in1, o))}, R, W, banks, ext, after, nm=nm)
 
-    def vcp(out, in_, n, R, W, banks=(), half=False, ext=(), after=()):
-        return op({"V": (cv(n, half), lambda: V.tensor_copy(out, in_))}, R, W, banks, ext, after)
+    def vcp(out, in_, n, R, W, banks=(), half=False, ext=(), after=(), nm=None):
+        return op({"V": (cv(n, half), lambda: V.tensor_copy(out, in_))}, R, W, banks, ext, after, nm=nm)
 
-    def vscan(out, d0, d1, init, o0, o1, n, R, W, banks=(), half=False):
-        return op({"V": (cv(n, half), lambda: V.tensor_tensor_scan(out, d0, d1, init, o0, o1))}, R, W, banks)
+    def vscan(out, d0, d1, init, o0, o1, n, R, W, banks=(), half=False, nm=None):
+        return op({"V": (cv(n, half), lambda: V.tensor_tensor_scan(out, d0, d1, init, o0, o1))}, R, W, banks, nm=nm)
 
     def vset(ap, val, n, W):
         if W[0] == "ones":
@@ -134,7 +150,7 @@ def build(g, core, T, topo, par):
         return op({"V": (cv(n, True), lambda: V.memset(ap, val)),
                    "S": (cv(n) + 20, lambda: S.activation(ap, T.ones[:, 0:n], AF.Copy, scale=val))}, ["ones"], W)
 
-    def act(out, in_, f, n, R, W, banks=(), bias=None, scale=None, accum=None, gather=False, ext=(), after=()):
+    def act(out, in_, f, n, R, W, banks=(), bias=None, scale=None, accum=None, gather=False, ext=(), after=(), nm=None):
         kw = {}
         if bias is not None:
             kw["bias"] = bias
@@ -142,46 +158,45 @@ def build(g, core, T, topo, par):
             kw["scale"] = scale
         if accum is not None:
             kw["accum_out"] = accum
-        c = n * par["g"] + 80 if gather else cv(n) + 20
-        return op({"S": (c, lambda: S.activation(out, in_, f, **kw))}, R, W, banks, ext, after)
+        c = n * par["g"] + 65 if gather else cv(n) + 20
+        return op({"S": (c, lambda: S.activation(out, in_, f, **kw))}, R, W, banks, ext, after, nm=nm)
 
-    def gath(out, win, off, n, R, W, engs="VS", ext=(), after=()):
+    def gath(out, win, off, n, R, W, engs="VS", ext=(), after=(), nm=None):
         alts = {}
         if "V" in engs:
-            alts["V"] = (n * par["g"] + 60, lambda: V.tensor_copy(out, win.indirect(off)))
+            alts["V"] = (n * par["g"] + 50, lambda: V.tensor_copy(out, win.indirect(off)))
         if "S" in engs:
-            alts["S"] = (n * par["g"] + 80, lambda: S.activation(out, win.indirect(off), AF.Copy))
-        return op(alts, R, W, (), ext, after)
+            alts["S"] = (n * par["g"] + 65, lambda: S.activation(out, win.indirect(off), AF.Copy))
+        return op(alts, R, W, (), ext, after, nm=nm)
 
-    def gtt(out, win, off, in1, o, n, R, W):
-        return op({"V": (n * par["g"] + 60, lambda: V.tensor_tensor(out, win.indirect(off), in1, o))}, R, W)
+    def gtt(out, win, off, in1, o, n, R, W, nm=None):
+        return op({"V": (n * par["g"] + 50, lambda: V.tensor_tensor(out, win.indirect(off), in1, o))}, R, W, nm=nm)
 
-    def scat(win, off, in_, n, R, W, ext=(), after=()):
-        return op({"V": (n * par["sc"] + 60, lambda: V.tensor_copy(win.indirect(off), in_))}, R, W, (), ext, after)
+    def scat(win, off, in_, n, R, W, ext=(), after=(), nm=None):
+        return op({"V": (n * par["sc"] + 50, lambda: V.tensor_copy(win.indirect(off), in_))}, R, W, (), ext, after, nm=nm)
 
-    def mm(lst, R, W, bank, start, stop, ext=(), after=(), nm=""):
-        c = sum(max(64, m[3]) for m in lst) * par["pe"] + 30
+    def mm(nm, lst, R, W, bank, start, stop, ext=(), after=()):
+        c = sum(max(64, m[3]) for m in lst) * par["pe"]
 
         def f():
             r = None
             for j, m in enumerate(lst):
                 r = PE.matmul(m[0], m[1], m[2], start and j == 0, stop and j == len(lst) - 1)
             return r
-        i = op({"P": (c, f)}, R, W, () if bank is None else (bank,), ext, after)
-        if bank is not None:
-            ops[i]["nm"] = W[0] + "<" + R[-1].rstrip("0123456789" if R[-1][0] in "KBzp" else "") + nm
+        i = op({"P": (c, f)}, R, W, () if bank is None else (bank,), ext, after, nm=nm)
+        ops[i]["calls"] = len(lst)
         return i
 
     def pool(c, f, R, W):
         return op({"G": (c, f)}, R, W)
 
-    def dma(q, out, in_, R, W, sem, lat):
+    def dma(q, out, in_, R, W, sem, lat, nm="dma"):
         e = {"Y": SY, "S": S}[q]
-        return op({q: (60, lambda: e.dma_start(out, in_))}, R, W, lat=lat, sem=sem, semn=16)
+        return op({q: (60, lambda: e.dma_start(out, in_))}, R, W, lat=lat, sem=sem, semn=16, nm=nm)
 
     nsent = [0]
 
-    def send(items, R, lat):
+    def send(nm, items, R, lat):
         def f():
             if len(items) == 1:
                 o, src, dst, sem = items[0]
@@ -200,19 +215,27 @@ def build(g, core, T, topo, par):
                 tr.append(RemoteDMATransfer(dst_ids=[DstId(rid=rid, pnc=pid)], dma_engine_mask=m, remote_sem=T.sem[sem], src=src, dst=dst))
             return g.remote_dma_fused(tr, local_sem=T.sem.sent)
         nsent[0] += NE
-        return op({"G": (par["rem"], f)}, R, [], lat=lat, sem="none")
+        return op({"G": (par["rem"], f)}, R, [], lat=lat, sem="none", nm=nm)
 
     NE = len(topo.engines(core, T.cores[(rank + 1) % NR]))
     B = [T["B%d" % i] for i in range(8)]
-    allx = ["x%d" % c for c in range(NCH)]
-    ally = ["y%d" % c for c in range(NCH)]
 
-    dma("Y", T.avI[:], T.av[:], [], ["avI"], "ld0", 2200)
-    dma("Y", T.P[:], T.rp[:], [], ["P"], "ld1", 4500)
-    dma("S", T.X[:, 0:4096], T.ph[:], [], ["Xm"], "ld2", 7000)
+    def cols(b, c0, c1):
+        return B[b][:, c0:c1]
+    allx = ["x%d" % c for c in range(16)]
+    ally = ["y%d" % c for c in range(16)]
+
+    def phrases(nm, lst, base, pieces):
+        for b0, nb, e in pieces:
+            gath(T.XY[:, base + 256 * b0:base + 256 * (b0 + nb)], T.X[:, 0:4096], T[lst][:, 16 * b0:16 * (b0 + nb)], 256 * nb, [lst, "Xm", "Xd"],
+                 ["%s%d" % (nm, b) for b in range(b0, b0 + nb)], e)
+
+    dma("Y", T.avI[:], T.av[:], [], ["avI"], "ld0", 2500)
     dma("Y", T.bvI[:], T.bv[:], [], ["bvI"], "ld3", 2500)
-    dma("Y", T.kcI[:], T.kc[:], [], ["kcI"], "ld4", 5000)
-    dma("Y", T.zb[:, 0:256], T.zs[:], [], ["z0"], "ld5", 5000)
+    dma("Y", T.P[:], T.rp[:], [], ["P"], "ld1", 4500)
+    dma("S", T.X[:, 0:4096], T.ph[:], [], ["Xm"], "ld2", 5500)
+    dma("Y", T.kcI[:], T.kc[:], [], ["kcI"], "ld4", 5500)
+    dma("Y", T.zb[:, 0:256], T.zs[:], [], ["z0"], "ld5", 5500)
     op({"G": (300, lambda: g.dma_start(T.thI[:, 0:1], T.th[:], allow_slow_non_contiguous=True))}, [], ["thI"], lat=3000, sem="ld6", semn=16)
 
     def iota(out, pat, base, cm, n, W, fl=True):
@@ -224,7 +247,7 @@ def build(g, core, T, topo, par):
     vset(T.ones[:], 1.0, 256, ["ones"])
     iota(T["io"][:, 0:1], [[0, 1]], 0, 1, 1, ["io"], False)
     iota(T.tJ[:], [[1, 160]], -16, -1, 160, ["tJ"])
-    iota(T.tI[:], [[0, 16], [1, 16]], 0, 0, 256, ["tI"])
+    iota(T.tI[:], [[0, 24], [1, 16]], 0, 0, 384, ["tI"])
     vts(T.ia[:, 0:1], T["io"][:, 0:1], 15, None, A.bitwise_and, None, 1, ["io"], ["ia0"])
     vts(T.ia[:, 1:2], T["io"][:, 0:1], 16, None, A.bitwise_and, None, 1, ["io"], ["ia1"])
     vcp(col[:, 0:2], T.ia[:, 0:2], 2, ["ia0", "ia1"], ["c0"])
@@ -233,13 +256,14 @@ def build(g, core, T, topo, par):
     vts(T.U64[:], T.tJ[:, 0:144], col[:, 2:3], 64.0, A.is_equal, A.mult, 144, ["tJ", "c2"], ["U64"])
     vts(T.Un32[:], T.U64[:], -0.5, None, A.mult, None, 144, ["U64"], ["Un32"], half=True)
     vts(T.Id[:], T.tJ[:, 16:144], 0.0, None, A.is_equal, None, 128, ["tJ"], ["Id"])
-    for nm, w in (("nId", -1.0), ("hId", 0.5), ("sId", 0.0625), ("xId", 16.0), ("mId", -16.0), ("n240", -240.0), ("I16", 1.0)):
+    for nm, w in (("nId", -1.0), ("hId", HALF), ("sId", 0.03125), ("xId", 15.0), ("tId", 16.0), ("mId", -16.0), ("I16", 1.0)):
         vts(T[nm][:], T.Id[:], w, None, A.mult, None, 128, ["Id"], [nm], half=True)
 
     def DG(U, k):
         return T[U][:, 15 - k:143 - k]
-    vts(T.cS[:, 0:128], T.tJ[:, 16:144], r_, -7.5, A.add, A.add, 128, ["tJ", "c0"], ["cS"])
-    vtt(T.cR[:, 0:128], T.cS[:, 0:128], T.cS[:, 0:128], A.mult, 128, ["cS"], ["cR"])
+    vts(T.kS[:, 0:128], T.tJ[:, 16:144], r_, -7.5, A.add, A.add, 128, ["tJ", "c0"], ["kS"])
+    vtt(T.cR[:, 0:128], T.kS[:, 0:128], T.kS[:, 0:128], A.mult, 128, ["kS"], ["cR"])
+    op({"V": (384, lambda: V.memset(T.cS[:], 0.0))}, [], ["cS0", "cS1", "cSx"])
     vts(T.BO[:], T.cR[:, 0:128], 60.0, None, A.is_lt, None, 128, ["cR"], ["BO"])
     vts(T.BO16[:], T.BO[:], 1.0, None, A.mult, None, 128, ["BO"], ["BO16"], half=True)
     vts(T.BOs[:], T.BO[:], 0.0625, None, A.mult, None, 128, ["BO"], ["BOs"], half=True)
@@ -248,53 +272,71 @@ def build(g, core, T, topo, par):
         vts(T.kT[:, 0:128], T.tI[:, 0:128], float(KV), -32.0, A.is_lt, A.mult, 128, ["tI"], ["kT"])
         vtt(T.ZC[:], T.kT[:, 0:128], T.BO[:], A.mult, 128, ["kT", "BO"], ["ZC"])
     vts(col[:, 3:4], r_, 2.0, 1.0, A.mult, A.add, 1, ["c0"], ["c3"])
-    vts(T.Wu[:], T.BO[:], col[:, 3:4], None, A.mult, None, 128, ["BO", "c3"], ["Wu"], half=True)
-    vts(col[:, 4:5], r_, 1.0, 65536.0, A.is_equal, A.mult, 1, ["c0"], ["c4"])
-    vts(col[:, 5:6], r_, 2.0, 2048.0, A.is_equal, A.mult, 1, ["c0"], ["c5"])
-    vtt(col[:, 6:7], col[:, 4:5], col[:, 5:6], A.add, 1, ["c4", "c5"], ["c6"])
-    vts(T.WC[:], T.BO[:], col[:, 6:7], None, A.mult, None, 128, ["BO", "c6"], ["WC"], half=True)
-    vts(T.uS[:, 0:128], T.tI[:, 0:128], 2.0, -15.0, A.mult, A.add, 128, ["tI"], ["uS"])
-    vts(T.nS[:, 0:128], T.uS[:, 0:128], col[:, 5:6], col[:, 4:5], A.mult, A.subtract, 128, ["uS", "c5", "c4"], ["nS"])
-    vtt(T.WT[:], T.nS[:, 0:128], T.BO[:], A.mult, 128, ["nS", "BO"], ["WT"])
-    vts(col[:, 7:8], col[:, 1:2], 0.0, None, A.is_equal, None, 1, ["c0"], ["c7"])
-    vts(col[:, 8:9], col[:, 1:2], 0.0625, None, A.mult, None, 1, ["c0"], ["c8"])
-    vts(col[:, 9:11], col[:, 7:9], 16.0, None, A.mult, None, 2, ["c7", "c8"], ["c9"])
-    for j in range(4):
-        vts(T.Vs[:, 160 * j:160 * j + 160], T.tJ[:], 0.0, col[:, 7 + j:8 + j], A.is_equal, A.mult, 160, ["tJ", "c7", "c8", "c9"], ["Vs%d" % j])
-
-    def SW(h, g2, big):
-        o = 160 * (h + 2 * big) + 16 - 16 * (g2 - h)
-        return T.Vs[:, o:o + 128]
-    vts(T.tri[:], T.tI[:], r_, 8192.0, A.is_gt, A.mult, 256, ["tI", "c0"], ["tri"])
-    vts(T.cmk[:], T.tri[:], 1.1875, 16.0, A.max, A.min, 256, ["tri"], ["cmk"], half=True)
-    vts(T.R2[:], T.tI[:], r_, 1048576.0, A.is_le, A.mult, 256, ["tI", "c0"], ["R2"])
-    vts(T.R1[:], T.tI[:], 0.0, 1048576.0, A.is_equal, A.mult, 256, ["tI"], ["R1"])
-    vts(T.R3[:], T.tI[:], 0.0, 2.0, A.not_equal, A.mult, 256, ["tI"], ["R3"])
-    vts(T.dg[:], T.tI[:], r_, None, A.is_equal, None, 256, ["tI", "c0"], ["dg"])
+    if par["pu"] == "P":
+        vts(T.Wu[:], T.tJ[:, 0:144], col[:, 2:3], col[:, 3:4], A.is_equal, A.mult, 144, ["tJ", "c2", "c3"], ["Wu"])
+    else:
+        vts(T.Wu[:, 0:128], T.BO[:], col[:, 3:4], None, A.mult, None, 128, ["BO", "c3"], ["Wu"], half=True)
+    iota(T.nS[:, 0:128], [[2, 8], [0, 16]], 0, -1, 128, ["nS0"])
+    vts(T.nS[:, 128:256], T.nS[:, 0:128], 0.0, 131072.0, A.is_equal, A.mult, 128, ["nS0"], ["nS1"])
+    vts(col[:, 5:6], T["io"][:, 0:1], 1.0, 4096.0, A.is_equal, A.mult, 1, ["io"], ["c5"])
+    vts(col[:, 6:7], col[:, 5:6], -39.0, None, A.mult, None, 1, ["c5"], ["c6"])
+    vts(T.WC[:], T.nS[:, 128:256], col[:, 6:7], None, A.add, None, 128, ["nS1", "c6"], ["WC"])
+    vts(T.kS[:, 128:256], T.tI[:, 0:128], 32.0, col[:, 5:6], A.add, A.mult, 128, ["tI", "c5"], ["kT2"])
+    vtt(T.WT[:], T.kS[:, 128:256], T.nS[:, 128:256], A.subtract, 128, ["kT2", "kS", "nS1"], ["WT"])
+    vts(T.tri[:], T.tI[:, 0:256], r_, 8192.0, A.is_gt, A.mult, 256, ["tI", "c0"], ["tri"])
+    spans = [(2 * min(cs), 2 * max(cs) + 2) for cs in par["parts"]]
+    for pi, (w0, w1) in enumerate(spans):
+        vts(T.cmk[:, 48 * w0:16 * w0 + 32 * w1], T.tri[:, 0:32 * (w1 - w0)], 1.1875, 16.0, A.max, A.min, 256, ["tri"], ["cmk_%d" % pi], half=True)
+        vset(T.cmk[:, 16 * w0 + 32 * w1:48 * w1], 1.1875, 16 * (w1 - w0), ["cmj_%d" % pi])
+    vts(T.R2[:], T.tI[:], r_, 1048576.0, A.is_le, A.mult, 384, ["tI", "c0"], ["R2"])
+    vts(T.bS[:, 0:256], T.tI[:, 0:256], 0.0, 1048576.0, A.is_equal, A.mult, 256, ["tI"], ["bS_0", "bS_1"], nm="uS")
+    vts(T.R1[:], T.bS[:, 0:256], 1.0, -1.0, A.mult, A.add, 256, ["bS_0", "bS_1"], ["R1"])
+    vts(T.R3[:], T.tI[:], 0.0, 2.0, A.not_equal, A.mult, 384, ["tI"], ["R3"])
+    vts(T.dg[:], T.tI[:, 0:256], r_, None, A.is_equal, None, 256, ["tI", "c0"], ["dg"])
     vscan(T.pw[:], T.R3[:, 0:16], T.dg[:, 0:16], 0.0, A.mult, A.add, 16, ["R3", "dg"], ["pw"])
-    vset(T.q25[:], -0.25, 256, ["q25"])
-    vts(col[:, 11:12], r_, -8.46875, None, A.add, None, 1, ["c0"], ["c11"])
-    vts(T.kc16[:], T.ones[:], col[:, 11:12], None, A.mult, None, 256, ["ones", "c11"], ["kc16"], half=True)
+    vset(col[:, 14:15], 0.1875, 1, ["c14"])
     vts(col[:, 12:13], r_, 4096.0, None, A.add, None, 1, ["c0"], ["c12"])
+    vts(col[:, 13:14], r_, 4112.0, None, A.add, None, 1, ["c0"], ["c13"])
     NSUB = par["sub"]
     DCH = CH // NSUB
     iota(T.wc[:], [[0, 256 // DCH], [16, DCH]], 0, 0, 256, ["wc"])
     iota(T.bcF[:, 0:16], [[16, 16]], 15, 0, 16, ["bc0"])
     iota(T.bcF[:, 16:48], [[1, 32]], 0, 0, 32, ["bc1"])
-    vcp(T.bcU[:], T.bcF[:], 48, ["bc0", "bc1"], ["bcU"])
+    for pi, (w0, w1) in enumerate(spans):
+        iota(T.bcF[:, 48 + 3 * w0:48 + w0 + 2 * w1], [[16, 2 * (w1 - w0)]], 48 * w0 + 15, 0, 16, ["bc2%d" % pi])
+        iota(T.bcF[:, 48 + w0 + 2 * w1:48 + 3 * w1], [[32, w1 - w0]], 48 * w0 + 31, 0, 8, ["bc3%d" % pi])
+    vcp(T.bcU[:], T.bcF[:], 72, ["bc0", "bc1", "bc20", "bc21", "bc30", "bc31"], ["bcU"])
     vts(T.lC[:], T.bcF[:, 0:16], r_, -15.0, A.add, A.add, 16, ["bc0", "c0"], ["lC"])
-    vts(T.vC[:, 0:16], T.lC[:], 16.0, 8.0, A.mult, A.add, 16, ["lC"], ["vC0"])
-    vts(T.vC[:, 16:32], T.lC[:], 16.0, 4103.5, A.mult, A.add, 16, ["lC"], ["vC1"])
+    vts(T.vC[:, 0:16], T.lC[:], 1.0, None, A.add, None, 16, ["lC"], ["vC0"])
+    for pi, cs in enumerate(par["parts"]):
+        q0, q1 = 4 * min(cs), 4 * max(cs) + 4
+        vts(T.vC[:, 16 + q0:16 + q1], T.lC[:, q0:q1], -2.0 - 16 * q0, None, A.add, None, 16, ["lC"], ["vC%d" % (pi + 1)])
     vts(T.jC[:, 0:4], T.lC[:, 0:4], 2.0, 1.0, A.mult, A.add, 4, ["lC"], ["jC0"])
     vts(T.jC[:, 4:8], T.lC[:, 0:4], -2.0, -1.0, A.mult, A.add, 4, ["lC"], ["jC1"])
     vts(T.jC[:, 8:12], T.lC[:, 0:4], 256.0, None, A.add, None, 4, ["lC"], ["jC2"])
-    vset(T.ZT[:], 0.0, 256, ["ZT0", "ZT1", "ZT2"])
-    vset(T.ZT[:, 2:256:16], 1.0, 16, ["ZT2"])
-    vset(T.X[:, 4096:4112], 0.0, 16, ["Xd"])
+    vset(T.ZT[:, 17:48:2], 1.0, 16, ["ZT2"])
+    iota(T.ia[:, 4:5], [[0, 1]], 128, -1, 1, ["ia4"], False)
+    vts(T.ia[:, 8:9], T["io"][:, 0:1], 4, None, A.arith_shift_right, None, 1, ["io"], ["ia8"])
+    vts(T.ia[:, 9:10], T["io"][:, 0:1], 8, None, A.bitwise_and, None, 1, ["io"], ["ia9"])
+    vtt(T.ia[:, 10:11], T.ia[:, 8:9], T["io"][:, 0:1], A.add, 1, ["ia8", "io"], ["ia10"])
+    vtt(T.ia[:, 11:12], T.ia[:, 8:9], T.ia[:, 4:5], A.add, 1, ["ia8", "ia4"], ["ia11"])
+    vts(T.ia[:, 12:14], T.ia[:, 10:12], 7, None, A.bitwise_and, None, 2, ["ia10", "ia11"], ["ia12"])
+    vcp(col[:, 7:8], T.ia[:, 9:10], 1, ["ia9"], ["c7"])
+    vts(col[:, 8:10], T.ia[:, 12:14], col[:, 7:8], None, A.add, None, 2, ["ia12", "c7"], ["c8"])
+    vcp(col[:, 16:20:2], col[:, 8:10], 2, ["c8"], ["c16"])
+    vts(col[:, 17:18], col[:, 8:9], 2.0, 16.0, A.mult, A.add, 1, ["c8"], ["c17"])
+    vts(col[:, 19:20], col[:, 9:10], 16.0, None, A.add, None, 1, ["c8"], ["c19"])
+    vcp(T.skU[:], col[:, 16:20], 4, ["c16", "c17", "c19"], ["skU"])
+    vset(T.skW[:, 0:16], 1.0, 16, ["skW0"])
+    vset(T.skW[:, 16:32], 32.0, 16, ["skW1"])
+    gath(T.vD[:], T.vC[:], T.skU[:, 2:4], 32, ["skU", "vC0", "vC1", "vC2"], ["vD"], "V")
+    for j, nm in enumerate(("Id2a", "Id2b")):
+        vts(T.Id2[:, 128 * j:128 * j + 128], T.Id[:], 1.0, None, A.mult, None, 128, ["Id"], [nm], half=True)
+    vset(T.X[:, 4096:4128], 0.0, 32, ["Xd"])
     vset(T.mis[:, 256:272], 0.0, 16, ["misd"])
     for t in range(ST):
         vset(T.pkS[:, PKW * t + 128:PKW * t + 136], 0.0, 8, ["pkp%d" % t])
-    vts(col[:, 15:16], r_, 16.0, None, A.mult, None, 1, ["c0"], ["c15"])
+    vts(col[:, 15:16], r_, 16.0, -15.0, A.mult, A.add, 1, ["c0"], ["c15"])
     vset(T.KB[:, 256:320], 0.0, 64, ["Kd0"])
     for t in range(ST):
         vset(T.KB[:, KBW * t + 576:KBW * t + 640], 0.0, 64, ["Be%d" % t])
@@ -305,17 +347,18 @@ def build(g, core, T, topo, par):
     vcp(T.aF[:, 0:16], T.avI[:], 16, ["avI"], ["a0"])
     vts(T.s1[:], T.lC[:], 2.0, None, A.mult, None, 16, ["lC"], ["s1"])
     vcp(T.bU[:], T.bvI[:], 16, ["bvI"], ["bU"])
-    vcp(T.KB[:, 0:256], T.kcI[:], 256, ["kcI"], ["K0"])
-    vts(T.thF[:, 0:1], T.thI[:, 0:1], -1.0, -0.5, A.mult, A.add, 1, ["thI"], ["thF"])
-    vcp(T.nth[:, 0:1], T.thF[:, 0:1], 1, ["thF"], ["nth"])
     vts(T.hJ[:, 0:16], T.bvI[:], 992, None, A.bitwise_and, None, 16, ["bvI"], ["hJ0"])
     vts(T.hJ[:, 16:32], T.bvI[:], 31, None, A.bitwise_and, None, 16, ["bvI"], ["hJ1"])
     vcp(T.hl[:], T.hJ[:], 32, ["hJ0", "hJ1"], ["hl"])
     for j in range(2):
         gtt(T.hm[:, 256 * j:256 * j + 256], T.hl[:, 0:32], T.bcU[:, 16 + 16 * j:32 + 16 * j], T.dg[:], A.mult, 256, ["hl", "bcU", "dg"], ["hm%d" % j])
-    mm([(B[7][:, 0:256], DG("U64", 0), T.hm[:, 0:256], 256), (B[7][:, 0:256], DG("U64", 1), T.hm[:, 256:512], 256)],
-       ["hm0", "hm1", "U64"], ["b7"], 7, True, True)
-    act(T.KB[:, 320:576], B[7][:, 0:256], AF.Copy, 256, ["b7"], ["Bd0"], (7,), scale=1.0 / 64)
+    mm("hm", [(B[3][:, 0:256], DG("U64", 0), T.hm[:, 0:256], 256), (B[3][:, 0:256], DG("U64", 1), T.hm[:, 256:512], 256)],
+       ["hm0", "hm1", "U64"], ["b3"], 3, True, True)
+    act(T.KB[:, 320:576], B[3][:, 0:256], AF.Copy, 256, ["b3"], ["Bd0"], (3,), scale=1.0 / 64)
+    cur[0] = 0
+    vts(T.thF[:, 0:1], T.thI[:, 0:1], -1.0, -0.5, A.mult, A.add, 1, ["thI"], ["thF"], nm="g1")
+    vcp(T.nth[:, 0:1], T.thF[:, 0:1], 1, ["thF"], ["nth"], nm="k1")
+    vcp(T.KB[:, 0:256], T.kcI[:], 256, ["kcI"], ["K0"], nm="n1")
 
     M32 = 1.5 * 2 ** 28
     M1 = 1.5 * 2 ** 23
@@ -346,26 +389,38 @@ def build(g, core, T, topo, par):
         vtt(T.g2[:], T.g1[:], o[:, own + 128:own + 132], A.add, 4, ["g1"] + oR("p"), ["g2"], ext=oE, after=oA)
         vtt(T.g3[:], T.g2[:], T.jC[:, 8:12], A.min, 4, ["g2", "jC2"], ["g3"])
         vcp(T.spU[:], T.g3[:], 4, ["g3"], ["spU"])
+        scat(T.KB[:, ko + 320:ko + 640], T.spU[:], m[:, own + 144:own + 208], 64, ["spU", "Be%d" % tk], ["Bd%d" % tk, "Be%d" % tk], ext=kE + mE, after=kA + mA, nm="scB")
+        if par["pb"] == "P":
+            mm("pb", [(B[5][:, 288:304], DG("U64", j), T.KB[:, ko + 320 + j:ko + 576:16], 16) for j in range(16)], ["U64", "Bd%d" % tk], ["b5b"], 5, True, True)
+            if last:
+                act(T.bF[:], B[5][:, 288:304], AF.Copy, 16, ["b5b"], ["bF"], (5,), scale=1.0 / 64)
+            else:
+                vts(T.bU[:], B[5][:, 288:304], 1.0 / 64, None, A.mult, None, 16, ["b5b"], ["bU"], (5,))
+        else:
+            mm("pa", [(B[5][:, 0:256], T.Id[:], T.tri[:], 256)], ["Id", "tri"], ["b5"], 5, True, False)
+            mm("pb", [(B[5][:, 0:256], T.BO[:], T.KB[:, ko + 320:ko + 576], 256)], ["BO", "Bd%d" % tk], ["b5"], 5, False, True)
+            vscan(T.uS[:], T.R2[:], B[5][:, 0:256], 0.0, A.add, A.min, 256, ["R2", "b5"], ["uS"], (5,), nm="bT")
+            if last:
+                act(T.bF[:], T.uS[:, 15:256:16], AF.Copy, 16, ["uS"], ["bF"])
+            else:
+                vcp(T.bU[:], T.uS[:, 15:256:16], 16, ["uS"], ["bU"])
         Ko, Km = o[:, own + 64:own + 128], m[:, own + 208:own + 272]
         for hb in range(2):
             bk = 3 + hb
             lst = []
             for j in range(8):
-                lst.append((B[bk][:, 64 * j:64 * j + 64], T.mId[:], Ko, 64))
+                lst.append((cols(bk, 64 * j, 64 * j + 64), T.mId[:], Ko, 64))
                 mi = 8 * hb + j
-                lst.append((B[bk][:, 64 * j:64 * j + 64], T.SEL[:, 128 * mi:128 * mi + 128], Km, 64))
-            mm(lst, ["SEL%d" % j for j in range(8)] + ["mId"] + oR("K"), ["b%d" % bk], bk, True, True, ext=oE + mE, after=oA + mA)
-            vts(T.CL[:, 512 * hb:512 * hb + 512], B[bk][:], 0.0, 16.0, A.max, A.min, 512, ["b%d" % bk], ["CL%d" % hb], (bk,))
-        mm([(B[6][:, 0:64], T.xId[:], Ko, 64), (B[6][:, 0:64], T.nId[:], Ko, 64), (B[6][:, 0:64], T.n240[:], T.ones[:, 0:64], 64)] +
+                lst.append((cols(bk, 64 * j, 64 * j + 64), T.SEL[:, 128 * mi:128 * mi + 128], Km, 64))
+            mm("pc%d" % hb, lst, ["SEL%d" % j for j in range(8)] + ["mId"] + oR("K"), ["b%d" % bk, "b%du" % bk], bk, True, True, ext=oE + mE, after=oA + mA)
+            vts(T.CL[:, 512 * hb:512 * hb + 512], B[bk][:], -15.0, 1.0, A.max, A.min, 512, ["b%d" % bk], ["CL%d" % hb], (bk,))
+        mm("ps0", [(B[6][:, 0:64], T.xId[:], Ko, 64)] +
            [(B[6][:, 0:64], T.Id[:], T.CL[:, 64 * j:64 * j + 64], 64) for j in range(8)],
-           ["xId", "nId", "n240", "Id", "CL0"] + oR("K"), ["b6"], 6, True, False, ext=oE, after=oA)
-        mm([(B[6][:, 0:64], T.Id[:], T.CL[:, 64 * j:64 * j + 64], 64) for j in range(8, 16)], ["CL1"], ["b6"], 6, False, True)
+           ["xId", "Id", "CL0"] + oR("K"), ["b6"], 6, True, False, ext=oE, after=oA)
+        mm("ps1", [(B[6][:, 0:64], T.Id[:], T.CL[:, 64 * j:64 * j + 64], 64) for j in range(8, 16)], ["CL1"], ["b6"], 6, False, True)
         vtt(T.k1[:], B[6][:, 0:64], o[:, own:own + 64], A.mult, 64, ["b6"] + oR("M"), ["k1"], (6,), ext=oE, after=oA)
-        vtt(T.k2[:], T.k1[:], Ko, A.add, 64, ["k1"] + oR("K"), ["k2"])
-        scat(T.KB[:, ko + 320:ko + 640], T.spU[:], m[:, own + 144:own + 208], 64, ["spU", "Be%d" % tk], ["Bd%d" % tk, "Be%d" % tk], ext=kE + mE, after=kA + mA)
-        scat(T.KB[:, ko:ko + 320], T.spU[:], T.k2[:], 64, ["spU", "k2"], ["K%d" % tk, "Kd%d" % tk], ext=kE, after=kA)
-        mm([(B[6][:, 64:80], DG("U64", j), T.KB[:, ko + 320 + j:ko + 576:16], 16) for j in range(16)], ["U64", "Bd%d" % tk], ["b6b"], 6, True, True)
-
+        op({"V": (64 * par["sc"] + 50, lambda: V.tensor_tensor(T.KB[:, ko:ko + 320].indirect(T.spU[:]), T.k1[:], Ko, A.add))},
+           ["spU", "k1"] + oR("K"), ["K%d" % tk, "Kd%d" % tk], (), kE, kA, nm="scK")
 
     for t in range(ST):
         last = t == ST - 1
@@ -381,268 +436,363 @@ def build(g, core, T, topo, par):
         vcp(T.aU[:], aF, 16, aR, ["aU"], ext=aE, after=aA)
         gath(T.ra[:], T.P[:], T.aU[:], 256, ["P", "aU"], ["ra"], "V")
         act(T.a5[:], aF, AF.Copy, 16, aR, ["a5"], scale=5.0, ext=aE, after=aA)
-        for c in range(NCH):
-            gath(T.XY[:, 16 * CH * c:16 * CH * (c + 1)], T.X[:, 0:4096], T.ra[:, CH * c:CH * (c + 1)], 16 * CH, ["ra"] + Xr, ["x%d" % c])
-        mm([(B[1][:, 0:256], T.I16[:], T.kc16[:], 256)], ["I16", "kc16"], ["b1", "b1s"], 1, True, False)
+        phrases("x", "ra", 0, par["xs"])
+        if t > 0:
+            patch(t - 1, t, False)
+        Kt, Bt = "K%d" % t, "Bd%d" % t
+        if not last:
+            snd["K", t] = send("toK", [(1, T.KB[:, ko:ko + 576], T.KB[:, ko + KBW:ko + KBW + 576], "rK%d" % (t + 1))], [Kt, Bt, "Kd%d" % t], par["lat"] + 2500)
+        gath(T.rb[:], T.P[:], T.bU[:], 256, ["P", "bU"], ["rb"], "VS")
+        mm("pw", [(B[6][:, 256:512], T.Id[:], T.wc[:], 256), (B[6][:, 256:512], T.Id[:], K, 256)], ["Id", "wc", Kt], ["b6c"], 6, True, True)
+        vcp(T.wo[:], B[6][:, 256:512], 256, ["b6c"], ["wo"], (6,))
+        vts(T.rb16[:], T.rb[:], -2048.0, None, A.add, None, 256, ["rb"], ["rb16"], half=True)
+        phrases("y", "rb", 4096, par["ys"])
         parts = []
-        if KV > 0:
-            mm([(B[2][:, 0:256], T.Id[:], z, 256)], ["Id"] + zR, ["b2"], 2, True, True, zE, zA)
-            mm([(B[1][:, 0:256], T.ZC[:], z, 256)], ["ZC", "b1s"] + zR, ["kz"], None, False, False, zE, zA)
-            parts.append("kz")
-            for c in range(NCH):
-                mm([(B[1][:, CH * c:CH * (c + 1)], DG("Un32", j), T.XY[:, 16 * CH * c + j:16 * CH * (c + 1):16], CH) for j in range(KV)],
-                   ["Un32", "b1s", "x%d" % c], ["kx%d" % c], None, False, False)
-                parts.append("kx%d" % c)
+        mm("pz", [(B[2][:, 0:256], T.Id[:], z, 256)], ["Id"] + zR, ["b2"], 2, True, True, zE, zA)
+        mm("kz", [(B[1][:, 128 * h:128 * h + 128], T.zb[:, 256 * t + 128 * h:256 * t + 128 * h + 128], T.ZC[:], 128) for h in range(2)], ["ZC"] + zR, ["b1", "b1s"], 1, True, False, zE, zA)
+        for c in range(0, KV, 2):
+            mm("kx%d" % c, [(B[1][:, 128 * h + j:128 * h + 128:16], T.XY[:, 2048 * h + j:2048 * h + 2048:16], T.Un32[:, 15:143:16], 8) for j in (c, c + 1) for h in range(2)],
+               ["Un32", "b1s"] + allx, ["kx%d" % c], None, False, False)
+            parts.append("kx%d" % c)
         for k in range(0, 16, 2):
             if k < KV:
                 for j in (k, k + 1):
                     vtt(T.MX[:, 256 * j:256 * j + 256], T.XY[:, j:4096:16], B[2][:, 0:256], A.max, 256, allx + ["b2"], ["mx%d" % j], (2,))
             else:
-                bk = (0, 7, 2)[(k // 2) % (2 if KV else 3)]
-                mm([m for j in (0, 1) for m in ((B[bk][:, 256 * j:256 * j + 256], T.nId[:], z, 256),
-                                                (B[bk][:, 256 * j:256 * j + 256], T.Id[:], T.XY[:, k + j:4096:16], 256))],
-                   zR + allx + ["Id", "nId"], ["b%d" % bk, "b%db" % bk], bk, True, True, zE, zA, nm=str(k))
+                bk = par["rows"][(k - KV) // 2 % len(par["rows"])]
+                mm("pm%d" % k, [m for j in (0, 1) for m in ((cols(bk, 256 * j, 256 * j + 256), T.nId[:], z, 256),
+                                                           (cols(bk, 256 * j, 256 * j + 256), T.Id[:], T.XY[:, k + j:4096:16], 256))],
+                   zR + allx + ["Id", "nId"], ["b%d" % bk, "b%db" % bk, "b%du" % bk], bk, True, True, zE, zA)
                 act(T.MX[:, 256 * k:256 * k + 512], B[bk][:], AF.Abs, 512, ["b%d" % bk, "b%db" % bk], ["mx%d" % k, "mx%d" % (k + 1)], (bk,), scale=0.5)
-            mm([(B[1][:, 0:256], DG("U64", j), T.MX[:, 256 * j:256 * j + 256], 256) for j in (k, k + 1)],
+            mm("km%d" % k, [(B[1][:, 128 * h + j:128 * h + 128:16], T.MX[:, 256 * j + 128 * h:256 * j + 128 * h + 128], T.U64[:, 15:143:16], 8) for j in (k, k + 1) for h in range(2)],
                ["U64", "b1s", "mx%d" % k, "mx%d" % (k + 1)], ["km%d" % k], None, False, False)
             parts.append("km%d" % k)
-        mm([(B[5][:, 0:256], T.Id[:], T.q25[:], 256), (B[5][:, 0:256], T.hId[:], z, 256), (B[5][:, 0:256], T.hId[:], T.XY[:, 0:4096:16], 256)],
-           ["Id", "hId", "q25"] + allx + zR, ["b5"], 5, True, True, zE, zA)
-        vts(T.ZW[:, 1:512:2], B[5][:, 0:256], M1, M1, A.add, A.subtract, 256, ["b5"], ["zd"], (5,))
-        if t > 0:
-            patch(t - 1, t, False)
-            vts(T.bU[:], B[6][:, 64:80], 1.0 / 64, None, A.mult, None, 16, ["b6b"], ["bU"], (6,))
-        Kt, Bt = "K%d" % t, "Bd%d" % t
-        if not last:
-            snd["K", t] = send([(1, T.KB[:, ko:ko + 576], T.KB[:, ko + KBW:ko + KBW + 576], "rK%d" % (t + 1))], [Kt, Bt, "Kd%d" % t], par["lat"] + 2500)
-        gath(T.rb[:], T.P[:], T.bU[:], 256, ["P", "bU"], ["rb"], "V")
-        mm([(B[6][:, 256:512], T.Id[:], T.wc[:], 256), (B[6][:, 256:512], T.Id[:], K, 256)], ["Id", "wc", Kt], ["b6c"], 6, True, True)
-        vcp(T.wo[:], B[6][:, 256:512], 256, ["b6c"], ["wo"], (6,))
-        vts(T.rb16[:], T.rb[:], -2048.0, None, A.add, None, 256, ["rb"], ["rb16"], half=True)
-        for c in range(NCH):
-            gath(T.XY[:, 4096 + 16 * CH * c:4096 + 16 * CH * (c + 1)], T.X[:, 0:4096], T.rb[:, CH * c:CH * (c + 1)], 16 * CH, ["rb"] + Xr, ["y%d" % c])
-        mm([(B[1][:, 0:256], T.sId[:], K, 256)], ["sId", Kt] + parts, ["b1"], 1, False, True)
-        op({"V": (cv(256), lambda: V.transpose(T.kT[:], B[1][:, 0:256]))}, ["b1"], ["kT"], (1,))
-        vscan(T.kS[:], T.R1[:], T.kT[:], 0.0, A.add, A.min, 256, ["R1", "kT"], ["kS"])
+        mm("kB", [(B[1][:, 128 * h:128 * h + 128], T.KB[:, ko + 128 * h:ko + 128 * h + 128], T.sId[:], 128) for h in range(2)], ["sId", Kt] + parts, ["b1"], 1, False, True)
+        vscan(T.kS[:], T.R1[:], B[1][:, 0:256], 0.0, A.add, A.min, 256, ["R1", "b1"], ["kS"], (1,))
         k16 = T.kS[:, 15:256:16]
         vts(T.r16[:], k16, M32, M32, A.add, A.subtract, 16, ["kS"], ["r16"])
-        vtt(T.low[:], k16, T.r16[:], A.subtract, 16, ["kS", "r16"], ["low"])
-        vts(T.ZT[:, 0:256:16], T.low[:], M1, M1, A.add, A.subtract, 16, ["low"], ["ZT0"])
-        vtt(T.ZT[:, 1:256:16], T.low[:], T.ZT[:, 0:256:16], A.subtract, 16, ["low", "ZT0"], ["ZT1"])
-        mm([(B[5][:, 256 + 16 * big + h:272 + 16 * big:2], SW(h, g2, big), T.ZT[:, 16 * g2 + big:256:32], 8)
-            for big in range(2) for h in range(2) for g2 in range(2)], ["ZT0", "ZT1", "Vs0", "Vs1", "Vs2", "Vs3"], ["b5v"], 5, True, True)
-        vtt(T.vF[:], B[5][:, 256:288], T.vC[:], A.add, 32, ["b5v", "vC0", "vC1"], ["vF"], (5,))
-        vcp(T.vU[:], T.vF[:], 32, ["vF"], ["vU"])
-        op({"V": (cv(256, True), lambda: V.transpose(T.ZB[:], T.ZT[:]))}, ["ZT0", "ZT1", "ZT2"], ["ZB"])
-        mm([(B[3][:, 0:256], T.I16[:], T.rb16[:], 256), (B[3][:, 0:256], T.WT[:], T.ZB[:], 256)], ["I16", "rb16", "WT", "ZB"], ["b3"], 3, True, True)
+        vts(T.low[:], k16, M1, M1 + 1, A.add, A.subtract, 16, ["kS"], ["low"])
+        vtt(T.ZT[:, 0:16], T.low[:], T.r16[:], A.subtract, 16, ["low", "r16"], ["ZT0"])
+        vtt(T.ZT[:, 16:48:2], k16, T.low[:], A.subtract, 16, ["kS", "low"], ["ZT1"])
+        gtt(T.SK[:], T.ZT[:], T.skU[:, 0:2], T.skW[:], A.mult, 32, ["ZT0", "ZT1", "ZT2", "skU", "skW0", "skW1"], ["SK"])
+        mm("pv", [(B[5][:, 256:288], T.tId[:], T.vD[:], 32)] + [(B[5][:, 256 + j:288:8], T.Id2[:, 128 - 16 * j:256 - 16 * j], T.SK[:, j:32:8], 4) for j in range(8)],
+           ["SK", "Id2a", "Id2b", "tId", "vD"], ["b5v"], 5, True, True)
+        vcp(T.vF[:], B[5][:, 256:288], 32, ["b5v"], ["vF"], (5,))
+        gath(T.vU[:], T.vF[:], T.skU[:, 2:4], 32, ["vF", "skU"], ["vU"], "V")
+        mm("pZ", [(B[3][0:16, 256 + 128 * h:384 + 128 * h], T.ZT[:, 16 + 16 * h:32 + 16 * h], T.Id[:], 128) for h in range(2)], ["ZT1", "ZT2", "Id"], ["b3u"], 3, True, True)
+        if par["zb"] == "S":
+            act(T.ZB[0:16], B[3][0:16, 256:512], AF.Copy, 256, ["b3u"], ["ZB"], (3,))
+        else:
+            vcp(T.ZB[0:16], B[3][0:16, 256:512], 256, ["b3u"], ["ZB"], (3,))
+        mm("pt", [(B[3][:, 0:256], T.I16[:], T.rb16[:], 256), (B[3][:, 0:256], T.WT[0:16, :], T.ZB[0:16], 256)], ["I16", "rb16", "WT", "ZB"], ["b3"], 3, True, True)
         vts(T.T16[:], B[3][:, 0:256], -2048.0, 2048.0, A.max, A.min, 256, ["b3"], ["T16"], (3,))
-        mm([(B[4][:, 0:256], T.Id[:], T.tri[:], 256), (B[4][:, 0:256], T.WC[:], T.ZB[:], 256), (B[4][:, 0:256], T.BO16[:], T.T16[:], 256)],
-           ["Id", "tri", "WC", "ZB", "BO16", "T16"], ["b4"], 4, True, True)
-        vscan(T.cS[:], T.R2[:], B[4][:, 0:256], 0.0, A.add, A.min, 256, ["R2", "b4"], ["cS"], (4,))
-        act(T.cR[:], B[4][:, 0:256], AF.Copy, 256, ["b4"], ["cR"], (4,))
-        gtt(T.eq[:], T.cS[:], T.bcU[:, 0:16], T.cR[:], A.is_equal, 256, ["cS", "cR", "bcU"], ["eq"])
-        gath(T.xw[:], T.XY[:], T.vU[:], 512, ["vU"] + allx + ally, ["xw"], "S")
-        mm([(B[5][:, 0:256], T.Id[:], z, 256), (B[5][:, 0:256], T.nId[:], T.xw[:, 256:512], 256)], ["Id", "nId", "xw"] + zR, ["b5"], 5, True, True)
+
+        def both(w, src, p):
+            return [m for w0, w1 in spans for m in ((B[4][:, 48 * w0:16 * w0 + 32 * w1], w, src[0:p, w0:w1, :], 32 * (w1 - w0)),
+                                                    (B[4][:, 16 * w0 + 32 * w1:48 * w1], w, src[0:p, w0:w1, 0:16], 16 * (w1 - w0)))]
+        mm("pA", [(B[4][:, 48 * w0:16 * w0 + 32 * w1], T.Id[:], T.tri[:, 0:32 * (w1 - w0)], 32 * (w1 - w0)) for w0, w1 in spans] + both(T.WC[0:16, :], T.ZB, 16),
+           ["Id", "tri", "WC", "ZB"], ["b4"], 4, True, False)
+        mm("pc", both(T.BO16[:], T.T16, 128), ["BO16", "T16"], ["b4"], 4, False, True)
+        for pi, (w0, w1) in enumerate(spans):
+            e0, n = 48 * w0, 32 * (w1 - w0)
+            vscan(T.cS[:, e0:e0 + n], T.R2[:, 0:n], B[4][:, e0:e0 + n], 0.0, A.add, A.min, n, ["R2", "b4"], ["cS%d" % pi], (4,))
+        act(T.cR[:], B[4][:, 0:384], AF.Copy, 384, ["b4"], ["cR"], (4,))
+        gtt(T.eq[:], T.cS[:], T.bcU[:, 48:72], T.cR[:], A.is_equal, 384, ["cS0", "cS1", "cSx", "cR", "bcU"], ["eq"])
+        if par["zd"] == "V":
+            mm("pd", [(B[1][:, 0:256], T.hId[:], z, 256), (B[1][:, 0:256], T.hId[:], T.XY[:, 0:4096:16], 256)],
+               ["hId"] + allx + zR, ["b1"], 1, True, True, zE, zA)
+            vts(T.ZW[:, 1:512:2], B[1][:, 0:256], M1, M1, A.add, A.subtract, 256, ["b1"], ["zd"], (1,))
+        gath(T.xw[:, 0:256], T.XY[:, 0:4096], T.vU[:, 0:16], 256, ["vU"] + allx, ["xk"], "VS")
+        for pi, cs in enumerate(par["parts"]):
+            a0, a1 = CH * min(cs), CH * (max(cs) + 1)
+            gath(T.xw[:, 256 + a0:256 + a1], T.XY[:, 4096 + 16 * a0:4096 + 16 * a1], T.vU[:, 16 + a0 // 16:16 + a1 // 16], a1 - a0,
+                 ["vU"] + ally[a0 // 16:a1 // 16], ["wk%d" % pi], "VS")
+            mm("ph%d" % pi, [(B[6][:, a0:a1], T.hId[:], T.xw[:, a0:a1], a1 - a0), (B[6][:, a0:a1], T.hId[:], T.xw[:, 256 + a0:256 + a1], a1 - a0)],
+               ["hId", "xk", "wk%d" % pi], ["b6"], 6, True, True)
+            vts(T.half[:, a0:a1], B[6][:, a0:a1], M1, M1, A.add, A.subtract, a1 - a0, ["b6"], ["half%d" % pi], (6,))
+        mm("pn", [(B[5][:, 0:256], T.Id[:], z, 256), (B[5][:, 0:256], T.nId[:], T.xw[:, 256:512], 256)], ["Id", "nId", "wk0", "wk1"] + zR, ["b5"], 5, True, True)
         act(T.ZW[:, 0:512:2], B[5][:, 0:256], AF.Abs, 256, ["b5"], ["zm"], (5,))
-        mm([(B[6][:, 0:256], T.Id[:], T.q25[:], 256), (B[6][:, 0:256], T.hId[:], T.xw[:, 0:256], 256), (B[6][:, 0:256], T.hId[:], T.xw[:, 256:512], 256)],
-           ["Id", "hId", "q25", "xw"], ["b6", "b6b"], 6, True, True)
-        mm([(B[3][:, 256:512], T.xId[:], T.tri[:], 256), (B[3][:, 256:512], T.Wu[:], T.ZW[:, 0:512:2], 256)], ["xId", "tri", "Wu", "zm"], ["b3u"], 3, True, True)
-        vscan(T.uS[:], T.R2[:], B[3][:, 256:512], 0.0, A.add, A.min, 256, ["R2", "b3u"], ["uS"], (3,))
-        vtt(T.amI[:], T.uS[:, 15:256:16], T.a5[:], A.add, 16, ["uS", "a5"], ["amI"])
+        if par["pu"] == "P":
+            mm("pu", [(B[3][:, 256:272], DG("Wu", j), T.ZW[:, 2 * j:512:32], 16) for j in range(16)], ["Wu", "zm"], ["b3u"], 3, True, True)
+            vtt(T.amI[:], B[3][:, 256:272], T.a5[:], A.add, 16, ["b3u", "a5"], ["amI"], (3,))
+        else:
+            mm("pe", [(B[3][:, 256:512], T.tId[:], T.tri[:], 256)], ["tId", "tri"], ["b3u"], 3, True, False)
+            mm("pu", [(B[3][:, 256:512], T.Wu[:, 0:128], T.ZW[:, 0:512:2], 256)], ["Wu", "zm"], ["b3u"], 3, False, True)
+            vscan(T.uS[:], T.R2[:], B[3][:, 256:512], 0.0, A.add, A.min, 256, ["R2", "b3u"], ["uS"], (3,))
+            vtt(T.amI[:], T.uS[:, 15:256:16], T.a5[:], A.add, 16, ["uS", "a5"], ["amI"])
         vts(T.amJ[:], T.amI[:], 1023, None, A.bitwise_and, None, 16, ["amI"], ["amJ"])
         vtt(T.da[:], aF, T.amJ[:], A.subtract, 16, ["aU", "amJ"], ["da"])
-        vts(T.half[:], B[6][:, 0:256], M1, M1, A.add, A.subtract, 256, ["b6"], ["half"], (6,))
-        def new_a():
-            vscan(T.nS[:], T.R2[:], B[7][:, 0:256], 0.0, A.add, A.min, 256, ["R2", "b7"], ["nS"], (7,))
-            vts(T.dl[:], T.nS[:, 15:256:16], 1.0, None, A.is_gt, None, 16, ["nS"], ["dl"])
-            vtt(T.t2[:], T.dl[:], T.da[:], A.mult, 16, ["dl", "da"], ["t2"])
-            aS = T.aS[:, 16 * t:16 * t + 16]
-            vtt(aS, T.t2[:], T.amJ[:], A.add, 16, ["t2", "amJ"], ["aS%d" % t])
-            if not last:
-                snd["a", t] = send([(1, aS, T.aF[:, 16 * t + 16:16 * t + 32], "ra%d" % (t + 1))], ["aS%d" % t], par["lat"])
-            else:
-                dma("Y", T.ya[:], aS, ["aS%d" % t], [], "out", 2500)
 
-        miss = ["mis%d" % pi for pi in range(len(par["parts"]))]
+        own = PKW * t
+        blocks = []
+
+        def number(a0, a1, pi, R):
+            n = a1 - a0
+            mm("pq%d" % pi, [(B[1][:, 256 + a0:256 + a1], T.BOs[:], T.mis[:, a0:a1], n)], ["BOs"] + R, ["b1q"], 1, True, True)
+            act(T.dvS[:, a0:a1], B[1][:, 256 + a0:256 + a1], AF.Sign, n, ["b1q", "c14"], ["dvS%d" % pi], (1,), bias=col[:, 14:15])
+            vscan(T.pref[:, a0:a1], T.ones[:, a0:a1], T.dvS[:, a0:a1], T.pref[:, a0 - 1:a0] if pi else 0.0, A.add, A.add, n,
+                  ["ones", "dvS%d" % pi] + (["pref%d" % (pi - 1)] if pi else []), ["pref%d" % pi], half=True)
+            for j in range(4):
+                act(T.junk[:, 256 * j + a0:256 * j + a1], T.pref[:, a0:a1], AF.Sign, n, ["pref%d" % pi, "jC1"], ["junk%d_%d" % (pi, j), "acc%d_%d" % (pi, j)],
+                    bias=T.jC[:, 4 + j:5 + j], accum=T.acc[:, 4 * pi + j:4 * pi + j + 1])
+            if pi:
+                prev, pR = (T.acc[:, 0:4], ["acc0_%d" % j for j in range(4)]) if pi == 1 else (T.accS[:, 4 * pi - 4:4 * pi], ["sum%d" % (pi - 1)])
+                vtt(T.accS[:, 4 * pi:4 * pi + 4], T.acc[:, 4 * pi:4 * pi + 4], prev, A.add, 4, ["acc%d_%d" % (pi, j) for j in range(4)] + pR, ["sum%d" % pi])
+
+        NP = len(par["parts"])
+        miss = ["mis%d" % pi for pi in range(NP)]
+        nSs = ["nS%d" % pi for pi in range(NP)]
         for pi, cs in enumerate(par["parts"]):
             bk, off, key = (0, 0, "b0") if pi % 2 == 0 else (2, 256, "b2b")
             a0, a1 = CH * min(cs), CH * (max(cs) + 1)
             n, nl, s = a1 - a0, (a1 - a0) // 16, "_%d" % pi
+            fresh = [True]
             for c in cs:
                 lo, hi = 16 * CH * c, 16 * CH * (c + 1)
                 for j in range(NSUB):
                     l0, l1 = CH * c + DCH * j, CH * c + DCH * (j + 1)
                     gtt(T.DF[:, 16 * l0:16 * l1], T.XY[:, 4096 + 16 * l0:4096 + 16 * l1], T.wo[:, l0:l1], T.XY[:, 16 * l0:16 * l1], A.subtract, 16 * DCH,
-                        ["x%d" % c, "y%d" % c, "wo"], ["df%d_%d" % (c, j)])
+                        allx[l0 // 16:l1 // 16] + ally[l0 // 16:l1 // 16] + ["wo"], ["df%d_%d" % (c, j)])
                 dfs = ["df%d_%d" % (c, j) for j in range(NSUB)]
-                out = B[bk][:, off + CH * c:off + CH * (c + 1)]
-                act(T.AB[:, lo:hi], T.DF[:, lo:hi], AF.Abs, 16 * CH, dfs, ["ab%d" % c], scale=0.5)
-                mm([(out, DG("U64", k), T.AB[:, lo + k:hi:16], CH) for k in range(16)], ["U64", "ab%d" % c], [key], bk, c == cs[0], c == cs[-1])
-            mm([(B[7][:, a0:a1], T.Id[:], T.cmk[:, a0:a1], n)], ["Id", "cmk"], ["b7"], 7, True, False, nm=s)
-            act(T.mis[:, a0:a1], B[bk][:, off + a0:off + a1], AF.Sign, n, [key, "nth"], [miss[pi]], (bk,), bias=T.nth[:, 0:1], scale=1.0 / 32)
-            mm([(B[7][:, a0:a1], T.BOs[:], T.mis[:, a0:a1], n)], ["BOs", miss[pi]], ["b7"], 7, False, True)
-            if cs is par["parts"][-1]:
-                new_a()
-            vtt(T.cm[:, a0:a1], T.eq[:, a0:a1], B[7][:, a0:a1], A.is_gt, n, ["eq", "b7"], ["cm" + s], (7,))
-            vscan(T.bS[:, a0:a1], T.R3[:, a0:a1], T.cm[:, a0:a1], 0.0, A.mult, A.add, n, ["R3", "cm" + s], ["bS" + s])
+                out = cols(bk, off + CH * c, off + CH * (c + 1))
+                if c in par["rv"]:
+                    for h in range(2):
+                        mm("dl%d_%d" % (c, h), [(out, DG("Un32", k), T.DF[:, lo + k:hi:16], CH) for k in range(8 * h, 8 * h + 8)], ["Un32"] + dfs, [key], bk,
+                           fresh[0], False)
+                        fresh[0] = False
+                    vts(T.AB[:, lo:hi], T.DF[:, lo:hi], 0.0, None, A.max, None, 16 * CH, dfs, ["ab%d" % c], half=True)
+                else:
+                    act(T.AB[:, lo:hi], T.DF[:, lo:hi], AF.Abs, 16 * CH, dfs, ["ab%d" % c], scale=0.5)
+                for gr in par["dg"]:
+                    if gr[-1] == c:
+                        l0, l1 = CH * gr[0], CH * (c + 1)
+                        for h in range(2):
+                            mm("da%d_%d" % (c, h), [(cols(bk, off + l0, off + l1), DG("U64", k), T.AB[:, 16 * l0 + k:16 * l1:16], l1 - l0) for k in range(8 * h, 8 * h + 8)],
+                               ["U64"] + ["ab%d" % j for j in gr], [key], bk, fresh[0], c == cs[-1] and h == 1)
+                            fresh[0] = False
+            nb, nk = (7, "b7") if pi % 2 == 0 else (0, "b0b")
+            w0, w1 = a0 // 32, a1 // 32
+            s0, n3, e0, e1 = 256 * pi, 48 * (w1 - w0), 48 * w0, 48 * w1
+            mm("n0" + s, [(B[nb][:, s0:s0 + n3], T.Id[:], T.cmk[:, e0:e1], n3)], ["Id", "cmk" + s, "cmj" + s], [nk], nb, True, False)
+            act(T.mis[:, a0:a1], cols(bk, off + a0, off + a1), AF.Sign, n, [key, "nth"], [miss[pi]], (bk,), bias=T.nth[:, 0:1], scale=1.0 / 32)
+            mm("n1" + s, [(B[nb][:, s0:s0 + n], T.BOs[:], T.mis[:, a0:a1], n)] +
+               [(B[nb][:, s0 + n + 16 * j:s0 + n + 16 * j + 16], T.BOs[:], T.mis[:, a0 + 32 * j:a0 + 32 * j + 16], 16) for j in range(w1 - w0)],
+               ["BOs", miss[pi]], [nk], nb, False, True)
+            vscan(T.nS[:, a0:a1], T.R2[:, a0:a1], B[nb][:, s0:s0 + n], 0.0, A.add, A.min, n, ["R2", nk], [nSs[pi]], (nb,))
+            if pi == NP - 1:
+                vts(T.dl[:], T.nS[:, 15:256:16], 1.0, None, A.is_gt, None, 16, nSs, ["dl"])
+                vtt(T.t2[:], T.dl[:], T.da[:], A.mult, 16, ["dl", "da"], ["t2"])
+                aS = T.aS[:, 16 * t:16 * t + 16]
+                vtt(aS, T.t2[:], T.amJ[:], A.add, 16, ["t2", "amJ"], ["aS%d" % t], nm="aS")
+                if not last:
+                    snd["a", t] = send("toa", [(1, aS, T.aF[:, 16 * t + 16:16 * t + 32], "ra%d" % (t + 1))], ["aS%d" % t], par["lat"])
+                else:
+                    dma("Y", T.ya[:], aS, ["aS%d" % t], [], "out", 2500, "oa")
+            vtt(T.cm[:, e0:e1], T.eq[:, e0:e1], B[nb][:, s0:s0 + n3], A.is_gt, n3, ["eq", nk], ["cm" + s], (nb,))
+            vscan(T.bS[:, e0:e1], T.R3[:, 0:n3], T.cm[:, e0:e1], 0.0, A.mult, A.add, n3, ["R3", "cm" + s], ["bS" + s])
             q0, q1 = a0 // 16, a1 // 16
-            vts(T.f1[:, q0:q1], T.bS[:, a0 + 15:a1:16], T.pw[:, 15:16], col[:, 12:13], A.not_equal, A.mult, nl, ["bS" + s, "pw", "c12"], ["f1" + s])
-            vtt(T.f2[:, q0:q1], T.f1[:, q0:q1], T.cS[:, a0 + 15:a1:16], A.max, nl, ["f1" + s, "cS"], ["f2" + s])
-            vcp(T.offU[:, 2 * q0:2 * q1:2], T.f2[:, q0:q1], nl, ["f2" + s], ["offU" + s])
-            for lh in range(q1 - 1, q0 - 1, -1):
-                scat(T.X[:], T.offU[:, 2 * lh:2 * lh + 1], T.half[:, 16 * lh:16 * lh + 16], 16, ["offU" + s, "half"], Xr)
-        mm([(B[0][:, 256:512], T.BOs[:], T.mis[:, 0:256], 256)], ["BOs"] + miss, ["b0b"], 0, True, True)
-        act(T.dvS[:], B[0][:, 256:512], AF.Sign, 256, ["b0b", "c14"], ["dvS"], (0,), bias=col[:, 14:15])
-        own = PKW * t
-        vscan(T.pref[:], T.ones[:], T.dvS[:], 0.0, A.add, A.add, 256, ["ones", "dvS"], ["pref"], half=True)
-        act(T.pkS[:, own + 136:own + 144], T.pref[:, 248:256], AF.Copy, 8, ["pref"], ["pkA%d" % t])
+            vts(T.f1[:, q0:q1:2], T.bS[:, e0 + 15:e0 + n:32], T.pw[:, 15:16], col[:, 12:13], A.not_equal, A.mult, nl, ["bS" + s, "pw", "c12"], ["f0" + s])
+            vts(T.f3[:, w0:w1], T.bS[:, e0 + 31:e0 + n:32], T.pw[:, 15:16], col[:, 13:14], A.not_equal, A.mult, nl, ["bS" + s, "pw", "c13"], ["f3" + s])
+            vts(T.f3[:, 8 + w0:8 + w1], T.bS[:, e0 + n + 15:e1:16], 0.0, col[:, 13:14], A.is_gt, A.mult, nl, ["bS" + s, "c13"], ["f4" + s])
+            vtt(T.f1[:, q0 + 1:q1:2], T.f3[:, w0:w1], T.f3[:, 8 + w0:8 + w1], A.max, nl, ["f3" + s, "f4" + s], ["f1" + s])
+            vtt(T.f2[:, q0:q1], T.f1[:, q0:q1], T.cS[:, e0 + 15:e0 + n:16], A.max, nl, ["f0" + s, "f1" + s, "cS%d" % pi], ["f2" + s])
+            vcp(T.offU[:, q0:q1], T.f2[:, q0:q1], nl, ["f2" + s], ["offU" + s])
+            blocks += [(w, s) for w in range(w0, w1)]
+            if par["split"]:
+                number(a0, a1, pi, [miss[pi]])
+            if not par["asc"] or pi == NP - 1:
+                for lh, s in sorted(blocks, reverse=True):
+                    scat(T.X[:], T.offU[:, 2 * lh:2 * lh + 2], T.half[:, 32 * lh:32 * lh + 32], 32, ["offU" + s, "half" + s[1:]], Xr, nm="sx%d" % lh)
+                blocks = []
+        if not par["split"]:
+            number(0, 256, 0, miss)
+        if par["zd"] == "S":
+            mm("pd", [(B[2][:, 0:256], T.hId[:], z, 256), (B[2][:, 0:256], T.hId[:], T.XY[:, 0:4096:16], 256)],
+               ["hId"] + allx + zR, ["b2"], 2, True, True, zE, zA)
+            act(T.kT[:], B[2][:, 0:256], AF.Copy, 256, ["b2"], ["kT"], (2,), bias=M1, nm="zc")
+            act(T.ZW[:, 1:512:2], T.kT[:], AF.Copy, 256, ["kT"], ["zd"], bias=-M1)
+        NJ = NP if par["split"] else 1
+        prl = "pref%d" % (NJ - 1)
+        act(T.pkS[:, own + 136:own + 144], T.pref[:, 248:256], AF.Copy, 8, [prl], ["pkA%d" % t], nm="pkA")
         src = T.pkS[:, own + 136:own + 144]
         if not last:
-            snd["A", t] = send([(2, src, T.pkA[:, 32 * t:32 * t + 8], "rA%d" % t)], ["pkA%d" % t], par["lat"])
+            snd["A", t] = send("toA", [(2, src, T.pkA[:, 32 * t:32 * t + 8], "rA%d" % t)], ["pkA%d" % t], par["lat"])
         else:
-            snd["A", t] = send([(1, src, T.pkA[:, 32 * t:32 * t + 8], "rA%d" % t), (3, src, T.pkA[:, 32 * t + 8:32 * t + 16], "rO%d" % t)], ["pkA%d" % t], par["lat"] + 600)
-        for j in range(4):
-            act(T.junk[:, 256 * j:256 * j + 256], T.pref[:], AF.Sign, 256, ["pref", "jC1"], ["junk%d" % j, "acc%d" % j], bias=T.jC[:, 4 + j:5 + j], accum=T.acc[:, j:j + 1])
-        accs = ["acc%d" % j for j in range(4)]
-        vts(T.posU[:], T.acc[:], -0.5, 128.0, A.mult, A.add, 4, accs, ["posU"])
-        act(T.pkS[:, own + 128:own + 132], T.acc[:], AF.Copy, 4, accs, ["pkp%d" % t], bias=128.0, scale=-0.5)
-        gath(T.pkS[:, own + 64:own + 128], T.KB[:, ko:ko + 320], T.posU[:], 64, ["posU", Kt, "Kd%d" % t], ["pkK%d" % t], "S")
-        gath(T.pkS[:, own + 144:own + 208], T.KB[:, ko + 320:ko + 640], T.posU[:], 64, ["posU", Bt, "Be%d" % t], ["pkB%d" % t], "S")
+            snd["A", t] = send("toA", [(1, src, T.pkA[:, 32 * t:32 * t + 8], "rA%d" % t), (3, src, T.pkA[:, 32 * t + 8:32 * t + 16], "rO%d" % t)], ["pkA%d" % t], par["lat"] + 600)
+        accs = ["acc%d_%d" % (NJ - 1, j) for j in range(4)] if NJ == 1 else ["sum%d" % (NJ - 1)]
+        acc = T.acc[:, 0:4] if NJ == 1 else T.accS[:, 4 * NJ - 4:4 * NJ]
+        vts(T.posU[:], acc, -0.5, 128.0, A.mult, A.add, 4, accs, ["posU"])
+        act(T.pkS[:, own + 128:own + 132], acc, AF.Copy, 4, accs, ["pkp%d" % t], bias=128.0, scale=-0.5, nm="pkp")
+        if not last:
+            gath(T.pkS[:, own + 64:own + 128], T.KB[:, ko:ko + 320], T.posU[:], 64, ["posU", Kt, "Kd%d" % t], ["pkK%d" % t], "VS", nm="pkK")
+        gath(T.pkS[:, own + 144:own + 208], T.KB[:, ko + 320:ko + 640], T.posU[:], 64, ["posU", Bt, "Be%d" % t], ["pkB%d" % t], "VS", nm="pkB")
         act(T.pkS[:, own + 208:own + 272], T.KB[:, ko:ko + 320].indirect(T.posU[:]), AF.Identity, 64, ["posU", Kt, "Kd%d" % t, "c15"], ["pkL%d" % t],
-            bias=col[:, 15:16], gather=True)
-        act(T.pkS[:, own:own + 64], T.mis[:].indirect(T.posU[:]), AF.Copy, 64, ["posU", "misd"] + miss, ["pkM%d" % t], bias=0.5, scale=0.5, gather=True)
+            bias=col[:, 15:16], gather=True, nm="pkL")
+        if last:
+            gath(T.pkS[:, own + 64:own + 128], T.KB[:, ko:ko + 320], T.posU[:], 64, ["posU", Kt, "Kd%d" % t], ["pkK%d" % t], "VS", nm="pkK")
+        act(T.pkS[:, own:own + 64], T.mis[:].indirect(T.posU[:]), AF.Copy, 64, ["posU", "misd"] + miss, ["pkM%d" % t], bias=0.5, scale=0.5, gather=True, nm="pkM")
         sO, sM = T.pkS[:, own:own + 144], T.pkS[:, own + 128:own + 272]
         pkR = ["pk%s%d" % (a, t) for a in ("BLpA" if last else "KMBLpA")]
         if not last:
-            snd["P", t] = send([(1, sO, T.pkO[:, own:own + 144], "rO%d" % t), (3, sM, T.pkM[:, own + 128:own + 272], "rM%d" % t)], pkR, par["lat"] + 800)
+            snd["P", t] = send("toP", [(1, sO, T.pkO[:, own:own + 144], "rO%d" % t), (3, sM, T.pkM[:, own + 128:own + 272], "rM%d" % t)], pkR, par["lat"] + 800)
         else:
-            snd["P", t] = send([(2, sM, T.pkM[:, own + 128:own + 272], "rM%d" % t)], ["pkK"] + pkR, par["lat"] + 300)
+            snd["P", t] = send("toP", [(2, sM, T.pkM[:, own + 128:own + 272], "rM%d" % t)], pkR, par["lat"] + 300)
         vtt(T.s2[:], T.s1[:], T.dl[:], A.add, 16, ["s1", "dl"], ["s2"])
         vcp(T.slU[:], T.s2[:], 16, ["s2"], ["slU"])
         zS = T.zS[:, 256 * t:256 * t + 256]
-        gath(zS, T.ZW[:], T.slU[:], 256, ["slU", "zm", "zd"], ["zS%d" % t], "S")
+        gath(zS, T.ZW[:], T.slU[:], 256, ["slU", "zm", "zd"], ["zS%d" % t], "VS", nm="zS")
         if not last:
-            snd["z", t] = send([(1, zS, T.zb[:, 256 * t + 256:256 * t + 512], "rz%d" % (t + 1))], ["zS%d" % t], par["lat"] + 600)
+            snd["z", t] = send("toz", [(1, zS, T.zb[:, 256 * t + 256:256 * t + 512], "rz%d" % (t + 1))], ["zS%d" % t], par["lat"] + 600)
         else:
-            dma("Y", T.yz[:], zS, ["zS%d" % t], [], "out", 2500)
+            dma("Y", T.yz[:], zS, ["zS%d" % t], [], "out", 2500, "oz")
         if not last:
-            vts(T.AI[:, 0:1], T.pref[:, 255:256], 0.5, None, A.mult, None, 1, ["pref"], ["AI"])
+            vts(T.AI[:, 0:1], T.pref[:, 255:256], 0.5, None, A.mult, None, 1, [prl], ["AI"])
             vts(T.AJ[:, 0:1], T.AI[:, 0:1], 31, None, A.bitwise_and, None, 1, ["AI"], ["AJ"])
             vtt(T.nth[:, 0:1], T.thF[:, 0:1], T.AJ[:, 0:1], A.subtract, 1, ["thF", "AJ"], ["nth"])
         else:
-            dma("Y", T.yx[:], T.X[:, 0:4096], Xr, [], "out", 7000)
+            dma("Y", T.yx[:], T.X[:, 0:4096], Xr, [], "out", 7500, "ox")
+            cur[0] = ST
             patch(t, t, True)
-            act(T.bF[:], B[6][:, 64:80], AF.Copy, 16, ["b6b"], ["bF"], (6,), scale=1.0 / 64)
-            dma("S", T.yk[:], K, [Kt], [], "out", 2500)
-            dma("S", T.yb[:], T.bF[:], ["bF"], [], "out", 2500)
+            dma("S", T.yk[:], K, [Kt], [], "out", 2500, "ok")
+            dma("S", T.yb[:], T.bF[:], ["bF"], [], "out", 2500, "ob")
     return ops, nsent[0]
 
 
-def schedule(ops, par):
-    n = len(ops)
+def first_calls(ops, par):
+    order, eng = greedy(ops, par)
+    later = set(x[1:] for q in par["queues"].values() for x in q if x[0] == "+")
+    return {e: [i for i in order if eng[i] == e and (ops[i]["t"] < 0 or ops[i]["t"] == 0 and ops[i]["nm"] not in later)] for e in "VSPGY"}, eng
+
+
+def greedy(ops, par):
+    n, hop = len(ops), par["hop"]
+    eng = [list(o["alts"])[-1] for o in ops]
+    cost = [o["alts"][e][0] for o, e in zip(ops, eng)]
     succ = [[] for _ in range(n)]
     for i, o in enumerate(ops):
         for d in o["deps"]:
             succ[d].append(i)
+    if "queues" in par:
+        place = {nm.lstrip("+"): 900.0 * j / len(q) + (1000 if nm[0] == "+" else 0) for q in par["queues"].values() for j, nm in enumerate(q)}
+    else:
+        place = {nm.lstrip("+"): j + (1000 if nm[0] == "+" else 0) for j, nm in enumerate(par["order"])}
     pr = [0.0] * n
     for i in range(n - 1, -1, -1):
-        c = min(a[0] for a in ops[i]["alts"].values())
-        pr[i] = c + ops[i]["lat"] + max([pr[s] + par["hop"] for s in succ[i]] + [0.0])
-    kind_of = [o["nm"].rstrip("0123456789") if o["nm"][:2] in ("K0", "K1", "K2", "K3", "K4", "Bd", "aS", "zS", "pk", "to") else o["nm"] for o in ops]
-    rank_of = {k: j for j, k in enumerate(par["tpl"].split())}
-    rank_last = {k: j for j, k in enumerate(par["tplL"].split())}
-    for i in range(n - 1, -1, -1):
-        if ops[i]["t"] >= 0 and kind_of[i] in rank_of:
-            pr[i] = -(1000.0 * ops[i]["t"] + (rank_last if ops[i]["t"] == ST - 1 else rank_of)[kind_of[i]])
+        o = ops[i]
+        if o["t"] == 0 and o["nm"] in par["first"]:
+            pr[i] = 5000.0 - place[o["nm"]]
+        elif o["t"] >= 0 and o["nm"] in place:
+            pr[i] = -1000.0 * o["t"] - place[o["nm"]]
+        elif o["nm"] == "dma":
+            pr[i] = 1e9 - i
         else:
-            pr[i] = max([pr[s] for s in succ[i]] + [-1e9]) + 0.001
+            pr[i] = max([pr[s] + (2000.0 if ops[s]["t"] >= 0 and o["t"] < 0 else 0) for s in succ[i]] + [-1e9]) + 1e-7 * (cost[i] + o["lat"] + hop)
     left = [len(o["deps"]) for o in ops]
-    cand = [i for i in range(n) if left[i] == 0]
-    free = {}
-    eng, end, start = [None] * n, [0.0] * n, [0.0] * n
+    rd, en = [0.0] * n, [0.0] * n
+    cand = {e: [i for i in range(n) if left[i] == 0 and eng[i] == e] for e in "VSPGY"}
+    free = dict.fromkeys(cand, 0.0)
     order = []
-    rdy = {}
-
-    def ready(i, e):
-        r = 0.0
-        for d, kind in ops[i]["deps"].items():
-            if eng[d] == e and ops[d]["lat"] == 0:
-                w = par["self"] if (kind != "bank" and e != "P") else 0.0
-            else:
-                w = par["hop"]
-            r = max(r, end[d] + w)
-        return r
-
-    while cand:
-        opts = []
-        for i in cand:
-            if i not in rdy:
-                es = list(ops[i]["alts"])
-                if len(es) > 1:
-                    es = par["eng"].get(kind_of[i] + "@%d" % ops[i]["t"], par["eng"].get(kind_of[i], "VS"))
-                rdy[i] = [(e, ready(i, e)) for e in es]
-            for e, r in rdy[i]:
-                opts.append((max(r, free[e][-1][1] if free.get(e) else 0.0), e, i))
-        s0, e0, _ = min(opts)
-        i = max((b[2] for b in opts if (b[1] == e0 or par["any"]) and b[0] <= s0 + par["slack"]), key=lambda c: (pr[c], -c))
-        alts = ops[i]["alts"]
-        es = [e for e, r in rdy[i]]
-        best = None
-        for e in es:
-            s, c = ready(i, e), alts[e][0]
-            busy = free.setdefault(e, [])
-            lo, hi = 0, len(busy)
-            while lo < hi:
-                mid = (lo + hi) // 2
-                if busy[mid][1] <= s:
-                    lo = mid + 1
-                else:
-                    hi = mid
-            while lo < len(busy) and busy[lo][0] < s + c:
-                s = max(s, busy[lo][1])
-                lo += 1
-            if best is None or s + c < best[0]:
-                best = (s + c, s, e, lo)
-        fin, s, e, lo = best
-        free[e].insert(lo, (s, fin))
-        eng[i], start[i] = e, s
-        end[i] = fin + ops[i]["lat"]
-        order.append(i)
-        cand.remove(i)
-        for j in succ[i]:
+    while len(order) < n:
+        now, e = min((max(free[e], min(rd[i] for i in q)), j, e) for j, (e, q) in enumerate(cand.items()) if q)[::2]
+        b = max((i for i in cand[e] if rd[i] <= now + par["near"]), key=lambda i: pr[i])
+        if rd[b] > now:
+            short = [i for i in cand[e] if rd[i] <= now and cost[i] <= rd[b] - now + par["slack"]]
+            if short:
+                b = max(short, key=lambda i: pr[i])
+        free[e] = max(now, rd[b]) + cost[b]
+        en[b] = free[e] + ops[b]["lat"]
+        cand[e].remove(b)
+        order.append(b)
+        for j in succ[b]:
             left[j] -= 1
             if left[j] == 0:
-                cand.append(j)
-    order.sort(key=lambda c: (start[c], c))
-    return order, eng, start, end
+                rd[j] = max(en[d] + (0 if eng[d] == eng[j] and ops[d]["lat"] == 0 and (k == "bank" or eng[j] == "P") else hop) for d, k in ops[j]["deps"].items())
+                cand[eng[j]].append(j)
+    return order, eng
 
 
-def merge(ops, table):
-    dig = "0123456789abcdefghijklmnopqrstuvwxyz"
-    seq = {e: [dig.index(s[j]) * 36 + dig.index(s[j + 1]) for j in range(0, len(s), 2)] for e, s in table.items()}
-    eng = [None] * len(ops)
-    pos = {e: 0 for e in seq}
-    order = []
+def schedule(ops, par):
+    if "queues" not in par:
+        return greedy(ops, par)
+    seq, eng = first_calls(ops, par)
+    at = {}
+    for i, o in enumerate(ops):
+        at.setdefault((o["nm"], o["t"], eng[i]), []).append(i)
+    for e in seq:
+        for t in range(1, ST + 1):
+            for x in par["queues"][e]:
+                seq[e] += at.get((x[1:], t - 1, e) if x[0] == "+" else (x, t, e), [])
+    done, order, pos = set(), [], dict.fromkeys(seq, 0)
     while len(order) < len(ops):
         before = len(order)
         for e, s in seq.items():
-            while pos[e] < len(s) and all(eng[d] is not None for d in ops[s[pos[e]]]["deps"]):
-                eng[s[pos[e]]] = e
+            while pos[e] < len(s) and all(d in done for d in ops[s[pos[e]]]["deps"]):
+                done.add(s[pos[e]])
                 order.append(s[pos[e]])
                 pos[e] += 1
         assert len(order) > before
     return order, eng
 
 
+def heft(ops, par, some):
+    n, hop = len(ops), par["hop"]
+    some = set(some)
+    succ = [[] for _ in range(n)]
+    for i, o in enumerate(ops):
+        for d in o["deps"]:
+            succ[d].append(i)
+    pr = [0.0] * n
+    place = {}
+    for j, nm in enumerate(par.get("order", [])):
+        place[nm.lstrip("+")] = j + (1000 if nm[0] == "+" else 0)
+    for i in range(n - 1, -1, -1):
+        o = ops[i]
+        if o["t"] >= 0 and o["nm"] in place:
+            pr[i] = -1000.0 * o["t"] - place[o["nm"]]
+        else:
+            pr[i] = max([pr[s] for s in succ[i]] + [-1e9 if place else 0]) + (1e-7 if place else 1) * (min(a[0] for a in o["alts"].values()) + o["lat"] + hop)
+        if o["nm"] == "dma":
+            pr[i] = 1e9 - i
+    succ = [[j for j in s if j in some] for s in succ]
+    eng, st, en = [None] * n, [0] * n, [0] * n
+    busy = {}
+    left = [len(o["deps"]) for o in ops]
+    ready = [i for i in some if left[i] == 0]
+    while ready:
+        i = max(ready, key=lambda j: (pr[j], -j))
+        ready.remove(i)
+        for j in succ[i]:
+            left[j] -= 1
+            if left[j] == 0:
+                ready.append(j)
+        best = None
+        for e, (c, f) in ops[i]["alts"].items():
+            s = 0
+            for d, k in ops[i]["deps"].items():
+                s = max(s, en[d] + (0 if (eng[d] == e and ops[d]["lat"] == 0 and (k == "bank" or e == "P")) else hop))
+            b = busy.setdefault(e, [])
+            lo = len(b)
+            while lo > 0 and b[lo - 1][1] > s:
+                lo -= 1
+            while lo < len(b) and b[lo][0] < s + c:
+                s = max(s, b[lo][1])
+                lo += 1
+            if best is None or s + c < best[0]:
+                best = (s + c, s, e, lo)
+        fin, s, e, lo = best
+        busy[e].insert(lo, (s, fin))
+        eng[i], st[i], en[i] = e, s, fin + ops[i]["lat"]
+    return sorted(some, key=lambda c: (st[c], c)), eng
+
+
 def rank_program(g, core, T, topo):
     if T.rank_of(core) is None:
         return
     par = PAR
-    g.vector.memset(T.col[:, 14:15], 0.1875).then_inc(T.sem.sV, 1)
     ops, nsent = build(g, core, T, topo, par)
-    order, eng = merge(ops, ORDER) if ORDER else schedule(ops, par)[:2]
+    order, eng = schedule(ops, par)
     Q = {"V": g.vector, "S": g.scalar, "P": g.tensor, "G": g, "Y": g.sync}
-    cnt = {"sV": 1, "out": 0}
+    cnt = {"out": 0}
     mark = {}
     seen = {e: {} for e in Q}
     allw = {}
@@ -655,8 +805,6 @@ def rank_program(g, core, T, topo):
                 continue
             need.add((d, i))
     raises = set(d for d, i in need)
-    g.scalar.wait_ge(T.sem.sV, 1)
-    seen["S"]["sV"] = 1
     for i in order:
         o, e = ops[i], eng[i]
         waits = {}

@@ -1,5 +1,5 @@
 from concourse.bass import DstId, RemoteDMATransfer
-from concourse.mybir import dt, AluOpType, AxisListType, ActivationFunctionType
+from concourse.mybir import AluOpType, ActivationFunctionType
 
 ST = 5
 NR = 4
@@ -9,72 +9,67 @@ BF, F32, I32, U16, F16 = "bfloat16", "float32", "int32", "uint16", "float16"
 
 SCRATCH = {}
 for _n, _c, _d in [
-    ("X", 4112, BF), ("P", 1024, I32), ("XY", 8192, BF), ("DF", 4096, BF), ("AB", 4096, BF), ("MX", 4096, BF),
+    ("X", 4128, BF), ("P", 1024 * ST, I32), ("XY", 8192, BF), ("DF", 4096, BF), ("AB", 4096, BF), ("MX", 4096, BF),
     ("KB", KBW * ST, BF), ("aU", 16, U16), ("aS", 16 * ST, F32), ("zb", 256 * ST, BF), ("zS", 256 * ST, BF),
     ("pkS", PKW * ST, BF), ("pkO", PKW * ST, BF), ("pkM", PKW * ST, BF), ("pkA", 32 * ST, BF),
     ("avI", 16, I32), ("bvI", 16, I32), ("kcI", 256, I32), ("thI", 4, I32),
     ("ra", 256, U16), ("rb", 256, U16), ("rb16", 256, F16), ("wo", 256, U16), ("bU", 16, U16), ("bF", 16, F32),
-    ("kT", 256, F32), ("kS", 256, F32), ("r16", 16, F32), ("low", 16, F32), ("ZT", 256, BF), ("ZB", 256, BF),
-    ("vF", 32, F32), ("vU", 32, U16), ("xw", 512, BF), ("T16", 256, F16), ("cS", 256, F32), ("cR", 256, F32),
-    ("eq", 256, BF), ("ZW", 512, BF), ("half", 256, BF), ("uS", 256, F32), ("a5", 16, F32), ("aF", 16 * ST, F32),
+    ("kT", 256, F32), ("kS", 256, F32), ("r16", 16, F32), ("low", 16, F32), ("ZT", 48, BF), ("SK", 32, BF),
+    ("vF", 32, F32), ("vU", 32, U16), ("xw", 512, BF), ("cS", 384, F32), ("cR", 384, F32),
+    ("eq", 384, BF), ("ZW", 512, BF), ("half", 256, BF), ("a5", 16, F32), ("aF", 16 * ST, F32),
     ("amI", 16, I32), ("amJ", 16, I32), ("da", 16, F32), ("mis", 272, BF), ("dvS", 256, BF), ("pref", 256, BF),
-    ("cm", 256, BF), ("bS", 256, F32), ("nS", 256, F32), ("f1", 16, F32), ("f2", 16, F32), ("offU", 32, U16),
+    ("cm", 384, BF), ("bS", 384, F32), ("nS", 256, F32), ("f1", 16, F32), ("f2", 16, F32), ("f3", 16, F32), ("offU", 16, U16),
     ("dl", 16, F32), ("t2", 16, F32), ("s1", 16, F32), ("s2", 16, F32), ("slU", 16, U16),
-    ("acc", 16, F32), ("accS", 16, F32), ("posU", 4, U16), ("junk", 1024, BF), ("AI", 4, I32), ("AJ", 4, I32), ("nth", 4, F32), ("thF", 4, F32),
+    ("acc", 4, F32), ("posU", 4, U16), ("junk", 1024, BF), ("AI", 4, I32), ("nth", 4, F32), ("thF", 4, F32),
     ("n1", 4, F32), ("n2", 4, F32), ("g1", 4, F32), ("g2", 4, F32), ("g3", 4, F32), ("spU", 4, U16),
-    ("CL", 1024, BF), ("k1", 64, BF),
-    ("ZC", 128, BF), ("hJ", 32, I32), ("hl", 32, BF), ("hm", 512, BF),
-    ("io", 4, I32), ("ia", 4, I32), ("col", 16, F32), ("ones", 256, BF), ("Id", 128, BF), ("nId", 128, BF), ("hId", 128, F16),
-    ("sId", 128, BF), ("xId", 128, BF), ("mId", 128, BF), ("I16", 128, F16), ("BO", 128, BF), ("BO16", 128, F16), ("BOs", 128, BF),
-    ("Wu", 144, BF), ("WT", 128, BF), ("WC", 128, BF), ("U64", 144, BF), ("Un32", 144, BF), ("Vs", 640, BF),
-    ("SEL", 2048, BF), ("tri", 256, BF), ("cmk", 256, BF), ("R1", 256, BF), ("R2", 256, BF), ("R3", 256, BF), ("dg", 256, BF),
-    ("tId", 128, BF), ("wc", 256, BF), ("tI", 256, F32), ("tJ", 160, F32),
-    ("vC", 32, F16), ("lC", 16, F32), ("bcF", 48, F32), ("bcU", 48, U16), ("jC", 12, F32), ("pw", 16, F32),
+    ("CL", 1024, BF), ("k1", 64, BF), ("hJ", 32, I32), ("hl", 32, BF), ("hm", 512, BF),
+    ("io", 4, I32), ("ia", 16, I32), ("col", 20, F32), ("ones", 256, BF), ("Id", 128, BF), ("Id2", 256, BF), ("nId", 128, BF),
+    ("hId", 128, F16), ("sId", 128, BF), ("xId", 128, BF), ("tId", 128, BF), ("mId", 128, BF), ("I16", 128, F16),
+    ("BO", 128, BF), ("BO16", 128, F16), ("BOs", 128, BF), ("ZC", 128, BF), ("Wu", 128, BF), ("WT", 128, BF), ("WC", 128, BF),
+    ("U64", 144, BF), ("Un32", 144, BF), ("SEL", 2048, BF), ("tri", 256, BF), ("t01", 256, BF), ("cmk", 384, BF),
+    ("R1", 256, BF), ("R2", 256, BF), ("R3", 384, BF), ("dg", 256, BF), ("wc", 256, BF), ("tI", 384, F32), ("tJ", 160, F32),
+    ("vC", 32, F32), ("vD", 32, F16), ("skU", 4, U16), ("skW", 32, BF), ("lC", 16, F32), ("bcF", 72, F32), ("bcU", 56, U16),
+    ("jC", 12, F32), ("pw", 16, F32),
 ]:
     SCRATCH[_n] = ("sbuf", [128, _c], _d)
-for _n, _c, _d in (("ZB", 32, BF), ("T16", 32, F16)):
-    SCRATCH[_n] = ("sbuf", [128, 8, _c], _d)
-for _n, _c, _d in (("X", 4128, BF), ("cR", 384, F32), ("eq", 384, BF), ("cm", 384, BF), ("bS", 384, F32), ("cmk", 384, BF), ("R3", 384, BF), ("R2", 384, BF),
-                   ("bcF", 72, F32), ("bcU", 72, U16), ("tI", 384, F32), ("cS", 384, F32), ("ZT", 48, BF), ("SK", 32, BF), ("skU", 4, U16), ("skW", 32, BF),
-                   ("vC", 32, F32), ("vD", 32, F16), ("Id2", 256, BF), ("ia", 16, I32), ("col", 20, F32), ("Vs", 16, BF), ("f3", 16, F32)):
-    SCRATCH[_n] = ("sbuf", [128, _c], _d)
-for _n in ("Vs", "accS", "uS"):
-    del SCRATCH[_n]
+for _n, _d in (("ZB", BF), ("T16", F16)):
+    SCRATCH[_n] = ("sbuf", [128, 8, 32], _d)
 for _b in range(8):
     SCRATCH["B%d" % _b] = ("psum", [128, 512], F32)
 
 SEMAPHORES = ["sV", "sS", "sP", "sG", "sent", "out"] + ["ld%d" % i for i in range(8)]
 for _t in range(ST):
-    SEMAPHORES += ["rK%d" % _t, "ra%d" % _t, "rz%d" % _t, "rO%d" % _t, "rM%d" % _t, "rA%d" % _t]
+    SEMAPHORES += ["rK%d" % _t, "ra%d" % _t, "rz%d" % _t, "rO%d" % _t, "rM%d" % _t, "rA%d" % _t, "cp%d" % _t]
 
-PAR = {"g": 1.3, "sc": 3.15, "pe": 0.5, "hop": 200, "rem": 540, "lat": 2400,
-       "parts": ((0, 1, 2), (3,)), "kv": 10, "sub": 2, "rv": (3,), "asc": True, "split": True, "zd": "S", "pu": "V", "pb": "P", "dg": ((0, 1), (2,), (3,)),
-       "xs": ((0, 1, "V"), (1, 1, "V"), (2, 1, "V"), (3, 1, "V"), (4, 4, "S"), (8, 4, "S"), (12, 4, "S")), "ys": ((0, 4, "S"), (4, 4, "S"), (8, 4, "S"), (12, 4, "S")),
-       "eng": {"xk": "S", "wk0": "S", "wk1": "S", "zS": "S", "pkB": "S", "pkK": "S", "rb": "V"}}
-PAR["queues"] = {
-    "V": "+sx2 aU +sx1 ra +sx0 n1 x0 n2 g1 g2 g3 spU scB CL1 CL0 bU rb mx0 mx1 k1 mx2 scK mx3 mx4 mx5 mx6 wo mx7 df0_1 mx8 +nth df0_0 df1_0 mx9 df1_1 df2_0 df2_1 kT kS r16 rb16 low ZT0 ZT1 ZB df3_0 vF T16 vU df3_1 cS ab3 eq nS0 pref0 uS cm_0 amI bS_0 amJ f1_0 da nS1 pref1 dl cm_1 t2 bS_1 aS sum1 f1_1 posU f2_1 half offU_1 f2_0 sx15 sx14 s2 sx13 offU_0 sx12 AI sx11 sx10 sx9 sx8 slU sx7 sx6 sx5 AJ sx4 sx3".split(),
-    "S": "+pkA +pkp +pkL +pkB +pkM +pkK +zc +zd +zS x6 x4 x2 y0 y2 mx10 mx12 y4 mx14 ab0 ab1 y6 ab2 a5 bF xw mis0 ob cR zm dvS0 junk0_1 junk0_3 mis1 junk0_0 dvS1 junk0_2 junk1_0 junk1_3 +oz junk1_2 junk1_1".split(),
-    "P": "+ph +pd pc1 pc0 pb pz ps0 kz ps1 pm10 kx8 pw pm12 km2 kx6 km6 km4 pm14 kx0 km12 kx2 km10 km14 km8 kx4 km0 kB da1_0 da1_1 pv pt n0_0 da2_0 pc da2_1 pe pn n1_0 pq0 dl3_0 dl3_1 pu da3_0 da3_1 n0_1 pq1 n1_1".split(),
-    "G": "toK toa toA toP toz".split(),
-    "Y": "ok oa ox".split(),
+PAR = {
+    "g": 1.3, "sc": 3.15, "pe": 0.5, "hop": 200, "rem": 540, "lat": 2400, "slack": 200.0, "near": 300.0,
+    "parts": ((3, 2, 1), (0,)),
+    "kv": 8, "rows": (0, 7, 3, 4),
+    "rv": (3, 0), "subs": (2, 4, 2, 1),
+    "xs": ((0, 2, "V"), (2, 2, "V"), (4, 12, "S")),
+    "xs0": ((0, 2, "V"), (2, 6, "V"), (8, 8, "S")),
+    "ys": ((12, 4, "S"), (8, 4, "S"), (4, 4, "S"), (0, 4, "S")),
+    "pk": "SS",
+    "first": ("aU", "ra", "rb", "x0", "x2", "x8"),
 }
-del PAR["queues"]
-PAR.update({"kv": 8, "rv": (3, 0), "pb": "P", "pu": "P", "asc": False, "split": False, "parts": ((3, 2, 1), (0,)), "dg": ((3,), (2,), (1,), (0,)), "zd": "V", "sub": 4,
-            "xs": ((0, 1, "V"), (1, 1, "V"), (2, 1, "V"), (3, 1, "V"), (12, 4, "S"), (8, 4, "S"), (4, 4, "S")), "ys": ((12, 4, "S"), (8, 4, "S"), (4, 4, "S"), (0, 4, "S")),
-            "first": ("aU", "ra", "rb", "x0", "x1", "x2", "x3", "x4", "x8", "x12"), "zb": "S", "rows": (0, 7, 3, 4), "slack": 200.0, "near": 300.0})
-PAR["order"] = "mx5 +sx5 df3_0 +mx1 mx6 df3_2 +pd kz k1 +a5 ps1 pc1 +mx4 scB +sx4 scK ra n1 rb kx4 pb kx6 g3 CL0 aU +sx0 +rb16 ps0 wo spU x4 +toA x1 x0 pc0 +g2 mx0 bU vU x3 km12 pw CL1 x12 pm8 df0_1 mx3 n2 mx2 x2 x8 pz pm12 da2_1 toK mx7 df3_1 +df1_3 kS kx0 pm10 df3_3 km0 kx2 km8 ZT1 pv wk1 kT km4 df1_0 ZT0 low +df0_0 +g1 km6 km2 zd ZB pm14 mx8 y12 mx14 wk0 ab2 km10 mx12 dl3_0 y8 mx10 pt y4 df2_0 df2_3 T16 dl3_1 df0_3 da1_1 zm ab1 da1_0 df2_1 pkB da0_0 kB n1_0 da0_1 r16 y0 pkL dl0_1 dl0_0 pA mis0 xk da2_0 dvS0 pc ab3 +df0_2 n1_1 cR km14 n0_0 +ph0 pn df2_2 ab0 da3_1 da3_0 cS pq0 df1_2 pkK df1_1 amJ pu junk0_2 cm_0 +bS_0 n0_1 cm_1 ph1 posU da pref0 sx1 pkM half0 dl nS1 bS_1 f0_0 sx6 junk0_1 eq nS0 junk0_3 amI junk0_0 aS f1_0 t2 toa f0_1 toz pkA sx3 f2_0 f1_1 pkp sx2 AI slU offU_0 toP s2 zS half1 offU_1 mis1 f2_1 sx7 nth +AJ".split()
-PAR["order"] = "x8 x12 dl0_1 kS +pkM g2 +sx7 +pz +toa +cR +dl3_1 +dl0_0 x4 ps1 scB ps0 +df2_1 n2 AJ x2 ra pb aU x0 spU g1 CL0 x3 kz g3 offU_0 pc1 mx10 x1 mx8 posU pm12 k1 bU CL1 pm14 mx12 wo y12 mx1 pc0 rb pw mx0 kx0 km2 mx14 n1 kx4 y8 scK km12 ab3 toK kx6 pm8 pm10 kx2 km4 r16 df1_2 rb16 low mx6 ZT1 ZT0 df1_1 mx4 km0 mx3 km8 df3_3 mx5 df3_0 df3_2 pt y4 km6 mx2 df2_0 df0_0 df3_1 kB mx7 ZB wk0 xk pA pv y0 df2_2 eq vU da2_0 kT df1_0 df2_3 da2_1 km14 da3_0 ab1 a5 ab0 km10 cm_0 half0 df0_3 pc dl3_0 ab2 cS nS0 T16 cm_1 df1_3 da3_1 n0_1 df0_1 amI amJ mis0 df0_2 offU_1 sx4 n0_0 dl s2 nS1 zm n1_0 bS_0 pref0 pkB bS_1 dvS0 ph0 pn sx5 sx3 pd toP f3_0 t2 f4_0 pq0 da f0_0 pkA sx1 f3_1 f1_0 da0_1 slU f1_1 mis1 wk1 da0_0 junk0_2 pkL pkp nth da1_1 ph1 da1_0 n1_1 pu half1 zS +aS junk0_0 sx0 sx6 f2_1 zd toz pkK junk0_1 toA sx2 +f2_0 +AI f0_1 f4_1 junk0_3".split()
-PAR.update({"zd": "S", "zb": "V", "eng": {"xk": "S", "wk0": "S", "wk1": "S", "zS": "S", "pkB": "S", "pkK": "S", "rb": "S"}})
-PAR["queues"] = {
-    "V": "aU +sx0 ra n1 x1 x2 x0 n2 g1 +AJ g2 g3 +nth spU x3 scB CL0 CL1 bU mx0 mx1 k1 mx2 scK mx3 mx4 mx5 wo mx6 df3_2 df3_3 df3_0 df3_1 mx7 df2_0 df2_2 df2_3 df2_1 ab3 kS rb16 low r16 ZT1 ZT0 df1_1 SK ZB df1_3 df1_0 vF T16 vU df0_2 df1_2 df0_0 df0_3 df0_1 cS0 half0 cS1 ab0 eq nS0 cm_0 nS1 pref0 amI bS_0 amJ cm_1 dl da f4_0 f3_0 f0_0 t2 f1_0 half1 aS bS_1 f2_0 posU offU_0 AI f3_1 f4_1 f0_1 sx7 s2 f1_1 sx6 slU f2_1 sx5 sx4 offU_1 sx3 sx2 sx1".split(),
-    "S": "a5 x4 x8 x12 rb y12 y8 bF mx12 mx8 mx14 mx10 y4 y0 ab2 wk0 wk1 xk ab1 cR mis0 mis1 zm dvS0 pkA junk0_2 ob junk0_1 junk0_0 junk0_3 pkp pkB pkL pkM pkK zc ok zd zS".split(),
-    "P": "+pq0 +n0_1 +n1_1 +pu +pd pc0 pc1 pz pb kz ps0 ps1 kx0 pm8 pw pm12 pm10 pm14 km0 km2 km12 km8 kx2 km6 km4 kx4 km14 kx6 km10 kB dl3_0 dl3_1 da3_0 n0_0 pZ da3_1 pv pt pA da2_0 pc da2_1 pn ph0 dl0_0 dl0_1 da1_0 da1_1 da0_0 da0_1 n1_0 ph1".split(),
-    "G": "+toa +toP +toz toK toA".split(),
-    "Y": "+oz oa ox".split(),
+STEP = {
+    "V": "+AI aU +sx1 ra +sx0 n1 x0 x2 n2 g1 g2 g3 spU scB CL0 CL1 bU +AJ mx0 mx1 k1 scK mx2 mx3 mx4 wo mx5 mx6 df3_0 +nth mx7 df2_0 ab3 df2_1 "
+         "kS rb16 low r16 ZT1 ZT0 df1_3 SK ZB df1_1 vF df1_0 vU df1_2 T16 df0_0 df0_1 cS0 cS1 ab0 uS amI eq amJ nS0 da cm_0 nS1 pref t2 bS_0 cm_1 aS "
+         "f3_0 f4_0 f0_0 f1_0 half0 f2_0 bS_1 dl offU_0 posU f0_1 sx7 f4_1 half1 f3_1 sx6 f1_1 sx5 f2_1 sx4 s2 offU_1 sx3 slU sx2",
+    "S": "+zc +zd +zS x4 rb a5 y12 y8 mx8 mx12 mx14 mx10 y4 y0 ab2 wk0 wk1 ab1 zm cR xk mis0 mis1 dvS junk1 junk0 junk2 junk3 pkA pkp pkB pkL pkK pkM",
+    "P": "po0 pc0 po1 pc1 pz pb ps0 ps1 kz pm8 pw pm12 kx6 pm14 kx0 pm10 km2 km0 kx2 km8 km6 km4 km14 kx4 km12 km10 kB dl3_0 dl3_1 da3_0 "
+         "pZ pv n0_0 da3_1 pt pA da2_0 pc da2_1 n0_1 pn pe da1_0 da1_1 pu dl0_0 dl0_1 da0_0 da0_1 n1_0 pq n1_1 pd ph0 ph1",
+    "G": "+toa +toA +toP +toz toK",
+    "Y": "+oz cp ox",
 }
+LAST = {"V": "aI n1 aJ aK n2 g1 g2 CL0 g3 spU CL1 scB k1 scK", "P": "po0 po1 pc0 pc1 ps0 ps1 pb", "G": "", "Y": "oa",
+        "S": "+pkA +junk1 +junk0 +junk2 +junk3 +pkp +pkB +pkL +pkK +pkM +zc +zd +zS bF ob ok"}
+PAR["queues"] = {e: s.split() for e, s in STEP.items()}
+PAR["last"] = {e: s.split() for e, s in LAST.items()}
 NCH = 4
-HALF = 0.5 - 2.0 ** -11
 CH = 256 // NCH
+HALF = 0.5 - 2.0 ** -11
+AS = 16384.0
 A = AluOpType
 AF = ActivationFunctionType
 
@@ -86,7 +81,7 @@ def build(g, core, T, topo, par):
     last_w, readers, bank_last = {}, {}, {}
     V, S, PE, SY = g.vector, g.scalar, g.tensor, g.sync
 
-    def op(alts, reads, writes, banks=(), ext=(), after=(), lat=0, sem=None, semn=1, nm=None):
+    def op(e, cost, f, reads, writes, banks=(), ext=(), after=(), lat=0, sem=None, semn=1, nm=None):
         i = len(ops)
         deps = {}
         for k in reads:
@@ -108,47 +103,33 @@ def build(g, core, T, topo, par):
             last_w[k] = i
             readers[k] = []
         for b in banks:
-            e = list(alts)[0]
             prev = bank_last.get(b, [])
-            if prev and list(ops[prev[-1]]["alts"])[0] == e:
-                bank_last[b] = prev + [i]
-            else:
-                bank_last[b] = [i]
+            bank_last[b] = prev + [i] if prev and ops[prev[-1]]["e"] == e else [i]
         deps.pop(i, None)
-        nm = nm or writes[0]
-        e = par["eng"].get(nm)
-        if e in alts:
-            alts = {e: alts[e]}
-        ops.append({"alts": alts, "deps": deps, "ext": list(ext), "lat": lat, "sem": sem, "semn": semn, "nm": nm, "t": cur[0]})
+        ops.append({"e": e, "alts": {e: (cost, f)}, "deps": deps, "ext": list(ext), "lat": lat, "sem": sem, "semn": semn, "nm": nm or writes[0], "t": cur[0]})
         return i
 
     def cv(n, half=False):
         return max(64, n * (0.5 if half else 1.0))
 
     def vts(out, in0, s1, s2, o0, o1, n, R, W, banks=(), half=False, ext=(), after=(), nm=None):
+        if cur[0] < 0 and o0 == A.mult and W[0] not in ("I16", "BO16", "hId") and (o1 is None or (o1 == A.add and isinstance(s2, float))):
+            return op("S", cv(n) + 20, lambda: S.activation(out, in0, AF.Copy, bias=s2 or 0.0, scale=s1), R, W, nm=nm)
         if o1 is None:
-            f = lambda: V.tensor_scalar(out, in0, s1, None, o0)
-        else:
-            f = lambda: V.tensor_scalar(out, in0, s1, s2, o0, o1)
-        alts = {"V": (cv(n, half), f)}
-        if cur[0] < 0 and o0 == A.mult and W[0] not in ("I16", "BO16", "hId", "thF") and (o1 is None or (o1 == A.add and isinstance(s2, float))):
-            alts["S"] = (cv(n) + 20, lambda: S.activation(out, in0, AF.Copy, bias=s2 or 0.0, scale=s1))
-        return op(alts, R, W, banks, ext, after, nm=nm)
+            return op("V", cv(n, half), lambda: V.tensor_scalar(out, in0, s1, None, o0), R, W, banks, ext, after, nm=nm)
+        return op("V", cv(n, half), lambda: V.tensor_scalar(out, in0, s1, s2, o0, o1), R, W, banks, ext, after, nm=nm)
 
     def vtt(out, in0, in1, o, n, R, W, banks=(), ext=(), after=(), nm=None):
-        return op({"V": (cv(n if banks else 2 * n), lambda: V.tensor_tensor(out, in0, in1, o))}, R, W, banks, ext, after, nm=nm)
+        return op("V", cv(n if banks else 2 * n), lambda: V.tensor_tensor(out, in0, in1, o), R, W, banks, ext, after, nm=nm)
 
-    def vcp(out, in_, n, R, W, banks=(), half=False, ext=(), after=(), nm=None):
-        return op({"V": (cv(n, half), lambda: V.tensor_copy(out, in_))}, R, W, banks, ext, after, nm=nm)
+    def vcp(out, in_, n, R, W, banks=(), ext=(), after=(), nm=None):
+        return op("V", cv(n), lambda: V.tensor_copy(out, in_), R, W, banks, ext, after, nm=nm)
 
-    def vscan(out, d0, d1, init, o0, o1, n, R, W, banks=(), half=False, nm=None):
-        return op({"V": (cv(n, half), lambda: V.tensor_tensor_scan(out, d0, d1, init, o0, o1))}, R, W, banks, nm=nm)
+    def vscan(out, d0, d1, o0, o1, n, R, W, banks=(), half=False, nm=None):
+        return op("V", cv(n, half), lambda: V.tensor_tensor_scan(out, d0, d1, 0.0, o0, o1), R, W, banks, nm=nm)
 
-    def vset(ap, val, n, W):
-        if W[0] == "ones":
-            return op({"V": (cv(n, True), lambda: V.memset(ap, val))}, [], W)
-        return op({"V": (cv(n, True), lambda: V.memset(ap, val)),
-                   "S": (cv(n) + 20, lambda: S.activation(ap, T.ones[:, 0:n], AF.Copy, scale=val))}, ["ones"], W)
+    def fill(ap, val, n, W):
+        return op("S", cv(n) + 20, lambda: S.activation(ap, T.ones[:, 0:n], AF.Copy, scale=val), ["ones"], W)
 
     def act(out, in_, f, n, R, W, banks=(), bias=None, scale=None, accum=None, gather=False, ext=(), after=(), nm=None):
         kw = {}
@@ -159,40 +140,30 @@ def build(g, core, T, topo, par):
         if accum is not None:
             kw["accum_out"] = accum
         c = n * par["g"] + 65 if gather else cv(n) + 20
-        return op({"S": (c, lambda: S.activation(out, in_, f, **kw))}, R, W, banks, ext, after, nm=nm)
+        return op("S", c, lambda: S.activation(out, in_, f, **kw), R, W, banks, ext, after, nm=nm)
 
-    def gath(out, win, off, n, R, W, engs="VS", ext=(), after=(), nm=None):
-        alts = {}
-        if "V" in engs:
-            alts["V"] = (n * par["g"] + 50, lambda: V.tensor_copy(out, win.indirect(off)))
-        if "S" in engs:
-            alts["S"] = (n * par["g"] + 65, lambda: S.activation(out, win.indirect(off), AF.Copy))
-        return op(alts, R, W, (), ext, after, nm=nm)
+    def gath(e, out, win, off, n, R, W, nm=None):
+        if e == "V":
+            return op("V", n * par["g"] + 50, lambda: V.tensor_copy(out, win.indirect(off)), R, W, nm=nm)
+        return op("S", n * par["g"] + 65, lambda: S.activation(out, win.indirect(off), AF.Copy), R, W, nm=nm)
 
-    def gtt(out, win, off, in1, o, n, R, W, nm=None):
-        return op({"V": (n * par["g"] + 50, lambda: V.tensor_tensor(out, win.indirect(off), in1, o))}, R, W, nm=nm)
+    def gtt(out, win, off, in1, o, n, R, W):
+        return op("V", n * par["g"] + 50, lambda: V.tensor_tensor(out, win.indirect(off), in1, o), R, W)
 
     def scat(win, off, in_, n, R, W, ext=(), after=(), nm=None):
-        return op({"V": (n * par["sc"] + 50, lambda: V.tensor_copy(win.indirect(off), in_))}, R, W, (), ext, after, nm=nm)
+        return op("V", n * par["sc"] + 50, lambda: V.tensor_copy(win.indirect(off), in_), R, W, (), ext, after, nm=nm)
 
     def mm(nm, lst, R, W, bank, start, stop, ext=(), after=()):
-        c = sum(max(64, m[3]) for m in lst) * par["pe"]
-
         def f():
             r = None
             for j, m in enumerate(lst):
                 r = PE.matmul(m[0], m[1], m[2], start and j == 0, stop and j == len(lst) - 1)
             return r
-        i = op({"P": (c, f)}, R, W, () if bank is None else (bank,), ext, after, nm=nm)
-        ops[i]["calls"] = len(lst)
-        return i
-
-    def pool(c, f, R, W):
-        return op({"G": (c, f)}, R, W)
+        return op("P", sum(max(64, m[3]) for m in lst) * par["pe"], f, R, W, () if bank is None else (bank,), ext, after, nm=nm)
 
     def dma(q, out, in_, R, W, sem, lat, nm="dma"):
         e = {"Y": SY, "S": S}[q]
-        return op({q: (60, lambda: e.dma_start(out, in_))}, R, W, lat=lat, sem=sem, semn=16, nm=nm)
+        return op(q, 60, lambda: e.dma_start(out, in_), R, W, lat=lat, sem=sem, semn=16, nm=nm)
 
     nsent = [0]
 
@@ -215,42 +186,39 @@ def build(g, core, T, topo, par):
                 tr.append(RemoteDMATransfer(dst_ids=[DstId(rid=rid, pnc=pid)], dma_engine_mask=m, remote_sem=T.sem[sem], src=src, dst=dst))
             return g.remote_dma_fused(tr, local_sem=T.sem.sent)
         nsent[0] += NE
-        return op({"G": (par["rem"], f)}, R, [], lat=lat, sem="none", nm=nm)
+        return op("G", par["rem"], f, R, [], lat=lat, sem="none", nm=nm)
 
     NE = len(topo.engines(core, T.cores[(rank + 1) % NR]))
     B = [T["B%d" % i] for i in range(8)]
-
-    def cols(b, c0, c1):
-        return B[b][:, c0:c1]
     allx = ["x%d" % c for c in range(16)]
     ally = ["y%d" % c for c in range(16)]
+    Xr = ["Xm", "Xd"]
 
     def phrases(nm, lst, base, pieces):
         for b0, nb, e in pieces:
-            gath(T.XY[:, base + 256 * b0:base + 256 * (b0 + nb)], T.X[:, 0:4096], T[lst][:, 16 * b0:16 * (b0 + nb)], 256 * nb, [lst, "Xm", "Xd"],
-                 ["%s%d" % (nm, b) for b in range(b0, b0 + nb)], e)
+            gath(e, T.XY[:, base + 256 * b0:base + 256 * (b0 + nb)], T.X[:, 0:4096], T[lst][:, 16 * b0:16 * (b0 + nb)], 256 * nb, [lst] + Xr,
+                 ["%s%d" % (nm, b) for b in range(b0, b0 + nb)])
 
     dma("Y", T.avI[:], T.av[:], [], ["avI"], "ld0", 2500)
     dma("Y", T.bvI[:], T.bv[:], [], ["bvI"], "ld3", 2500)
-    dma("Y", T.P[:], T.rp[:], [], ["P"], "ld1", 4500)
+    dma("Y", T.P[:, 0:1024], T.rp[:], [], ["P0"], "ld1", 4500)
     dma("S", T.X[:, 0:4096], T.ph[:], [], ["Xm"], "ld2", 5500)
     dma("Y", T.kcI[:], T.kc[:], [], ["kcI"], "ld4", 5500)
     dma("Y", T.zb[:, 0:256], T.zs[:], [], ["z0"], "ld5", 5500)
-    op({"G": (300, lambda: g.dma_start(T.thI[:, 0:1], T.th[:], allow_slow_non_contiguous=True))}, [], ["thI"], lat=3000, sem="ld6", semn=16)
+    op("G", 300, lambda: g.dma_start(T.thI[:, 0:1], T.th[:], allow_slow_non_contiguous=True), [], ["thI"], lat=4000, sem="ld6", semn=16)
 
     def iota(out, pat, base, cm, n, W, fl=True):
         if fl:
-            return pool(160 + 2 * n, lambda: g.iota(out, pat, base, cm, allow_small_or_imprecise_dtypes=True), [], W)
-        return pool(160 + 2 * n, lambda: g.iota(out, pat, base, cm), [], W)
+            return op("G", 160 + 2 * n, lambda: g.iota(out, pat, base, cm, allow_small_or_imprecise_dtypes=True), [], W)
+        return op("G", 160 + 2 * n, lambda: g.iota(out, pat, base, cm), [], W)
 
-    col = T.col
-    vset(T.ones[:], 1.0, 256, ["ones"])
-    iota(T["io"][:, 0:1], [[0, 1]], 0, 1, 1, ["io"], False)
+    col, p_ = T.col, T["io"][:, 0:1]
+    op("V", 128, lambda: V.memset(T.ones[:], 1.0), [], ["ones"])
+    iota(p_, [[0, 1]], 0, 1, 1, ["io"], False)
     iota(T.tJ[:], [[1, 160]], -16, -1, 160, ["tJ"])
     iota(T.tI[:], [[0, 24], [1, 16]], 0, 0, 384, ["tI"])
-    vts(T.ia[:, 0:1], T["io"][:, 0:1], 15, None, A.bitwise_and, None, 1, ["io"], ["ia0"])
-    vts(T.ia[:, 1:2], T["io"][:, 0:1], 16, None, A.bitwise_and, None, 1, ["io"], ["ia1"])
-    vcp(col[:, 0:2], T.ia[:, 0:2], 2, ["ia0", "ia1"], ["c0"])
+    vts(T.ia[:, 0:1], p_, 15, None, A.bitwise_and, None, 1, ["io"], ["ia0"])
+    vcp(col[:, 0:1], T.ia[:, 0:1], 1, ["ia0"], ["c0"])
     r_ = col[:, 0:1]
     vts(col[:, 2:3], r_, -1.0, -1.0, A.mult, A.add, 1, ["c0"], ["c2"])
     vts(T.U64[:], T.tJ[:, 0:144], col[:, 2:3], 64.0, A.is_equal, A.mult, 144, ["tJ", "c2"], ["U64"])
@@ -263,101 +231,94 @@ def build(g, core, T, topo, par):
         return T[U][:, 15 - k:143 - k]
     vts(T.kS[:, 0:128], T.tJ[:, 16:144], r_, -7.5, A.add, A.add, 128, ["tJ", "c0"], ["kS"])
     vtt(T.cR[:, 0:128], T.kS[:, 0:128], T.kS[:, 0:128], A.mult, 128, ["kS"], ["cR"])
-    op({"V": (384, lambda: V.memset(T.cS[:], 0.0))}, [], ["cS0", "cS1", "cSx"])
     vts(T.BO[:], T.cR[:, 0:128], 60.0, None, A.is_lt, None, 128, ["cR"], ["BO"])
     vts(T.BO16[:], T.BO[:], 1.0, None, A.mult, None, 128, ["BO"], ["BO16"], half=True)
-    vts(T.BOs[:], T.BO[:], 0.0625, None, A.mult, None, 128, ["BO"], ["BOs"], half=True)
+    vts(T.BOs[:], T.BO[:], -0.0625, None, A.mult, None, 128, ["BO"], ["BOs"], half=True)
     KV = par["kv"]
-    if KV > 0:
-        vts(T.kT[:, 0:128], T.tI[:, 0:128], float(KV), -32.0, A.is_lt, A.mult, 128, ["tI"], ["kT"])
-        vtt(T.ZC[:], T.kT[:, 0:128], T.BO[:], A.mult, 128, ["kT", "BO"], ["ZC"])
+    vts(T.kT[:, 0:128], T.tI[:, 0:128], float(KV), -32.0, A.is_lt, A.mult, 128, ["tI"], ["kT"])
+    vtt(T.ZC[:], T.kT[:, 0:128], T.BO[:], A.mult, 128, ["kT", "BO"], ["ZC"])
     vts(col[:, 3:4], r_, 2.0, 1.0, A.mult, A.add, 1, ["c0"], ["c3"])
-    if par["pu"] == "P":
-        vts(T.Wu[:], T.tJ[:, 0:144], col[:, 2:3], col[:, 3:4], A.is_equal, A.mult, 144, ["tJ", "c2", "c3"], ["Wu"])
-    else:
-        vts(T.Wu[:, 0:128], T.BO[:], col[:, 3:4], None, A.mult, None, 128, ["BO", "c3"], ["Wu"], half=True)
+    vts(T.Wu[:], T.BO[:], col[:, 3:4], None, A.mult, None, 128, ["BO", "c3"], ["Wu"], half=True)
     iota(T.nS[:, 0:128], [[2, 8], [0, 16]], 0, -1, 128, ["nS0"])
     vts(T.nS[:, 128:256], T.nS[:, 0:128], 0.0, 131072.0, A.is_equal, A.mult, 128, ["nS0"], ["nS1"])
-    vts(col[:, 5:6], T["io"][:, 0:1], 1.0, 4096.0, A.is_equal, A.mult, 1, ["io"], ["c5"])
+    vts(col[:, 5:6], p_, 1.0, 4096.0, A.is_equal, A.mult, 1, ["io"], ["c5"])
     vts(col[:, 6:7], col[:, 5:6], -39.0, None, A.mult, None, 1, ["c5"], ["c6"])
     vts(T.WC[:], T.nS[:, 128:256], col[:, 6:7], None, A.add, None, 128, ["nS1", "c6"], ["WC"])
     vts(T.kS[:, 128:256], T.tI[:, 0:128], 32.0, col[:, 5:6], A.add, A.mult, 128, ["tI", "c5"], ["kT2"])
     vtt(T.WT[:], T.kS[:, 128:256], T.nS[:, 128:256], A.subtract, 128, ["kT2", "kS", "nS1"], ["WT"])
     vts(T.tri[:], T.tI[:, 0:256], r_, 8192.0, A.is_gt, A.mult, 256, ["tI", "c0"], ["tri"])
+    vts(T.t01[:], T.tri[:], 1.0 / 8192, None, A.mult, None, 256, ["tri"], ["t01"], half=True)
     spans = [(2 * min(cs), 2 * max(cs) + 2) for cs in par["parts"]]
     for pi, (w0, w1) in enumerate(spans):
-        vts(T.cmk[:, 48 * w0:16 * w0 + 32 * w1], T.tri[:, 0:32 * (w1 - w0)], 1.1875, 16.0, A.max, A.min, 256, ["tri"], ["cmk_%d" % pi], half=True)
-        vset(T.cmk[:, 16 * w0 + 32 * w1:48 * w1], 1.1875, 16 * (w1 - w0), ["cmj_%d" % pi])
-    vts(T.R2[:], T.tI[:], r_, 1048576.0, A.is_le, A.mult, 384, ["tI", "c0"], ["R2"])
-    vts(T.bS[:, 0:256], T.tI[:, 0:256], 0.0, 1048576.0, A.is_equal, A.mult, 256, ["tI"], ["bS_0", "bS_1"], nm="uS")
+        vts(T.cmk[:, 48 * w0:16 * w0 + 32 * w1], T.t01[:, 0:32 * (w1 - w0)], -15.0, -0.1875, A.mult, A.add, 256, ["t01"], ["cmk_%d" % pi], half=True)
+        fill(T.cmk[:, 16 * w0 + 32 * w1:48 * w1], -0.1875, 16 * (w1 - w0), ["cmj_%d" % pi])
+        fill(T.cS[:, 16 * w0 + 32 * w1:48 * w1], 0.0, 16 * (w1 - w0), ["cSx%d" % pi])
+    vts(T.R2[:], T.t01[:], -1048576.0, 1048576.0, A.mult, A.add, 256, ["t01"], ["R2"])
+    vts(T.bS[:, 0:256], T.tI[:, 0:256], 0.0, 1048576.0, A.is_equal, A.mult, 256, ["tI"], ["bS_0", "bS_1"])
     vts(T.R1[:], T.bS[:, 0:256], 1.0, -1.0, A.mult, A.add, 256, ["bS_0", "bS_1"], ["R1"])
     vts(T.R3[:], T.tI[:], 0.0, 2.0, A.not_equal, A.mult, 384, ["tI"], ["R3"])
     vts(T.dg[:], T.tI[:, 0:256], r_, None, A.is_equal, None, 256, ["tI", "c0"], ["dg"])
-    vscan(T.pw[:], T.R3[:, 0:16], T.dg[:, 0:16], 0.0, A.mult, A.add, 16, ["R3", "dg"], ["pw"])
-    vset(col[:, 14:15], 0.1875, 1, ["c14"])
+    vscan(T.pw[:], T.R3[:, 0:16], T.dg[:, 0:16], A.mult, A.add, 16, ["R3", "dg"], ["pw"])
+    fill(col[:, 14:15], 0.1875, 1, ["c14"])
     vts(col[:, 12:13], r_, 4096.0, None, A.add, None, 1, ["c0"], ["c12"])
     vts(col[:, 13:14], r_, 4112.0, None, A.add, None, 1, ["c0"], ["c13"])
-    NSUB = par["sub"]
-    DCH = CH // NSUB
-    iota(T.wc[:], [[0, 256 // DCH], [16, DCH]], 0, 0, 256, ["wc"])
+    iota(T.wc[:], [[0, NCH], [16, CH]], 0, 0, 256, ["wc"])
     iota(T.bcF[:, 0:16], [[16, 16]], 15, 0, 16, ["bc0"])
     iota(T.bcF[:, 16:48], [[1, 32]], 0, 0, 32, ["bc1"])
     for pi, (w0, w1) in enumerate(spans):
         iota(T.bcF[:, 48 + 3 * w0:48 + w0 + 2 * w1], [[16, 2 * (w1 - w0)]], 48 * w0 + 15, 0, 16, ["bc2%d" % pi])
         iota(T.bcF[:, 48 + w0 + 2 * w1:48 + 3 * w1], [[32, w1 - w0]], 48 * w0 + 31, 0, 8, ["bc3%d" % pi])
-    vcp(T.bcU[:], T.bcF[:], 72, ["bc0", "bc1", "bc20", "bc21", "bc30", "bc31"], ["bcU"])
+    vcp(T.bcU[:], T.bcF[:, 16:72], 56, ["bc1", "bc20", "bc21", "bc30", "bc31"], ["bcU"])
     vts(T.lC[:], T.bcF[:, 0:16], r_, -15.0, A.add, A.add, 16, ["bc0", "c0"], ["lC"])
     vts(T.vC[:, 0:16], T.lC[:], 1.0, None, A.add, None, 16, ["lC"], ["vC0"])
-    for pi, cs in enumerate(par["parts"]):
-        q0, q1 = 4 * min(cs), 4 * max(cs) + 4
-        vts(T.vC[:, 16 + q0:16 + q1], T.lC[:, q0:q1], -2.0 - 16 * q0, None, A.add, None, 16, ["lC"], ["vC%d" % (pi + 1)])
+    for pi, (w0, w1) in enumerate(spans):
+        vts(T.vC[:, 16 + 2 * w0:16 + 2 * w1], T.lC[:, 2 * w0:2 * w1], -2.0 - 32 * w0, None, A.add, None, 16, ["lC"], ["vC%d" % (pi + 1)])
     vts(T.jC[:, 0:4], T.lC[:, 0:4], 2.0, 1.0, A.mult, A.add, 4, ["lC"], ["jC0"])
     vts(T.jC[:, 4:8], T.lC[:, 0:4], -2.0, -1.0, A.mult, A.add, 4, ["lC"], ["jC1"])
     vts(T.jC[:, 8:12], T.lC[:, 0:4], 256.0, None, A.add, None, 4, ["lC"], ["jC2"])
-    vset(T.ZT[:, 17:48:2], 1.0, 16, ["ZT2"])
+    fill(T.ZT[:, 17:48:2], 1.0, 16, ["ZT2"])
     iota(T.ia[:, 4:5], [[0, 1]], 128, -1, 1, ["ia4"], False)
-    vts(T.ia[:, 8:9], T["io"][:, 0:1], 4, None, A.arith_shift_right, None, 1, ["io"], ["ia8"])
-    vts(T.ia[:, 9:10], T["io"][:, 0:1], 8, None, A.bitwise_and, None, 1, ["io"], ["ia9"])
-    vtt(T.ia[:, 10:11], T.ia[:, 8:9], T["io"][:, 0:1], A.add, 1, ["ia8", "io"], ["ia10"])
+    vts(T.ia[:, 8:9], p_, 4, None, A.arith_shift_right, None, 1, ["io"], ["ia8"])
+    vts(T.ia[:, 9:10], p_, 8, None, A.bitwise_and, None, 1, ["io"], ["ia9"])
+    vtt(T.ia[:, 10:11], T.ia[:, 8:9], p_, A.add, 1, ["ia8", "io"], ["ia10"])
     vtt(T.ia[:, 11:12], T.ia[:, 8:9], T.ia[:, 4:5], A.add, 1, ["ia8", "ia4"], ["ia11"])
     vts(T.ia[:, 12:14], T.ia[:, 10:12], 7, None, A.bitwise_and, None, 2, ["ia10", "ia11"], ["ia12"])
     vcp(col[:, 7:8], T.ia[:, 9:10], 1, ["ia9"], ["c7"])
     vts(col[:, 8:10], T.ia[:, 12:14], col[:, 7:8], None, A.add, None, 2, ["ia12", "c7"], ["c8"])
-    vcp(col[:, 16:20:2], col[:, 8:10], 2, ["c8"], ["c16"])
+    vts(col[:, 16:20:2], col[:, 8:10], 1.0, None, A.mult, None, 2, ["c8"], ["c16"])
     vts(col[:, 17:18], col[:, 8:9], 2.0, 16.0, A.mult, A.add, 1, ["c8"], ["c17"])
-    vts(col[:, 19:20], col[:, 9:10], 16.0, None, A.add, None, 1, ["c8"], ["c19"])
+    vts(col[:, 19:20], col[:, 9:10], 1.0, 16.0, A.mult, A.add, 1, ["c8"], ["c19"])
     vcp(T.skU[:], col[:, 16:20], 4, ["c16", "c17", "c19"], ["skU"])
-    vset(T.skW[:, 0:16], 1.0, 16, ["skW0"])
-    vset(T.skW[:, 16:32], 32.0, 16, ["skW1"])
-    gath(T.vD[:], T.vC[:], T.skU[:, 2:4], 32, ["skU", "vC0", "vC1", "vC2"], ["vD"], "V")
+    fill(T.skW[:, 0:16], 1.0, 16, ["skW0"])
+    fill(T.skW[:, 16:32], 32.0, 16, ["skW1"])
+    gath("V", T.vD[:], T.vC[:], T.skU[:, 2:4], 32, ["skU", "vC0", "vC1", "vC2"], ["vD"])
     for j, nm in enumerate(("Id2a", "Id2b")):
         vts(T.Id2[:, 128 * j:128 * j + 128], T.Id[:], 1.0, None, A.mult, None, 128, ["Id"], [nm], half=True)
-    vset(T.X[:, 4096:4128], 0.0, 32, ["Xd"])
-    vset(T.mis[:, 256:272], 0.0, 16, ["misd"])
-    for t in range(ST):
-        vset(T.pkS[:, PKW * t + 128:PKW * t + 136], 0.0, 8, ["pkp%d" % t])
+    fill(T.X[:, 4096:4128], 0.0, 32, ["Xd"])
+    fill(T.mis[:, 256:272], 0.0, 16, ["misd"])
     vts(col[:, 15:16], r_, 16.0, -15.0, A.mult, A.add, 1, ["c0"], ["c15"])
-    vset(T.KB[:, 256:320], 0.0, 64, ["Kd0"])
+    fill(T.KB[:, 256:320], 0.0, 64, ["Kd0"])
     for t in range(ST):
-        vset(T.KB[:, KBW * t + 576:KBW * t + 640], 0.0, 64, ["Be%d" % t])
+        fill(T.pkS[:, PKW * t + 128:PKW * t + 136], 0.0, 8, ["pkp%d" % t])
+        fill(T.KB[:, KBW * t + 576:KBW * t + 640], 0.0, 64, ["Be%d" % t])
     for j in range(8):
-        pool(720, lambda j=j: g.affine_select(T.SEL[:, 256 * j:256 * j + 256], T.ones[:], [[1, 2], [16, 8], [0, 16]], A.is_equal, 0.0, 2 * j, -1),
-             ["ones"], ["SEL%d" % j])
+        op("G", 720, lambda j=j: g.affine_select(T.SEL[:, 256 * j:256 * j + 256], T.ones[:], [[1, 2], [16, 8], [0, 16]], A.is_equal, 0.0, 2 * j, -1),
+           ["ones"], ["SEL%d" % j])
 
-    vcp(T.aF[:, 0:16], T.avI[:], 16, ["avI"], ["a0"])
+    vts(T.aF[:, 0:16], T.avI[:], 0.0, 1.0 / AS, A.add, A.mult, 16, ["avI"], ["a0"])
     vts(T.s1[:], T.lC[:], 2.0, None, A.mult, None, 16, ["lC"], ["s1"])
     vcp(T.bU[:], T.bvI[:], 16, ["bvI"], ["bU"])
     vts(T.hJ[:, 0:16], T.bvI[:], 992, None, A.bitwise_and, None, 16, ["bvI"], ["hJ0"])
     vts(T.hJ[:, 16:32], T.bvI[:], 31, None, A.bitwise_and, None, 16, ["bvI"], ["hJ1"])
     vcp(T.hl[:], T.hJ[:], 32, ["hJ0", "hJ1"], ["hl"])
     for j in range(2):
-        gtt(T.hm[:, 256 * j:256 * j + 256], T.hl[:, 0:32], T.bcU[:, 16 + 16 * j:32 + 16 * j], T.dg[:], A.mult, 256, ["hl", "bcU", "dg"], ["hm%d" % j])
+        gtt(T.hm[:, 256 * j:256 * j + 256], T.hl[:, 0:32], T.bcU[:, 16 * j:16 + 16 * j], T.dg[:], A.mult, 256, ["hl", "bcU", "dg"], ["hm%d" % j])
     mm("hm", [(B[3][:, 0:256], DG("U64", 0), T.hm[:, 0:256], 256), (B[3][:, 0:256], DG("U64", 1), T.hm[:, 256:512], 256)],
        ["hm0", "hm1", "U64"], ["b3"], 3, True, True)
     act(T.KB[:, 320:576], B[3][:, 0:256], AF.Copy, 256, ["b3"], ["Bd0"], (3,), scale=1.0 / 64)
     cur[0] = 0
-    vts(T.thF[:, 0:1], T.thI[:, 0:1], -1.0, -0.5, A.mult, A.add, 1, ["thI"], ["thF"], nm="g1")
-    vcp(T.nth[:, 0:1], T.thF[:, 0:1], 1, ["thF"], ["nth"], nm="k1")
+    vts(T.thF[:, 0:1], T.thI[:, 0:1], -1.0, -0.5, A.mult, A.add, 1, ["thI"], ["thF"])
+    vcp(T.nth[:, 0:1], T.thF[:, 0:1], 1, ["thF"], ["nth"], nm="nth0")
     vcp(T.KB[:, 0:256], T.kcI[:], 256, ["kcI"], ["K0"], nm="n1")
 
     M32 = 1.5 * 2 ** 28
@@ -390,85 +351,74 @@ def build(g, core, T, topo, par):
         vtt(T.g3[:], T.g2[:], T.jC[:, 8:12], A.min, 4, ["g2", "jC2"], ["g3"])
         vcp(T.spU[:], T.g3[:], 4, ["g3"], ["spU"])
         scat(T.KB[:, ko + 320:ko + 640], T.spU[:], m[:, own + 144:own + 208], 64, ["spU", "Be%d" % tk], ["Bd%d" % tk, "Be%d" % tk], ext=kE + mE, after=kA + mA, nm="scB")
-        if par["pb"] == "P":
-            mm("pb", [(B[5][:, 288:304], DG("U64", j), T.KB[:, ko + 320 + j:ko + 576:16], 16) for j in range(16)], ["U64", "Bd%d" % tk], ["b5b"], 5, True, True)
-            if last:
-                act(T.bF[:], B[5][:, 288:304], AF.Copy, 16, ["b5b"], ["bF"], (5,), scale=1.0 / 64)
-            else:
-                vts(T.bU[:], B[5][:, 288:304], 1.0 / 64, None, A.mult, None, 16, ["b5b"], ["bU"], (5,))
+        mm("pb", [(B[5][:, 288:304], DG("U64", j), T.KB[:, ko + 320 + j:ko + 576:16], 16) for j in range(16)], ["U64", "Bd%d" % tk], ["b5b"], 5, True, True)
+        if last:
+            act(T.bF[:], B[5][:, 288:304], AF.Copy, 16, ["b5b"], ["bF"], (5,), scale=1.0 / 64)
         else:
-            mm("pa", [(B[5][:, 0:256], T.Id[:], T.tri[:], 256)], ["Id", "tri"], ["b5"], 5, True, False)
-            mm("pb", [(B[5][:, 0:256], T.BO[:], T.KB[:, ko + 320:ko + 576], 256)], ["BO", "Bd%d" % tk], ["b5"], 5, False, True)
-            vscan(T.uS[:], T.R2[:], B[5][:, 0:256], 0.0, A.add, A.min, 256, ["R2", "b5"], ["uS"], (5,), nm="bT")
-            if last:
-                act(T.bF[:], T.uS[:, 15:256:16], AF.Copy, 16, ["uS"], ["bF"])
-            else:
-                vcp(T.bU[:], T.uS[:, 15:256:16], 16, ["uS"], ["bU"])
+            vts(T.bU[:], B[5][:, 288:304], 1.0 / 64, None, A.mult, None, 16, ["b5b"], ["bU"], (5,))
         Ko, Km = o[:, own + 64:own + 128], m[:, own + 208:own + 272]
         for hb in range(2):
             bk = 3 + hb
-            lst = []
-            for j in range(8):
-                lst.append((cols(bk, 64 * j, 64 * j + 64), T.mId[:], Ko, 64))
-                mi = 8 * hb + j
-                lst.append((cols(bk, 64 * j, 64 * j + 64), T.SEL[:, 128 * mi:128 * mi + 128], Km, 64))
-            mm("pc%d" % hb, lst, ["SEL%d" % j for j in range(8)] + ["mId"] + oR("K"), ["b%d" % bk, "b%du" % bk], bk, True, True, ext=oE + mE, after=oA + mA)
+            mm("po%d" % hb, [(B[bk][:, 64 * j:64 * j + 64], T.mId[:], Ko, 64) for j in range(8)], ["mId"] + oR("K"), ["b%d" % bk, "b%du" % bk], bk, True, False, ext=oE, after=oA)
+            mm("pc%d" % hb, [(B[bk][:, 64 * j:64 * j + 64], T.SEL[:, 128 * (8 * hb + j):128 * (8 * hb + j) + 128], Km, 64) for j in range(8)],
+               ["SEL%d" % j for j in range(8)], ["b%d" % bk], bk, False, True, ext=mE, after=mA)
             vts(T.CL[:, 512 * hb:512 * hb + 512], B[bk][:], -15.0, 1.0, A.max, A.min, 512, ["b%d" % bk], ["CL%d" % hb], (bk,))
-        mm("ps0", [(B[6][:, 0:64], T.xId[:], Ko, 64)] +
-           [(B[6][:, 0:64], T.Id[:], T.CL[:, 64 * j:64 * j + 64], 64) for j in range(8)],
+        mm("ps0", [(B[6][:, 0:64], T.xId[:], Ko, 64)] + [(B[6][:, 0:64], T.Id[:], T.CL[:, 64 * j:64 * j + 64], 64) for j in range(8)],
            ["xId", "Id", "CL0"] + oR("K"), ["b6"], 6, True, False, ext=oE, after=oA)
         mm("ps1", [(B[6][:, 0:64], T.Id[:], T.CL[:, 64 * j:64 * j + 64], 64) for j in range(8, 16)], ["CL1"], ["b6"], 6, False, True)
         vtt(T.k1[:], B[6][:, 0:64], o[:, own:own + 64], A.mult, 64, ["b6"] + oR("M"), ["k1"], (6,), ext=oE, after=oA)
-        op({"V": (64 * par["sc"] + 50, lambda: V.tensor_tensor(T.KB[:, ko:ko + 320].indirect(T.spU[:]), T.k1[:], Ko, A.add))},
+        op("V", 64 * par["sc"] + 50, lambda: V.tensor_tensor(T.KB[:, ko:ko + 320].indirect(T.spU[:]), T.k1[:], Ko, A.add),
            ["spU", "k1"] + oR("K"), ["K%d" % tk, "Kd%d" % tk], (), kE, kA, nm="scK")
 
     for t in range(ST):
         last = t == ST - 1
         cur[0] = t
         ko = KBW * t
+        own = PKW * t
         K = T.KB[:, ko:ko + 256]
         z = T.zb[:, 256 * t:256 * t + 256]
         aF = T.aF[:, 16 * t:16 * t + 16]
         aR, zR = (["a0"], ["z0"]) if t == 0 else ([], [])
         aE, aA = ([], []) if t == 0 else ([("ra%d" % t, NE)], [snd["a", t - 1]])
         zE, zA = ([], []) if t == 0 else ([("rz%d" % t, NE)], [snd["z", t - 1]])
-        Xr = ["Xm", "Xd"]
-        vcp(T.aU[:], aF, 16, aR, ["aU"], ext=aE, after=aA)
-        gath(T.ra[:], T.P[:], T.aU[:], 256, ["P", "aU"], ["ra"], "V")
-        act(T.a5[:], aF, AF.Copy, 16, aR, ["a5"], scale=5.0, ext=aE, after=aA)
-        phrases("x", "ra", 0, par["xs"])
+        vts(T.aU[:], aF, AS, None, A.mult, None, 16, aR, ["aU"], ext=aE, after=aA)
+        gath("V", T.ra[:], T.P[:, 0:1024 * (t + 1)], T.aU[:], 256, ["P%d" % j for j in range(t + 1)] + ["aU"], ["ra"])
+        act(T.a5[:], aF, AF.Copy, 16, aR, ["a5"], scale=4.0 * AS, ext=aE, after=aA)
+        phrases("x", "ra", 0, par["xs"] if t else par["xs0"])
         if t > 0:
             patch(t - 1, t, False)
         Kt, Bt = "K%d" % t, "Bd%d" % t
         if not last:
             snd["K", t] = send("toK", [(1, T.KB[:, ko:ko + 576], T.KB[:, ko + KBW:ko + KBW + 576], "rK%d" % (t + 1))], [Kt, Bt, "Kd%d" % t], par["lat"] + 2500)
-        gath(T.rb[:], T.P[:], T.bU[:], 256, ["P", "bU"], ["rb"], "VS")
+        gath("S", T.rb[:], T.P[:, 0:1024], T.bU[:], 256, ["P0", "bU"], ["rb"])
         mm("pw", [(B[6][:, 256:512], T.Id[:], T.wc[:], 256), (B[6][:, 256:512], T.Id[:], K, 256)], ["Id", "wc", Kt], ["b6c"], 6, True, True)
         vcp(T.wo[:], B[6][:, 256:512], 256, ["b6c"], ["wo"], (6,))
         vts(T.rb16[:], T.rb[:], -2048.0, None, A.add, None, 256, ["rb"], ["rb16"], half=True)
         phrases("y", "rb", 4096, par["ys"])
-        parts = []
+        terms = []
         mm("pz", [(B[2][:, 0:256], T.Id[:], z, 256)], ["Id"] + zR, ["b2"], 2, True, True, zE, zA)
-        mm("kz", [(B[1][:, 128 * h:128 * h + 128], T.zb[:, 256 * t + 128 * h:256 * t + 128 * h + 128], T.ZC[:], 128) for h in range(2)], ["ZC"] + zR, ["b1", "b1s"], 1, True, False, zE, zA)
-        for c in range(0, KV, 2):
-            mm("kx%d" % c, [(B[1][:, 128 * h + j:128 * h + 128:16], T.XY[:, 2048 * h + j:2048 * h + 2048:16], T.Un32[:, 15:143:16], 8) for j in (c, c + 1) for h in range(2)],
-               ["Un32", "b1s"] + allx, ["kx%d" % c], None, False, False)
-            parts.append("kx%d" % c)
+        mm("kz", [(B[1][:, 128 * h:128 * h + 128], T.zb[:, 256 * t + 128 * h:256 * t + 128 * h + 128], T.ZC[:], 128) for h in range(2)],
+           ["ZC"] + zR, ["b1", "b1s"], 1, True, False, zE, zA)
+        for k in range(0, KV, 2):
+            mm("kx%d" % k, [(B[1][:, 128 * h + j:128 * h + 128:16], T.XY[:, 2048 * h + j:2048 * h + 2048:16], T.Un32[:, 15:143:16], 8) for j in (k, k + 1) for h in range(2)],
+               ["Un32", "b1s"] + allx, ["kx%d" % k], None, False, False)
+            terms.append("kx%d" % k)
         for k in range(0, 16, 2):
             if k < KV:
                 for j in (k, k + 1):
                     vtt(T.MX[:, 256 * j:256 * j + 256], T.XY[:, j:4096:16], B[2][:, 0:256], A.max, 256, allx + ["b2"], ["mx%d" % j], (2,))
             else:
                 bk = par["rows"][(k - KV) // 2 % len(par["rows"])]
-                mm("pm%d" % k, [m for j in (0, 1) for m in ((cols(bk, 256 * j, 256 * j + 256), T.nId[:], z, 256),
-                                                           (cols(bk, 256 * j, 256 * j + 256), T.Id[:], T.XY[:, k + j:4096:16], 256))],
+                mm("pm%d" % k, [(B[bk][:, 256 * j:256 * j + 256], w, r, 256) for j in (0, 1) for w, r in ((T.nId[:], z), (T.Id[:], T.XY[:, k + j:4096:16]))],
                    zR + allx + ["Id", "nId"], ["b%d" % bk, "b%db" % bk, "b%du" % bk], bk, True, True, zE, zA)
                 act(T.MX[:, 256 * k:256 * k + 512], B[bk][:], AF.Abs, 512, ["b%d" % bk, "b%db" % bk], ["mx%d" % k, "mx%d" % (k + 1)], (bk,), scale=0.5)
             mm("km%d" % k, [(B[1][:, 128 * h + j:128 * h + 128:16], T.MX[:, 256 * j + 128 * h:256 * j + 128 * h + 128], T.U64[:, 15:143:16], 8) for j in (k, k + 1) for h in range(2)],
                ["U64", "b1s", "mx%d" % k, "mx%d" % (k + 1)], ["km%d" % k], None, False, False)
-            parts.append("km%d" % k)
-        mm("kB", [(B[1][:, 128 * h:128 * h + 128], T.KB[:, ko + 128 * h:ko + 128 * h + 128], T.sId[:], 128) for h in range(2)], ["sId", Kt] + parts, ["b1"], 1, False, True)
-        vscan(T.kS[:], T.R1[:], B[1][:, 0:256], 0.0, A.add, A.min, 256, ["R1", "b1"], ["kS"], (1,))
+            terms.append("km%d" % k)
+        mm("kB", [(B[1][:, 128 * h:128 * h + 128], T.KB[:, ko + 128 * h:ko + 128 * h + 128], T.sId[:], 128) for h in range(2)], ["sId", Kt] + terms, ["b1"], 1, False, True)
+        vscan(T.kS[:], T.R1[:], B[1][:, 0:256], A.add, A.min, 256, ["R1", "b1"], ["kS"], (1,))
+        if not last:
+            dma("Y", T.P[:, 1024 * (t + 1):1024 * (t + 2)], T.P[:, 0:1024], ["P0", "mx14"], ["P%d" % (t + 1)], "cp%d" % t, 3000, "cp")
         k16 = T.kS[:, 15:256:16]
         vts(T.r16[:], k16, M32, M32, A.add, A.subtract, 16, ["kS"], ["r16"])
         vts(T.low[:], k16, M1, M1 + 1, A.add, A.subtract, 16, ["kS"], ["low"])
@@ -478,12 +428,9 @@ def build(g, core, T, topo, par):
         mm("pv", [(B[5][:, 256:288], T.tId[:], T.vD[:], 32)] + [(B[5][:, 256 + j:288:8], T.Id2[:, 128 - 16 * j:256 - 16 * j], T.SK[:, j:32:8], 4) for j in range(8)],
            ["SK", "Id2a", "Id2b", "tId", "vD"], ["b5v"], 5, True, True)
         vcp(T.vF[:], B[5][:, 256:288], 32, ["b5v"], ["vF"], (5,))
-        gath(T.vU[:], T.vF[:], T.skU[:, 2:4], 32, ["vF", "skU"], ["vU"], "V")
+        gath("V", T.vU[:], T.vF[:], T.skU[:, 2:4], 32, ["vF", "skU"], ["vU"])
         mm("pZ", [(B[3][0:16, 256 + 128 * h:384 + 128 * h], T.ZT[:, 16 + 16 * h:32 + 16 * h], T.Id[:], 128) for h in range(2)], ["ZT1", "ZT2", "Id"], ["b3u"], 3, True, True)
-        if par["zb"] == "S":
-            act(T.ZB[0:16], B[3][0:16, 256:512], AF.Copy, 256, ["b3u"], ["ZB"], (3,))
-        else:
-            vcp(T.ZB[0:16], B[3][0:16, 256:512], 256, ["b3u"], ["ZB"], (3,))
+        vcp(T.ZB[0:16], B[3][0:16, 256:512], 256, ["b3u"], ["ZB"], (3,))
         mm("pt", [(B[3][:, 0:256], T.I16[:], T.rb16[:], 256), (B[3][:, 0:256], T.WT[0:16, :], T.ZB[0:16], 256)], ["I16", "rb16", "WT", "ZB"], ["b3"], 3, True, True)
         vts(T.T16[:], B[3][:, 0:256], -2048.0, 2048.0, A.max, A.min, 256, ["b3"], ["T16"], (3,))
 
@@ -495,141 +442,103 @@ def build(g, core, T, topo, par):
         mm("pc", both(T.BO16[:], T.T16, 128), ["BO16", "T16"], ["b4"], 4, False, True)
         for pi, (w0, w1) in enumerate(spans):
             e0, n = 48 * w0, 32 * (w1 - w0)
-            vscan(T.cS[:, e0:e0 + n], T.R2[:, 0:n], B[4][:, e0:e0 + n], 0.0, A.add, A.min, n, ["R2", "b4"], ["cS%d" % pi], (4,))
+            vscan(T.cS[:, e0:e0 + n], T.R2[:, 0:n], B[4][:, e0:e0 + n], A.add, A.min, n, ["R2", "b4"], ["cS%d" % pi], (4,))
         act(T.cR[:], B[4][:, 0:384], AF.Copy, 384, ["b4"], ["cR"], (4,))
-        gtt(T.eq[:], T.cS[:], T.bcU[:, 48:72], T.cR[:], A.is_equal, 384, ["cS0", "cS1", "cSx", "cR", "bcU"], ["eq"])
-        if par["zd"] == "V":
-            mm("pd", [(B[1][:, 0:256], T.hId[:], z, 256), (B[1][:, 0:256], T.hId[:], T.XY[:, 0:4096:16], 256)],
-               ["hId"] + allx + zR, ["b1"], 1, True, True, zE, zA)
-            vts(T.ZW[:, 1:512:2], B[1][:, 0:256], M1, M1, A.add, A.subtract, 256, ["b1"], ["zd"], (1,))
-        gath(T.xw[:, 0:256], T.XY[:, 0:4096], T.vU[:, 0:16], 256, ["vU"] + allx, ["xk"], "VS")
-        for pi, cs in enumerate(par["parts"]):
-            a0, a1 = CH * min(cs), CH * (max(cs) + 1)
-            gath(T.xw[:, 256 + a0:256 + a1], T.XY[:, 4096 + 16 * a0:4096 + 16 * a1], T.vU[:, 16 + a0 // 16:16 + a1 // 16], a1 - a0,
-                 ["vU"] + ally[a0 // 16:a1 // 16], ["wk%d" % pi], "VS")
+        gtt(T.eq[:], T.cS[:], T.bcU[:, 32:56], T.cR[:], A.not_equal, 384, ["cS0", "cS1", "cSx0", "cSx1", "cR", "bcU"], ["eq"])
+        gath("S", T.xw[:, 0:256], T.XY[:, 0:4096], T.vU[:, 0:16], 256, ["vU"] + allx, ["xk"])
+        for pi, (w0, w1) in enumerate(spans):
+            a0, a1 = 32 * w0, 32 * w1
+            gath("S", T.xw[:, 256 + a0:256 + a1], T.XY[:, 4096 + 16 * a0:4096 + 16 * a1], T.vU[:, 16 + 2 * w0:16 + 2 * w1], a1 - a0,
+                 ["vU"] + ally[2 * w0:2 * w1], ["wk%d" % pi])
             mm("ph%d" % pi, [(B[6][:, a0:a1], T.hId[:], T.xw[:, a0:a1], a1 - a0), (B[6][:, a0:a1], T.hId[:], T.xw[:, 256 + a0:256 + a1], a1 - a0)],
                ["hId", "xk", "wk%d" % pi], ["b6"], 6, True, True)
             vts(T.half[:, a0:a1], B[6][:, a0:a1], M1, M1, A.add, A.subtract, a1 - a0, ["b6"], ["half%d" % pi], (6,))
         mm("pn", [(B[5][:, 0:256], T.Id[:], z, 256), (B[5][:, 0:256], T.nId[:], T.xw[:, 256:512], 256)], ["Id", "nId", "wk0", "wk1"] + zR, ["b5"], 5, True, True)
         act(T.ZW[:, 0:512:2], B[5][:, 0:256], AF.Abs, 256, ["b5"], ["zm"], (5,))
-        if par["pu"] == "P":
-            mm("pu", [(B[3][:, 256:272], DG("Wu", j), T.ZW[:, 2 * j:512:32], 16) for j in range(16)], ["Wu", "zm"], ["b3u"], 3, True, True)
-            vtt(T.amI[:], B[3][:, 256:272], T.a5[:], A.add, 16, ["b3u", "a5"], ["amI"], (3,))
-        else:
-            mm("pe", [(B[3][:, 256:512], T.tId[:], T.tri[:], 256)], ["tId", "tri"], ["b3u"], 3, True, False)
-            mm("pu", [(B[3][:, 256:512], T.Wu[:, 0:128], T.ZW[:, 0:512:2], 256)], ["Wu", "zm"], ["b3u"], 3, False, True)
-            vscan(T.uS[:], T.R2[:], B[3][:, 256:512], 0.0, A.add, A.min, 256, ["R2", "b3u"], ["uS"], (3,))
-            vtt(T.amI[:], T.uS[:, 15:256:16], T.a5[:], A.add, 16, ["uS", "a5"], ["amI"])
+        mm("pe", [(B[3][:, 256:512], T.tId[:], T.tri[:], 256)], ["tId", "tri"], ["b3u"], 3, True, False)
+        mm("pu", [(B[3][:, 256:512], T.Wu[:], T.ZW[:, 0:512:2], 256)], ["Wu", "zm"], ["b3u"], 3, False, True)
+        vscan(T.kS[:], T.R2[:], B[3][:, 256:512], A.add, A.min, 256, ["R2", "b3u"], ["kS"], (3,), nm="uS")
+        vtt(T.amI[:], T.kS[:, 15:256:16], T.a5[:], A.add, 16, ["kS", "a5"], ["amI"])
         vts(T.amJ[:], T.amI[:], 1023, None, A.bitwise_and, None, 16, ["amI"], ["amJ"])
-        vtt(T.da[:], aF, T.amJ[:], A.subtract, 16, ["aU", "amJ"], ["da"])
+        vts(T.da[:], T.amJ[:], 1.0 / AS, None, A.mult, None, 16, ["amJ"], ["da"])
 
-        own = PKW * t
-        blocks = []
-
-        def number(a0, a1, pi, R):
-            n = a1 - a0
-            mm("pq%d" % pi, [(B[1][:, 256 + a0:256 + a1], T.BOs[:], T.mis[:, a0:a1], n)], ["BOs"] + R, ["b1q"], 1, True, True)
-            act(T.dvS[:, a0:a1], B[1][:, 256 + a0:256 + a1], AF.Sign, n, ["b1q", "c14"], ["dvS%d" % pi], (1,), bias=col[:, 14:15])
-            vscan(T.pref[:, a0:a1], T.ones[:, a0:a1], T.dvS[:, a0:a1], T.pref[:, a0 - 1:a0] if pi else 0.0, A.add, A.add, n,
-                  ["ones", "dvS%d" % pi] + (["pref%d" % (pi - 1)] if pi else []), ["pref%d" % pi], half=True)
-            for j in range(4):
-                act(T.junk[:, 256 * j + a0:256 * j + a1], T.pref[:, a0:a1], AF.Sign, n, ["pref%d" % pi, "jC1"], ["junk%d_%d" % (pi, j), "acc%d_%d" % (pi, j)],
-                    bias=T.jC[:, 4 + j:5 + j], accum=T.acc[:, 4 * pi + j:4 * pi + j + 1])
-            if pi:
-                prev, pR = (T.acc[:, 0:4], ["acc0_%d" % j for j in range(4)]) if pi == 1 else (T.accS[:, 4 * pi - 4:4 * pi], ["sum%d" % (pi - 1)])
-                vtt(T.accS[:, 4 * pi:4 * pi + 4], T.acc[:, 4 * pi:4 * pi + 4], prev, A.add, 4, ["acc%d_%d" % (pi, j) for j in range(4)] + pR, ["sum%d" % pi])
-
-        NP = len(par["parts"])
-        miss = ["mis%d" % pi for pi in range(NP)]
-        nSs = ["nS%d" % pi for pi in range(NP)]
         for pi, cs in enumerate(par["parts"]):
-            bk, off, key = (0, 0, "b0") if pi % 2 == 0 else (2, 256, "b2b")
-            a0, a1 = CH * min(cs), CH * (max(cs) + 1)
-            n, nl, s = a1 - a0, (a1 - a0) // 16, "_%d" % pi
-            fresh = [True]
+            bk, off, key = ((0, 0, "b0"), (2, 256, "b2b"))[pi]
+            nb, s0, nk = ((7, 0, "b7"), (1, 256, "b1q"))[pi]
+            w0, w1 = spans[pi]
+            a0, a1, q0, q1, e0, e1 = 32 * w0, 32 * w1, 2 * w0, 2 * w1, 48 * w0, 48 * w1
+            n, n3, s = a1 - a0, e1 - e0, "_%d" % pi
             for c in cs:
-                lo, hi = 16 * CH * c, 16 * CH * (c + 1)
-                for j in range(NSUB):
-                    l0, l1 = CH * c + DCH * j, CH * c + DCH * (j + 1)
-                    gtt(T.DF[:, 16 * l0:16 * l1], T.XY[:, 4096 + 16 * l0:4096 + 16 * l1], T.wo[:, l0:l1], T.XY[:, 16 * l0:16 * l1], A.subtract, 16 * DCH,
-                        allx[l0 // 16:l1 // 16] + ally[l0 // 16:l1 // 16] + ["wo"], ["df%d_%d" % (c, j)])
-                dfs = ["df%d_%d" % (c, j) for j in range(NSUB)]
-                out = cols(bk, off + CH * c, off + CH * (c + 1))
-                if c in par["rv"]:
+                lo, hi, ns = 16 * CH * c, 16 * CH * (c + 1), par["subs"][c]
+                for j in range(ns):
+                    l0, l1 = CH * c + CH // ns * j, CH * c + CH // ns * (j + 1)
+                    gtt(T.DF[:, 16 * l0:16 * l1], T.XY[:, 4096 + lo:4096 + hi], T.wo[:, l0:l1], T.XY[:, 16 * l0:16 * l1], A.subtract, 16 * CH // ns,
+                        allx[l0 // 16:l1 // 16] + ally[4 * c:4 * c + 4] + ["wo"], ["df%d_%d" % (c, j)])
+                dfs = ["df%d_%d" % (c, j) for j in range(ns)]
+                out = B[bk][:, off + CH * c:off + CH * (c + 1)]
+                relu = c in par["rv"]
+                if relu:
                     for h in range(2):
                         mm("dl%d_%d" % (c, h), [(out, DG("Un32", k), T.DF[:, lo + k:hi:16], CH) for k in range(8 * h, 8 * h + 8)], ["Un32"] + dfs, [key], bk,
-                           fresh[0], False)
-                        fresh[0] = False
+                           c == cs[0] and h == 0, False)
                     vts(T.AB[:, lo:hi], T.DF[:, lo:hi], 0.0, None, A.max, None, 16 * CH, dfs, ["ab%d" % c], half=True)
                 else:
                     act(T.AB[:, lo:hi], T.DF[:, lo:hi], AF.Abs, 16 * CH, dfs, ["ab%d" % c], scale=0.5)
-                for gr in par["dg"]:
-                    if gr[-1] == c:
-                        l0, l1 = CH * gr[0], CH * (c + 1)
-                        for h in range(2):
-                            mm("da%d_%d" % (c, h), [(cols(bk, off + l0, off + l1), DG("U64", k), T.AB[:, 16 * l0 + k:16 * l1:16], l1 - l0) for k in range(8 * h, 8 * h + 8)],
-                               ["U64"] + ["ab%d" % j for j in gr], [key], bk, fresh[0], c == cs[-1] and h == 1)
-                            fresh[0] = False
-            nb, nk = (7, "b7") if pi % 2 == 0 else (0, "b0b")
-            w0, w1 = a0 // 32, a1 // 32
-            s0, n3, e0, e1 = 256 * pi, 48 * (w1 - w0), 48 * w0, 48 * w1
+                for h in range(2):
+                    mm("da%d_%d" % (c, h), [(out, DG("U64", k), T.AB[:, lo + k:hi:16], CH) for k in range(8 * h, 8 * h + 8)], ["U64", "ab%d" % c], [key], bk,
+                       c == cs[0] and h == 0 and not relu, c == cs[-1] and h == 1)
             mm("n0" + s, [(B[nb][:, s0:s0 + n3], T.Id[:], T.cmk[:, e0:e1], n3)], ["Id", "cmk" + s, "cmj" + s], [nk], nb, True, False)
-            act(T.mis[:, a0:a1], cols(bk, off + a0, off + a1), AF.Sign, n, [key, "nth"], [miss[pi]], (bk,), bias=T.nth[:, 0:1], scale=1.0 / 32)
+            act(T.mis[:, a0:a1], B[bk][:, off + a0:off + a1], AF.Sign, n, [key, "nth"], ["mis%d" % pi], (bk,), bias=T.nth[:, 0:1], scale=1.0 / 32)
             mm("n1" + s, [(B[nb][:, s0:s0 + n], T.BOs[:], T.mis[:, a0:a1], n)] +
                [(B[nb][:, s0 + n + 16 * j:s0 + n + 16 * j + 16], T.BOs[:], T.mis[:, a0 + 32 * j:a0 + 32 * j + 16], 16) for j in range(w1 - w0)],
-               ["BOs", miss[pi]], [nk], nb, False, True)
-            vscan(T.nS[:, a0:a1], T.R2[:, a0:a1], B[nb][:, s0:s0 + n], 0.0, A.add, A.min, n, ["R2", nk], [nSs[pi]], (nb,))
-            if pi == NP - 1:
-                vts(T.dl[:], T.nS[:, 15:256:16], 1.0, None, A.is_gt, None, 16, nSs, ["dl"])
-                vtt(T.t2[:], T.dl[:], T.da[:], A.mult, 16, ["dl", "da"], ["t2"])
+               ["BOs", "mis%d" % pi], [nk], nb, False, True)
+            vscan(T.nS[:, a0:a1], T.t01[:, a0:a1], B[nb][:, s0:s0 + n], A.mult, A.max, n, ["t01", nk], ["nS%d" % pi], (nb,))
+            if pi == 1:
+                vts(T.dl[:], T.nS[:, 15:256:16], 0.0, None, A.is_le, None, 16, ["nS0", "nS1"], ["dl"])
+                vtt(T.t2[:], T.nS[:, 15:256:16], T.da[:], A.min, 16, ["nS0", "nS1", "da"], ["t2"])
                 aS = T.aS[:, 16 * t:16 * t + 16]
-                vtt(aS, T.t2[:], T.amJ[:], A.add, 16, ["t2", "amJ"], ["aS%d" % t], nm="aS")
+                vtt(aS, T.t2[:], aF, A.add, 16, ["t2", "aU"], ["aS%d" % t], nm="aS")
                 if not last:
                     snd["a", t] = send("toa", [(1, aS, T.aF[:, 16 * t + 16:16 * t + 32], "ra%d" % (t + 1))], ["aS%d" % t], par["lat"])
                 else:
-                    dma("Y", T.ya[:], aS, ["aS%d" % t], [], "out", 2500, "oa")
-            vtt(T.cm[:, e0:e1], T.eq[:, e0:e1], B[nb][:, s0:s0 + n3], A.is_gt, n3, ["eq", nk], ["cm" + s], (nb,))
-            vscan(T.bS[:, e0:e1], T.R3[:, 0:n3], T.cm[:, e0:e1], 0.0, A.mult, A.add, n3, ["R3", "cm" + s], ["bS" + s])
-            q0, q1 = a0 // 16, a1 // 16
-            vts(T.f1[:, q0:q1:2], T.bS[:, e0 + 15:e0 + n:32], T.pw[:, 15:16], col[:, 12:13], A.not_equal, A.mult, nl, ["bS" + s, "pw", "c12"], ["f0" + s])
-            vts(T.f3[:, w0:w1], T.bS[:, e0 + 31:e0 + n:32], T.pw[:, 15:16], col[:, 13:14], A.not_equal, A.mult, nl, ["bS" + s, "pw", "c13"], ["f3" + s])
-            vts(T.f3[:, 8 + w0:8 + w1], T.bS[:, e0 + n + 15:e1:16], 0.0, col[:, 13:14], A.is_gt, A.mult, nl, ["bS" + s, "c13"], ["f4" + s])
-            vtt(T.f1[:, q0 + 1:q1:2], T.f3[:, w0:w1], T.f3[:, 8 + w0:8 + w1], A.max, nl, ["f3" + s, "f4" + s], ["f1" + s])
-            vtt(T.f2[:, q0:q1], T.f1[:, q0:q1], T.cS[:, e0 + 15:e0 + n:16], A.max, nl, ["f0" + s, "f1" + s, "cS%d" % pi], ["f2" + s])
-            vcp(T.offU[:, q0:q1], T.f2[:, q0:q1], nl, ["f2" + s], ["offU" + s])
-            blocks += [(w, s) for w in range(w0, w1)]
-            if par["split"]:
-                number(a0, a1, pi, [miss[pi]])
-            if not par["asc"] or pi == NP - 1:
-                for lh, s in sorted(blocks, reverse=True):
-                    scat(T.X[:], T.offU[:, 2 * lh:2 * lh + 2], T.half[:, 32 * lh:32 * lh + 32], 32, ["offU" + s, "half" + s[1:]], Xr, nm="sx%d" % lh)
-                blocks = []
-        if not par["split"]:
-            number(0, 256, 0, miss)
-        if par["zd"] == "S":
-            mm("pd", [(B[2][:, 0:256], T.hId[:], z, 256), (B[2][:, 0:256], T.hId[:], T.XY[:, 0:4096:16], 256)],
-               ["hId"] + allx + zR, ["b2"], 2, True, True, zE, zA)
-            act(T.kT[:], B[2][:, 0:256], AF.Copy, 256, ["b2"], ["kT"], (2,), bias=M1, nm="zc")
-            act(T.ZW[:, 1:512:2], T.kT[:], AF.Copy, 256, ["kT"], ["zd"], bias=-M1)
-        NJ = NP if par["split"] else 1
-        prl = "pref%d" % (NJ - 1)
-        act(T.pkS[:, own + 136:own + 144], T.pref[:, 248:256], AF.Copy, 8, [prl], ["pkA%d" % t], nm="pkA")
+                    cur[0] = ST
+                    vts(T.amI[:], aS, AS, None, A.mult, None, 16, ["aS%d" % t], ["amI"], nm="aI")
+                    vts(T.amJ[:], T.amI[:], 1023, None, A.bitwise_and, None, 16, ["amI"], ["amJ"], nm="aJ")
+                    vcp(T.a5[:], T.amJ[:], 16, ["amJ"], ["a5"], nm="aK")
+                    dma("Y", T.ya[:], T.a5[:], ["a5"], [], "out", 2500, "oa")
+                    cur[0] = t
+            vtt(T.cm[:, e0:e1], T.eq[:, e0:e1], B[nb][:, s0:s0 + n3], A.is_lt, n3, ["eq", nk], ["cm" + s], (nb,))
+            vscan(T.bS[:, e0:e1], T.R3[:, 0:n3], T.cm[:, e0:e1], A.mult, A.add, n3, ["R3", "cm" + s], ["bS" + s])
+            vts(T.f1[:, q0:q1:2], T.bS[:, e0 + 15:e0 + n:32], T.pw[:, 15:16], col[:, 12:13], A.not_equal, A.mult, 8, ["bS" + s, "pw", "c12"], ["f0" + s])
+            vts(T.f3[:, w0:w1], T.bS[:, e0 + 31:e0 + n:32], T.pw[:, 15:16], col[:, 13:14], A.not_equal, A.mult, 8, ["bS" + s, "pw", "c13"], ["f3" + s])
+            vts(T.f3[:, 8 + w0:8 + w1], T.bS[:, e0 + n + 15:e1:16], 0.0, col[:, 13:14], A.is_gt, A.mult, 8, ["bS" + s, "c13"], ["f4" + s])
+            vtt(T.f1[:, q0 + 1:q1:2], T.f3[:, w0:w1], T.f3[:, 8 + w0:8 + w1], A.max, 8, ["f3" + s, "f4" + s], ["f1" + s])
+            vtt(T.f2[:, q0:q1], T.f1[:, q0:q1], T.cS[:, e0 + 15:e0 + n:16], A.max, 16, ["f0" + s, "f1" + s, "cS%d" % pi], ["f2" + s])
+            vcp(T.offU[:, q0:q1], T.f2[:, q0:q1], 16, ["f2" + s], ["offU" + s])
+            for w in range(w1 - 1, w0 - 1, -1):
+                scat(T.X[:], T.offU[:, 2 * w:2 * w + 2], T.half[:, 32 * w:32 * w + 32], 32, ["offU" + s, "half%d" % pi], Xr, nm="sx%d" % w)
+        miss = ["mis0", "mis1"]
+        mm("pq", [(B[0][:, 256:512], T.BOs[:], T.mis[:, 0:256], 256)], ["BOs"] + miss, ["b0b"], 0, True, True)
+        act(T.dvS[:], B[0][:, 256:512], AF.Sign, 256, ["b0b", "c14"], ["dvS"], (0,), bias=col[:, 14:15], scale=-1.0)
+        vscan(T.pref[:], T.ones[:], T.dvS[:], A.add, A.add, 256, ["ones", "dvS"], ["pref"], half=True)
+        for j in range(4):
+            act(T.junk[:, 256 * j:256 * j + 256], T.pref[:], AF.Sign, 256, ["pref", "jC1"], ["junk%d" % j, "acc%d" % j], bias=T.jC[:, 4 + j:5 + j], accum=T.acc[:, j:j + 1])
+        mm("pd", [(B[2][:, 0:256], T.hId[:], z, 256), (B[2][:, 0:256], T.hId[:], T.XY[:, 0:4096:16], 256)], ["hId"] + allx + zR, ["b2"], 2, True, True, zE, zA)
+        act(T.kT[:], B[2][:, 0:256], AF.Copy, 256, ["b2"], ["kT"], (2,), bias=M1, nm="zc")
+        act(T.ZW[:, 1:512:2], T.kT[:], AF.Copy, 256, ["kT"], ["zd"], bias=-M1)
         src = T.pkS[:, own + 136:own + 144]
+        act(src, T.pref[:, 248:256], AF.Copy, 8, ["pref"], ["pkA%d" % t], nm="pkA")
         if not last:
             snd["A", t] = send("toA", [(2, src, T.pkA[:, 32 * t:32 * t + 8], "rA%d" % t)], ["pkA%d" % t], par["lat"])
         else:
             snd["A", t] = send("toA", [(1, src, T.pkA[:, 32 * t:32 * t + 8], "rA%d" % t), (3, src, T.pkA[:, 32 * t + 8:32 * t + 16], "rO%d" % t)], ["pkA%d" % t], par["lat"] + 600)
-        accs = ["acc%d_%d" % (NJ - 1, j) for j in range(4)] if NJ == 1 else ["sum%d" % (NJ - 1)]
-        acc = T.acc[:, 0:4] if NJ == 1 else T.accS[:, 4 * NJ - 4:4 * NJ]
-        vts(T.posU[:], acc, -0.5, 128.0, A.mult, A.add, 4, accs, ["posU"])
-        act(T.pkS[:, own + 128:own + 132], acc, AF.Copy, 4, accs, ["pkp%d" % t], bias=128.0, scale=-0.5, nm="pkp")
-        if not last:
-            gath(T.pkS[:, own + 64:own + 128], T.KB[:, ko:ko + 320], T.posU[:], 64, ["posU", Kt, "Kd%d" % t], ["pkK%d" % t], "VS", nm="pkK")
-        gath(T.pkS[:, own + 144:own + 208], T.KB[:, ko + 320:ko + 640], T.posU[:], 64, ["posU", Bt, "Be%d" % t], ["pkB%d" % t], "VS", nm="pkB")
+        accs = ["acc%d" % j for j in range(4)]
+        vts(T.posU[:], T.acc[:], -0.5, 128.0, A.mult, A.add, 4, accs, ["posU"])
+        act(T.pkS[:, own + 128:own + 132], T.acc[:], AF.Copy, 4, accs, ["pkp%d" % t], bias=128.0, scale=-0.5, nm="pkp")
+        gath(par["pk"][0], T.pkS[:, own + 64:own + 128], T.KB[:, ko:ko + 320], T.posU[:], 64, ["posU", Kt, "Kd%d" % t], ["pkK%d" % t], nm="pkK")
+        gath(par["pk"][1], T.pkS[:, own + 144:own + 208], T.KB[:, ko + 320:ko + 640], T.posU[:], 64, ["posU", Bt, "Be%d" % t], ["pkB%d" % t], nm="pkB")
         act(T.pkS[:, own + 208:own + 272], T.KB[:, ko:ko + 320].indirect(T.posU[:]), AF.Identity, 64, ["posU", Kt, "Kd%d" % t, "c15"], ["pkL%d" % t],
             bias=col[:, 15:16], gather=True, nm="pkL")
-        if last:
-            gath(T.pkS[:, own + 64:own + 128], T.KB[:, ko:ko + 320], T.posU[:], 64, ["posU", Kt, "Kd%d" % t], ["pkK%d" % t], "VS", nm="pkK")
         act(T.pkS[:, own:own + 64], T.mis[:].indirect(T.posU[:]), AF.Copy, 64, ["posU", "misd"] + miss, ["pkM%d" % t], bias=0.5, scale=0.5, gather=True, nm="pkM")
         sO, sM = T.pkS[:, own:own + 144], T.pkS[:, own + 128:own + 272]
         pkR = ["pk%s%d" % (a, t) for a in ("BLpA" if last else "KMBLpA")]
@@ -640,16 +549,14 @@ def build(g, core, T, topo, par):
         vtt(T.s2[:], T.s1[:], T.dl[:], A.add, 16, ["s1", "dl"], ["s2"])
         vcp(T.slU[:], T.s2[:], 16, ["s2"], ["slU"])
         zS = T.zS[:, 256 * t:256 * t + 256]
-        gath(zS, T.ZW[:], T.slU[:], 256, ["slU", "zm", "zd"], ["zS%d" % t], "VS", nm="zS")
+        gath("S", zS, T.ZW[:], T.slU[:], 256, ["slU", "zm", "zd"], ["zS%d" % t], nm="zS")
         if not last:
             snd["z", t] = send("toz", [(1, zS, T.zb[:, 256 * t + 256:256 * t + 512], "rz%d" % (t + 1))], ["zS%d" % t], par["lat"] + 600)
+            vts(T.AI[:, 0:1], T.pref[:, 255:256], 0.5, None, A.mult, None, 1, ["pref"], ["AI"])
+            vts(T.AI[:, 1:2], T.AI[:, 0:1], 31, None, A.bitwise_and, None, 1, ["AI"], ["AJ"])
+            vtt(T.nth[:, 0:1], T.thF[:, 0:1], T.AI[:, 1:2], A.subtract, 1, ["thF", "AJ"], ["nth"])
         else:
             dma("Y", T.yz[:], zS, ["zS%d" % t], [], "out", 2500, "oz")
-        if not last:
-            vts(T.AI[:, 0:1], T.pref[:, 255:256], 0.5, None, A.mult, None, 1, [prl], ["AI"])
-            vts(T.AJ[:, 0:1], T.AI[:, 0:1], 31, None, A.bitwise_and, None, 1, ["AI"], ["AJ"])
-            vtt(T.nth[:, 0:1], T.thF[:, 0:1], T.AJ[:, 0:1], A.subtract, 1, ["thF", "AJ"], ["nth"])
-        else:
             dma("Y", T.yx[:], T.X[:, 0:4096], Xr, [], "out", 7500, "ox")
             cur[0] = ST
             patch(t, t, True)
@@ -659,28 +566,19 @@ def build(g, core, T, topo, par):
 
 
 def first_calls(ops, par):
-    order, eng = greedy(ops, par)
-    later = set(x[1:] for q in par["queues"].values() for x in q if x[0] == "+")
-    return {e: [i for i in order if eng[i] == e and (ops[i]["t"] < 0 or ops[i]["t"] == 0 and ops[i]["nm"] not in later)] for e in "VSPGY"}, eng
-
-
-def greedy(ops, par):
     n, hop = len(ops), par["hop"]
-    eng = [list(o["alts"])[-1] for o in ops]
-    cost = [o["alts"][e][0] for o, e in zip(ops, eng)]
+    eng = [o["e"] for o in ops]
+    cost = [o["alts"][o["e"]][0] for o in ops]
     succ = [[] for _ in range(n)]
     for i, o in enumerate(ops):
         for d in o["deps"]:
             succ[d].append(i)
-    if "queues" in par:
-        place = {nm.lstrip("+"): 900.0 * j / len(q) + (1000 if nm[0] == "+" else 0) for q in par["queues"].values() for j, nm in enumerate(q)}
-    else:
-        place = {nm.lstrip("+"): j + (1000 if nm[0] == "+" else 0) for j, nm in enumerate(par["order"])}
+    place = {nm.lstrip("+"): 900.0 * j / len(q) + (1000 if nm[0] == "+" else 0) for q in par["queues"].values() for j, nm in enumerate(q)}
     pr = [0.0] * n
     for i in range(n - 1, -1, -1):
         o = ops[i]
         if o["t"] == 0 and o["nm"] in par["first"]:
-            pr[i] = 5000.0 - place[o["nm"]]
+            pr[i] = 5000.0 - par["first"].index(o["nm"])
         elif o["t"] >= 0 and o["nm"] in place:
             pr[i] = -1000.0 * o["t"] - place[o["nm"]]
         elif o["nm"] == "dma":
@@ -708,12 +606,11 @@ def greedy(ops, par):
             if left[j] == 0:
                 rd[j] = max(en[d] + (0 if eng[d] == eng[j] and ops[d]["lat"] == 0 and (k == "bank" or eng[j] == "P") else hop) for d, k in ops[j]["deps"].items())
                 cand[eng[j]].append(j)
-    return order, eng
+    later = set(x[1:] for q in par["queues"].values() for x in q if x[0] == "+")
+    return {e: [i for i in order if eng[i] == e and (ops[i]["t"] < 0 or ops[i]["t"] == 0 and ops[i]["nm"] not in later)] for e in "VSPGY"}, eng
 
 
 def schedule(ops, par):
-    if "queues" not in par:
-        return greedy(ops, par)
     seq, eng = first_calls(ops, par)
     at = {}
     for i, o in enumerate(ops):
@@ -721,7 +618,11 @@ def schedule(ops, par):
     for e in seq:
         for t in range(1, ST + 1):
             for x in par["queues"][e]:
-                seq[e] += at.get((x[1:], t - 1, e) if x[0] == "+" else (x, t, e), [])
+                k = (x[1:], t - 1, e) if x[0] == "+" else (x, t, e)
+                if k[1] < ST - 1 or k[1] == ST - 1 and ("+" + k[0]) not in par["last"][e]:
+                    seq[e] += at.get(k, [])
+        for x in par["last"][e]:
+            seq[e] += at[(x[1:], ST - 1, e) if x[0] == "+" else (x, ST, e)]
     done, order, pos = set(), [], dict.fromkeys(seq, 0)
     while len(order) < len(ops):
         before = len(order)
@@ -734,63 +635,11 @@ def schedule(ops, par):
     return order, eng
 
 
-def heft(ops, par, some):
-    n, hop = len(ops), par["hop"]
-    some = set(some)
-    succ = [[] for _ in range(n)]
-    for i, o in enumerate(ops):
-        for d in o["deps"]:
-            succ[d].append(i)
-    pr = [0.0] * n
-    place = {}
-    for j, nm in enumerate(par.get("order", [])):
-        place[nm.lstrip("+")] = j + (1000 if nm[0] == "+" else 0)
-    for i in range(n - 1, -1, -1):
-        o = ops[i]
-        if o["t"] >= 0 and o["nm"] in place:
-            pr[i] = -1000.0 * o["t"] - place[o["nm"]]
-        else:
-            pr[i] = max([pr[s] for s in succ[i]] + [-1e9 if place else 0]) + (1e-7 if place else 1) * (min(a[0] for a in o["alts"].values()) + o["lat"] + hop)
-        if o["nm"] == "dma":
-            pr[i] = 1e9 - i
-    succ = [[j for j in s if j in some] for s in succ]
-    eng, st, en = [None] * n, [0] * n, [0] * n
-    busy = {}
-    left = [len(o["deps"]) for o in ops]
-    ready = [i for i in some if left[i] == 0]
-    while ready:
-        i = max(ready, key=lambda j: (pr[j], -j))
-        ready.remove(i)
-        for j in succ[i]:
-            left[j] -= 1
-            if left[j] == 0:
-                ready.append(j)
-        best = None
-        for e, (c, f) in ops[i]["alts"].items():
-            s = 0
-            for d, k in ops[i]["deps"].items():
-                s = max(s, en[d] + (0 if (eng[d] == e and ops[d]["lat"] == 0 and (k == "bank" or e == "P")) else hop))
-            b = busy.setdefault(e, [])
-            lo = len(b)
-            while lo > 0 and b[lo - 1][1] > s:
-                lo -= 1
-            while lo < len(b) and b[lo][0] < s + c:
-                s = max(s, b[lo][1])
-                lo += 1
-            if best is None or s + c < best[0]:
-                best = (s + c, s, e, lo)
-        fin, s, e, lo = best
-        busy[e].insert(lo, (s, fin))
-        eng[i], st[i], en[i] = e, s, fin + ops[i]["lat"]
-    return sorted(some, key=lambda c: (st[c], c)), eng
-
-
 def rank_program(g, core, T, topo):
     if T.rank_of(core) is None:
         return
-    par = PAR
-    ops, nsent = build(g, core, T, topo, par)
-    order, eng = schedule(ops, par)
+    ops, nsent = build(g, core, T, topo, PAR)
+    order, eng = schedule(ops, PAR)
     Q = {"V": g.vector, "S": g.scalar, "P": g.tensor, "G": g, "Y": g.sync}
     cnt = {"out": 0}
     mark = {}

from concourse.bass import DstId, RemoteDMATransfer
from concourse.mybir import AluOpType, ActivationFunctionType

ST = 5
NR = 4
KBW = 640
PKW = 272
BF, F32, I32, U16, F16 = "bfloat16", "float32", "int32", "uint16", "float16"

SCRATCH = {}
for _n, _c, _d in [
    ("X", 4128, BF), ("P", 1024 * ST, I32), ("XY", 8192, BF), ("DF", 4096, BF), ("AB", 4096, BF), ("MX", 4096, BF),
    ("KB", KBW * ST, BF), ("aU", 16, U16), ("aS", 16 * ST, F32), ("zb", 256 * ST, BF), ("zS", 256 * ST, BF),
    ("pkS", PKW * ST, BF), ("pkO", PKW * ST, BF), ("pkM", PKW * ST, BF), ("pkA", 32 * ST, BF),
    ("avI", 16, I32), ("bvI", 16, I32), ("kcI", 256, I32), ("thI", 4, I32),
    ("ra", 256, U16), ("rb", 256, U16), ("rb16", 256, F16), ("wo", 256, U16), ("bU", 16, U16), ("bF", 16, F32),
    ("kT", 256, F32), ("kS", 256, F32), ("r16", 16, F32), ("low", 16, F32), ("ZT", 48, BF), ("SK", 32, BF),
    ("vF", 32, F32), ("vU", 32, U16), ("xw", 512, BF), ("cS", 384, F32), ("cR", 384, F32),
    ("eq", 384, BF), ("ZW", 512, BF), ("half", 256, BF), ("a5", 16, F32), ("aF", 16 * ST, F32),
    ("amI", 16, I32), ("amJ", 16, I32), ("da", 16, F32), ("mis", 272, BF), ("dvS", 256, BF), ("pref", 256, BF),
    ("cm", 384, BF), ("bS", 384, F32), ("nS", 256, F32), ("f1", 16, F32), ("f2", 16, F32), ("f3", 16, F32), ("offU", 16, U16),
    ("dl", 16, F32), ("t2", 16, F32), ("s1", 16, F32), ("s2", 16, F32), ("slU", 16, U16),
    ("acc", 4, F32), ("posU", 4, U16), ("junk", 1024, BF), ("AI", 4, I32), ("nth", 4, F32), ("thF", 4, F32),
    ("n1", 4, F32), ("n2", 4, F32), ("g1", 4, F32), ("g2", 4, F32), ("g3", 4, F32), ("spU", 4, U16),
    ("CL", 1024, BF), ("k1", 64, BF), ("hJ", 32, I32), ("hl", 32, BF), ("hm", 512, BF),
    ("io", 4, I32), ("ia", 16, I32), ("col", 20, F32), ("ones", 256, BF), ("Id", 128, BF), ("Id2", 256, BF), ("nId", 128, BF),
    ("hId", 128, F16), ("sId", 128, BF), ("xId", 128, BF), ("tId", 128, BF), ("mId", 128, BF), ("I16", 128, F16),
    ("BO", 128, BF), ("BO16", 128, F16), ("BOs", 128, BF), ("ZC", 128, BF), ("Wu", 128, BF), ("WT", 128, BF), ("WC", 128, BF),
    ("U64", 144, BF), ("Un32", 144, BF), ("SEL", 2048, BF), ("tri", 256, BF), ("t01", 256, BF), ("cmk", 384, BF),
    ("R1", 256, BF), ("R2", 256, BF), ("R3", 384, BF), ("dg", 256, BF), ("wc", 256, BF), ("tI", 384, F32), ("tJ", 160, F32),
    ("vC", 32, F32), ("vD", 32, F16), ("skU", 4, U16), ("skW", 32, BF), ("lC", 16, F32), ("bcF", 72, F32), ("bcU", 56, U16),
    ("jC", 12, F32), ("pw", 16, F32),
]:
    SCRATCH[_n] = ("sbuf", [128, _c], _d)
for _n, _d in (("ZB", BF), ("T16", F16)):
    SCRATCH[_n] = ("sbuf", [128, 8, 32], _d)
for _b in range(8):
    SCRATCH["B%d" % _b] = ("psum", [128, 512], F32)

SEMAPHORES = ["sV", "sS", "sP", "sG", "sent", "out"] + ["ld%d" % i for i in range(8)]
for _t in range(ST):
    SEMAPHORES += ["rK%d" % _t, "ra%d" % _t, "rz%d" % _t, "rO%d" % _t, "rM%d" % _t, "rA%d" % _t, "cp%d" % _t]

PAR = {
    "g": 1.3, "sc": 3.15, "pe": 0.5, "hop": 200, "rem": 540, "lat": 2400, "slack": 200.0, "near": 300.0,
    "parts": ((3, 2, 1), (0,)),
    "kv": 8, "rows": (0, 7, 3, 4),
    "rv": (3, 0), "subs": (2, 4, 2, 1),
    "xs": ((0, 2, "V"), (2, 2, "V"), (4, 12, "S")),
    "xs0": ((0, 2, "V"), (2, 6, "V"), (8, 8, "S")),
    "ys": ((12, 4, "S"), (8, 4, "S"), (4, 4, "S"), (0, 4, "S")),
    "pk": "SS",
    "first": ("aU", "ra", "rb", "x0", "x2", "x8"),
}
STEP = {
    "V": "+AI aU +sx1 ra +sx0 n1 x0 x2 n2 g1 g2 g3 spU scB CL0 CL1 bU +AJ mx0 mx1 k1 scK mx2 mx3 mx4 wo mx5 mx6 df3_0 +nth mx7 df2_0 ab3 df2_1 "
         "kS rb16 low r16 ZT1 ZT0 df1_3 SK ZB df1_1 vF df1_0 vU df1_2 T16 df0_0 df0_1 cS0 cS1 ab0 uS amI eq amJ nS0 da cm_0 nS1 pref t2 bS_0 cm_1 aS "
         "f3_0 f4_0 f0_0 f1_0 half0 f2_0 bS_1 dl offU_0 posU f0_1 sx7 f4_1 half1 f3_1 sx6 f1_1 sx5 f2_1 sx4 s2 offU_1 sx3 slU sx2",
    "S": "+zc +zd +zS x4 rb a5 y12 y8 mx8 mx12 mx14 mx10 y4 y0 ab2 wk0 wk1 ab1 zm cR xk mis0 mis1 dvS junk1 junk0 junk2 junk3 pkA pkp pkB pkL pkK pkM",
    "P": "po0 pc0 po1 pc1 pz pb ps0 ps1 kz pm8 pw pm12 kx6 pm14 kx0 pm10 km2 km0 kx2 km8 km6 km4 km14 kx4 km12 km10 kB dl3_0 dl3_1 da3_0 "
         "pZ pv n0_0 da3_1 pt pA da2_0 pc da2_1 n0_1 pn pe da1_0 da1_1 pu dl0_0 dl0_1 da0_0 da0_1 n1_0 pq n1_1 pd ph0 ph1",
    "G": "+toa +toA +toP +toz toK",
    "Y": "+oz cp ox",
}
LAST = {"V": "aI n1 aJ aK n2 g1 g2 CL0 g3 spU CL1 scB k1 scK", "P": "po0 po1 pc0 pc1 ps0 ps1 pb", "G": "", "Y": "oa",
        "S": "+pkA +junk1 +junk0 +junk2 +junk3 +pkp +pkB +pkL +pkK +pkM +zc +zd +zS bF ob ok"}
PAR["queues"] = {e: s.split() for e, s in STEP.items()}
PAR["last"] = {e: s.split() for e, s in LAST.items()}
NCH = 4
CH = 256 // NCH
HALF = 0.5 - 2.0 ** -11
AS = 16384.0
A = AluOpType
AF = ActivationFunctionType


def build(g, core, T, topo, par):
    rank = T.rank_of(core)
    ops = []
    cur = [-1]
    last_w, readers, bank_last = {}, {}, {}
    V, S, PE, SY = g.vector, g.scalar, g.tensor, g.sync

    def op(e, cost, f, reads, writes, banks=(), ext=(), after=(), lat=0, sem=None, semn=1, nm=None):
        i = len(ops)
        deps = {}
        for k in reads:
            if k in last_w:
                deps[last_w[k]] = "raw"
        for k in writes:
            if k in last_w:
                deps.setdefault(last_w[k], "ww")
            for r in readers.get(k, ()):
                deps.setdefault(r, "ww")
        for b in banks:
            for r in bank_last.get(b, ()):
                deps.setdefault(r, "bank")
        for a in after:
            deps.setdefault(a, "far")
        for k in reads:
            readers.setdefault(k, []).append(i)
        for k in writes:
            last_w[k] = i
            readers[k] = []
        for b in banks:
            prev = bank_last.get(b, [])
            bank_last[b] = prev + [i] if prev and ops[prev[-1]]["e"] == e else [i]
        deps.pop(i, None)
        ops.append({"e": e, "alts": {e: (cost, f)}, "deps": deps, "ext": list(ext), "lat": lat, "sem": sem, "semn": semn, "nm": nm or writes[0], "t": cur[0]})
        return i

    def cv(n, half=False):
        return max(64, n * (0.5 if half else 1.0))

    def vts(out, in0, s1, s2, o0, o1, n, R, W, banks=(), half=False, ext=(), after=(), nm=None):
        if cur[0] < 0 and o0 == A.mult and W[0] not in ("I16", "BO16", "hId") and (o1 is None or (o1 == A.add and isinstance(s2, float))):
            return op("S", cv(n) + 20, lambda: S.activation(out, in0, AF.Copy, bias=s2 or 0.0, scale=s1), R, W, nm=nm)
        if o1 is None:
            return op("V", cv(n, half), lambda: V.tensor_scalar(out, in0, s1, None, o0), R, W, banks, ext, after, nm=nm)
        return op("V", cv(n, half), lambda: V.tensor_scalar(out, in0, s1, s2, o0, o1), R, W, banks, ext, after, nm=nm)

    def vtt(out, in0, in1, o, n, R, W, banks=(), ext=(), after=(), nm=None):
        return op("V", cv(n if banks else 2 * n), lambda: V.tensor_tensor(out, in0, in1, o), R, W, banks, ext, after, nm=nm)

    def vcp(out, in_, n, R, W, banks=(), ext=(), after=(), nm=None):
        return op("V", cv(n), lambda: V.tensor_copy(out, in_), R, W, banks, ext, after, nm=nm)

    def vscan(out, d0, d1, o0, o1, n, R, W, banks=(), half=False, nm=None):
        return op("V", cv(n, half), lambda: V.tensor_tensor_scan(out, d0, d1, 0.0, o0, o1), R, W, banks, nm=nm)

    def fill(ap, val, n, W):
        return op("S", cv(n) + 20, lambda: S.activation(ap, T.ones[:, 0:n], AF.Copy, scale=val), ["ones"], W)

    def act(out, in_, f, n, R, W, banks=(), bias=None, scale=None, accum=None, gather=False, ext=(), after=(), nm=None):
        kw = {}
        if bias is not None:
            kw["bias"] = bias
        if scale is not None:
            kw["scale"] = scale
        if accum is not None:
            kw["accum_out"] = accum
        c = n * par["g"] + 65 if gather else cv(n) + 20
        return op("S", c, lambda: S.activation(out, in_, f, **kw), R, W, banks, ext, after, nm=nm)

    def gath(e, out, win, off, n, R, W, nm=None):
        if e == "V":
            return op("V", n * par["g"] + 50, lambda: V.tensor_copy(out, win.indirect(off)), R, W, nm=nm)
        return op("S", n * par["g"] + 65, lambda: S.activation(out, win.indirect(off), AF.Copy), R, W, nm=nm)

    def gtt(out, win, off, in1, o, n, R, W):
        return op("V", n * par["g"] + 50, lambda: V.tensor_tensor(out, win.indirect(off), in1, o), R, W)

    def scat(win, off, in_, n, R, W, ext=(), after=(), nm=None):
        return op("V", n * par["sc"] + 50, lambda: V.tensor_copy(win.indirect(off), in_), R, W, (), ext, after, nm=nm)

    def mm(nm, lst, R, W, bank, start, stop, ext=(), after=()):
        def f():
            r = None
            for j, m in enumerate(lst):
                r = PE.matmul(m[0], m[1], m[2], start and j == 0, stop and j == len(lst) - 1)
            return r
        return op("P", sum(max(64, m[3]) for m in lst) * par["pe"], f, R, W, () if bank is None else (bank,), ext, after, nm=nm)

    def dma(q, out, in_, R, W, sem, lat, nm="dma"):
        e = {"Y": SY, "S": S}[q]
        return op(q, 60, lambda: e.dma_start(out, in_), R, W, lat=lat, sem=sem, semn=16, nm=nm)

    nsent = [0]

    def send(nm, items, R, lat):
        def f():
            if len(items) == 1:
                o, src, dst, sem = items[0]
                d = T.cores[(rank + o) % NR]
                rid, pid, _ = topo.addr(d)
                return g.remote_dma(dst, src, T.sem[sem], T.sem.sent, pid, rid, topo.mask(core, d))
            tr = []
            for j, (o, src, dst, sem) in enumerate(items):
                d = T.cores[(rank + o) % NR]
                rid, pid, _ = topo.addr(d)
                en = topo.engines(core, d)
                per = len(en) // len(items)
                m = 0
                for e in en[j * per:(j + 1) * per]:
                    m |= 1 << e
                tr.append(RemoteDMATransfer(dst_ids=[DstId(rid=rid, pnc=pid)], dma_engine_mask=m, remote_sem=T.sem[sem], src=src, dst=dst))
            return g.remote_dma_fused(tr, local_sem=T.sem.sent)
        nsent[0] += NE
        return op("G", par["rem"], f, R, [], lat=lat, sem="none", nm=nm)

    NE = len(topo.engines(core, T.cores[(rank + 1) % NR]))
    B = [T["B%d" % i] for i in range(8)]
    allx = ["x%d" % c for c in range(16)]
    ally = ["y%d" % c for c in range(16)]
    Xr = ["Xm", "Xd"]

    def phrases(nm, lst, base, pieces):
        for b0, nb, e in pieces:
            gath(e, T.XY[:, base + 256 * b0:base + 256 * (b0 + nb)], T.X[:, 0:4096], T[lst][:, 16 * b0:16 * (b0 + nb)], 256 * nb, [lst] + Xr,
                 ["%s%d" % (nm, b) for b in range(b0, b0 + nb)])

    dma("Y", T.avI[:], T.av[:], [], ["avI"], "ld0", 2500)
    dma("Y", T.bvI[:], T.bv[:], [], ["bvI"], "ld3", 2500)
    dma("Y", T.P[:, 0:1024], T.rp[:], [], ["P0"], "ld1", 4500)
    dma("S", T.X[:, 0:4096], T.ph[:], [], ["Xm"], "ld2", 5500)
    dma("Y", T.kcI[:], T.kc[:], [], ["kcI"], "ld4", 5500)
    dma("Y", T.zb[:, 0:256], T.zs[:], [], ["z0"], "ld5", 5500)
    op("G", 300, lambda: g.dma_start(T.thI[:, 0:1], T.th[:], allow_slow_non_contiguous=True), [], ["thI"], lat=4000, sem="ld6", semn=16)

    def iota(out, pat, base, cm, n, W, fl=True):
        if fl:
            return op("G", 160 + 2 * n, lambda: g.iota(out, pat, base, cm, allow_small_or_imprecise_dtypes=True), [], W)
        return op("G", 160 + 2 * n, lambda: g.iota(out, pat, base, cm), [], W)

    col, p_ = T.col, T["io"][:, 0:1]
    op("V", 128, lambda: V.memset(T.ones[:], 1.0), [], ["ones"])
    iota(p_, [[0, 1]], 0, 1, 1, ["io"], False)
    iota(T.tJ[:], [[1, 160]], -16, -1, 160, ["tJ"])
    iota(T.tI[:], [[0, 24], [1, 16]], 0, 0, 384, ["tI"])
    vts(T.ia[:, 0:1], p_, 15, None, A.bitwise_and, None, 1, ["io"], ["ia0"])
    vcp(col[:, 0:1], T.ia[:, 0:1], 1, ["ia0"], ["c0"])
    r_ = col[:, 0:1]
    vts(col[:, 2:3], r_, -1.0, -1.0, A.mult, A.add, 1, ["c0"], ["c2"])
    vts(T.U64[:], T.tJ[:, 0:144], col[:, 2:3], 64.0, A.is_equal, A.mult, 144, ["tJ", "c2"], ["U64"])
    vts(T.Un32[:], T.U64[:], -0.5, None, A.mult, None, 144, ["U64"], ["Un32"], half=True)
    vts(T.Id[:], T.tJ[:, 16:144], 0.0, None, A.is_equal, None, 128, ["tJ"], ["Id"])
    for nm, w in (("nId", -1.0), ("hId", HALF), ("sId", 0.03125), ("xId", 15.0), ("tId", 16.0), ("mId", -16.0), ("I16", 1.0)):
        vts(T[nm][:], T.Id[:], w, None, A.mult, None, 128, ["Id"], [nm], half=True)

    def DG(U, k):
        return T[U][:, 15 - k:143 - k]
    vts(T.kS[:, 0:128], T.tJ[:, 16:144], r_, -7.5, A.add, A.add, 128, ["tJ", "c0"], ["kS"])
    vtt(T.cR[:, 0:128], T.kS[:, 0:128], T.kS[:, 0:128], A.mult, 128, ["kS"], ["cR"])
    vts(T.BO[:], T.cR[:, 0:128], 60.0, None, A.is_lt, None, 128, ["cR"], ["BO"])
    vts(T.BO16[:], T.BO[:], 1.0, None, A.mult, None, 128, ["BO"], ["BO16"], half=True)
    vts(T.BOs[:], T.BO[:], -0.0625, None, A.mult, None, 128, ["BO"], ["BOs"], half=True)
    KV = par["kv"]
    vts(T.kT[:, 0:128], T.tI[:, 0:128], float(KV), -32.0, A.is_lt, A.mult, 128, ["tI"], ["kT"])
    vtt(T.ZC[:], T.kT[:, 0:128], T.BO[:], A.mult, 128, ["kT", "BO"], ["ZC"])
    vts(col[:, 3:4], r_, 2.0, 1.0, A.mult, A.add, 1, ["c0"], ["c3"])
    vts(T.Wu[:], T.BO[:], col[:, 3:4], None, A.mult, None, 128, ["BO", "c3"], ["Wu"], half=True)
    iota(T.nS[:, 0:128], [[2, 8], [0, 16]], 0, -1, 128, ["nS0"])
    vts(T.nS[:, 128:256], T.nS[:, 0:128], 0.0, 131072.0, A.is_equal, A.mult, 128, ["nS0"], ["nS1"])
    vts(col[:, 5:6], p_, 1.0, 4096.0, A.is_equal, A.mult, 1, ["io"], ["c5"])
    vts(col[:, 6:7], col[:, 5:6], -39.0, None, A.mult, None, 1, ["c5"], ["c6"])
    vts(T.WC[:], T.nS[:, 128:256], col[:, 6:7], None, A.add, None, 128, ["nS1", "c6"], ["WC"])
    vts(T.kS[:, 128:256], T.tI[:, 0:128], 32.0, col[:, 5:6], A.add, A.mult, 128, ["tI", "c5"], ["kT2"])
    vtt(T.WT[:], T.kS[:, 128:256], T.nS[:, 128:256], A.subtract, 128, ["kT2", "kS", "nS1"], ["WT"])
    vts(T.tri[:], T.tI[:, 0:256], r_, 8192.0, A.is_gt, A.mult, 256, ["tI", "c0"], ["tri"])
    vts(T.t01[:], T.tri[:], 1.0 / 8192, None, A.mult, None, 256, ["tri"], ["t01"], half=True)
    spans = [(2 * min(cs), 2 * max(cs) + 2) for cs in par["parts"]]
    for pi, (w0, w1) in enumerate(spans):
        vts(T.cmk[:, 48 * w0:16 * w0 + 32 * w1], T.t01[:, 0:32 * (w1 - w0)], -15.0, -0.1875, A.mult, A.add, 256, ["t01"], ["cmk_%d" % pi], half=True)
        fill(T.cmk[:, 16 * w0 + 32 * w1:48 * w1], -0.1875, 16 * (w1 - w0), ["cmj_%d" % pi])
        fill(T.cS[:, 16 * w0 + 32 * w1:48 * w1], 0.0, 16 * (w1 - w0), ["cSx%d" % pi])
    vts(T.R2[:], T.t01[:], -1048576.0, 1048576.0, A.mult, A.add, 256, ["t01"], ["R2"])
    vts(T.bS[:, 0:256], T.tI[:, 0:256], 0.0, 1048576.0, A.is_equal, A.mult, 256, ["tI"], ["bS_0", "bS_1"])
    vts(T.R1[:], T.bS[:, 0:256], 1.0, -1.0, A.mult, A.add, 256, ["bS_0", "bS_1"], ["R1"])
    vts(T.R3[:], T.tI[:], 0.0, 2.0, A.not_equal, A.mult, 384, ["tI"], ["R3"])
    vts(T.dg[:], T.tI[:, 0:256], r_, None, A.is_equal, None, 256, ["tI", "c0"], ["dg"])
    vscan(T.pw[:], T.R3[:, 0:16], T.dg[:, 0:16], A.mult, A.add, 16, ["R3", "dg"], ["pw"])
    fill(col[:, 14:15], 0.1875, 1, ["c14"])
    vts(col[:, 12:13], r_, 4096.0, None, A.add, None, 1, ["c0"], ["c12"])
    vts(col[:, 13:14], r_, 4112.0, None, A.add, None, 1, ["c0"], ["c13"])
    iota(T.wc[:], [[0, NCH], [16, CH]], 0, 0, 256, ["wc"])
    iota(T.bcF[:, 0:16], [[16, 16]], 15, 0, 16, ["bc0"])
    iota(T.bcF[:, 16:48], [[1, 32]], 0, 0, 32, ["bc1"])
    for pi, (w0, w1) in enumerate(spans):
        iota(T.bcF[:, 48 + 3 * w0:48 + w0 + 2 * w1], [[16, 2 * (w1 - w0)]], 48 * w0 + 15, 0, 16, ["bc2%d" % pi])
        iota(T.bcF[:, 48 + w0 + 2 * w1:48 + 3 * w1], [[32, w1 - w0]], 48 * w0 + 31, 0, 8, ["bc3%d" % pi])
    vcp(T.bcU[:], T.bcF[:, 16:72], 56, ["bc1", "bc20", "bc21", "bc30", "bc31"], ["bcU"])
    vts(T.lC[:], T.bcF[:, 0:16], r_, -15.0, A.add, A.add, 16, ["bc0", "c0"], ["lC"])
    vts(T.vC[:, 0:16], T.lC[:], 1.0, None, A.add, None, 16, ["lC"], ["vC0"])
    for pi, (w0, w1) in enumerate(spans):
        vts(T.vC[:, 16 + 2 * w0:16 + 2 * w1], T.lC[:, 2 * w0:2 * w1], -2.0 - 32 * w0, None, A.add, None, 16, ["lC"], ["vC%d" % (pi + 1)])
    vts(T.jC[:, 0:4], T.lC[:, 0:4], 2.0, 1.0, A.mult, A.add, 4, ["lC"], ["jC0"])
    vts(T.jC[:, 4:8], T.lC[:, 0:4], -2.0, -1.0, A.mult, A.add, 4, ["lC"], ["jC1"])
    vts(T.jC[:, 8:12], T.lC[:, 0:4], 256.0, None, A.add, None, 4, ["lC"], ["jC2"])
    fill(T.ZT[:, 17:48:2], 1.0, 16, ["ZT2"])
    iota(T.ia[:, 4:5], [[0, 1]], 128, -1, 1, ["ia4"], False)
    vts(T.ia[:, 8:9], p_, 4, None, A.arith_shift_right, None, 1, ["io"], ["ia8"])
    vts(T.ia[:, 9:10], p_, 8, None, A.bitwise_and, None, 1, ["io"], ["ia9"])
    vtt(T.ia[:, 10:11], T.ia[:, 8:9], p_, A.add, 1, ["ia8", "io"], ["ia10"])
    vtt(T.ia[:, 11:12], T.ia[:, 8:9], T.ia[:, 4:5], A.add, 1, ["ia8", "ia4"], ["ia11"])
    vts(T.ia[:, 12:14], T.ia[:, 10:12], 7, None, A.bitwise_and, None, 2, ["ia10", "ia11"], ["ia12"])
    vcp(col[:, 7:8], T.ia[:, 9:10], 1, ["ia9"], ["c7"])
    vts(col[:, 8:10], T.ia[:, 12:14], col[:, 7:8], None, A.add, None, 2, ["ia12", "c7"], ["c8"])
    vts(col[:, 16:20:2], col[:, 8:10], 1.0, None, A.mult, None, 2, ["c8"], ["c16"])
    vts(col[:, 17:18], col[:, 8:9], 2.0, 16.0, A.mult, A.add, 1, ["c8"], ["c17"])
    vts(col[:, 19:20], col[:, 9:10], 1.0, 16.0, A.mult, A.add, 1, ["c8"], ["c19"])
    vcp(T.skU[:], col[:, 16:20], 4, ["c16", "c17", "c19"], ["skU"])
    fill(T.skW[:, 0:16], 1.0, 16, ["skW0"])
    fill(T.skW[:, 16:32], 32.0, 16, ["skW1"])
    gath("V", T.vD[:], T.vC[:], T.skU[:, 2:4], 32, ["skU", "vC0", "vC1", "vC2"], ["vD"])
    for j, nm in enumerate(("Id2a", "Id2b")):
        vts(T.Id2[:, 128 * j:128 * j + 128], T.Id[:], 1.0, None, A.mult, None, 128, ["Id"], [nm], half=True)
    fill(T.X[:, 4096:4128], 0.0, 32, ["Xd"])
    fill(T.mis[:, 256:272], 0.0, 16, ["misd"])
    vts(col[:, 15:16], r_, 16.0, -15.0, A.mult, A.add, 1, ["c0"], ["c15"])
    fill(T.KB[:, 256:320], 0.0, 64, ["Kd0"])
    for t in range(ST):
        fill(T.pkS[:, PKW * t + 128:PKW * t + 136], 0.0, 8, ["pkp%d" % t])
        fill(T.KB[:, KBW * t + 576:KBW * t + 640], 0.0, 64, ["Be%d" % t])
    for j in range(8):
        op("G", 720, lambda j=j: g.affine_select(T.SEL[:, 256 * j:256 * j + 256], T.ones[:], [[1, 2], [16, 8], [0, 16]], A.is_equal, 0.0, 2 * j, -1),
           ["ones"], ["SEL%d" % j])

    vts(T.aF[:, 0:16], T.avI[:], 0.0, 1.0 / AS, A.add, A.mult, 16, ["avI"], ["a0"])
    vts(T.s1[:], T.lC[:], 2.0, None, A.mult, None, 16, ["lC"], ["s1"])
    vcp(T.bU[:], T.bvI[:], 16, ["bvI"], ["bU"])
    vts(T.hJ[:, 0:16], T.bvI[:], 992, None, A.bitwise_and, None, 16, ["bvI"], ["hJ0"])
    vts(T.hJ[:, 16:32], T.bvI[:], 31, None, A.bitwise_and, None, 16, ["bvI"], ["hJ1"])
    vcp(T.hl[:], T.hJ[:], 32, ["hJ0", "hJ1"], ["hl"])
    for j in range(2):
        gtt(T.hm[:, 256 * j:256 * j + 256], T.hl[:, 0:32], T.bcU[:, 16 * j:16 + 16 * j], T.dg[:], A.mult, 256, ["hl", "bcU", "dg"], ["hm%d" % j])
    mm("hm", [(B[3][:, 0:256], DG("U64", 0), T.hm[:, 0:256], 256), (B[3][:, 0:256], DG("U64", 1), T.hm[:, 256:512], 256)],
       ["hm0", "hm1", "U64"], ["b3"], 3, True, True)
    act(T.KB[:, 320:576], B[3][:, 0:256], AF.Copy, 256, ["b3"], ["Bd0"], (3,), scale=1.0 / 64)
    cur[0] = 0
    vts(T.thF[:, 0:1], T.thI[:, 0:1], -1.0, -0.5, A.mult, A.add, 1, ["thI"], ["thF"])
    vcp(T.nth[:, 0:1], T.thF[:, 0:1], 1, ["thF"], ["nth"], nm="nth0")
    vcp(T.KB[:, 0:256], T.kcI[:], 256, ["kcI"], ["K0"], nm="n1")

    M32 = 1.5 * 2 ** 28
    M1 = 1.5 * 2 ** 23
    snd = {}

    def patch(t, tk, last):
        ko = KBW * tk
        own = PKW * t
        if last:
            o, m = T.pkS, T.pkM
            oR = lambda a: ["pk%s%d" % (a, t)]
            oE, oA = [], []
            mE, mA = [("rM%d" % t, NE)], [snd["P", t]]
            aE, aA = [("rA%d" % t, NE // 2), ("rO%d" % t, NE // 2)], [snd["A", t]]
            c1, c2 = T.pkA[:, 32 * t + 7:32 * t + 8], T.pkA[:, 32 * t + 15:32 * t + 16]
            kE, kA = [], []
        else:
            o, m = T.pkO, T.pkM
            oR = lambda a: []
            oE, oA = [("rO%d" % t, NE // 2)], [snd["P", t]]
            mE, mA = [("rM%d" % t, NE // 2)], [snd["P", t]]
            aE, aA = [("rA%d" % t, NE)] + oE, [snd["A", t]] + oA
            c1, c2 = T.pkA[:, 32 * t + 7:32 * t + 8], T.pkO[:, own + 143:own + 144]
            kE, kA = [("rK%d" % tk, NE)], [snd["K", t]]
        vts(T.n1[:, 0:1], T.pkS[:, own + 143:own + 144], c1, None, A.min, None, 1, ["pkA%d" % t], ["n1"], ext=aE[:1], after=aA[:1])
        vts(T.n2[:, 0:1], T.n1[:, 0:1], m[:, own + 143:own + 144], c2, A.min, A.min, 1, ["n1"], ["n2"], ext=mE + aE, after=mA + aA)
        vts(T.g1[:], T.jC[:, 0:4], T.n2[:, 0:1], 512.0, A.is_gt, A.mult, 4, ["jC0", "n2"], ["g1"])
        vtt(T.g2[:], T.g1[:], o[:, own + 128:own + 132], A.add, 4, ["g1"] + oR("p"), ["g2"], ext=oE, after=oA)
        vtt(T.g3[:], T.g2[:], T.jC[:, 8:12], A.min, 4, ["g2", "jC2"], ["g3"])
        vcp(T.spU[:], T.g3[:], 4, ["g3"], ["spU"])
        scat(T.KB[:, ko + 320:ko + 640], T.spU[:], m[:, own + 144:own + 208], 64, ["spU", "Be%d" % tk], ["Bd%d" % tk, "Be%d" % tk], ext=kE + mE, after=kA + mA, nm="scB")
        mm("pb", [(B[5][:, 288:304], DG("U64", j), T.KB[:, ko + 320 + j:ko + 576:16], 16) for j in range(16)], ["U64", "Bd%d" % tk], ["b5b"], 5, True, True)
        if last:
            act(T.bF[:], B[5][:, 288:304], AF.Copy, 16, ["b5b"], ["bF"], (5,), scale=1.0 / 64)
        else:
            vts(T.bU[:], B[5][:, 288:304], 1.0 / 64, None, A.mult, None, 16, ["b5b"], ["bU"], (5,))
        Ko, Km = o[:, own + 64:own + 128], m[:, own + 208:own + 272]
        for hb in range(2):
            bk = 3 + hb
            mm("po%d" % hb, [(B[bk][:, 64 * j:64 * j + 64], T.mId[:], Ko, 64) for j in range(8)], ["mId"] + oR("K"), ["b%d" % bk, "b%du" % bk], bk, True, False, ext=oE, after=oA)
            mm("pc%d" % hb, [(B[bk][:, 64 * j:64 * j + 64], T.SEL[:, 128 * (8 * hb + j):128 * (8 * hb + j) + 128], Km, 64) for j in range(8)],
               ["SEL%d" % j for j in range(8)], ["b%d" % bk], bk, False, True, ext=mE, after=mA)
            vts(T.CL[:, 512 * hb:512 * hb + 512], B[bk][:], -15.0, 1.0, A.max, A.min, 512, ["b%d" % bk], ["CL%d" % hb], (bk,))
        mm("ps0", [(B[6][:, 0:64], T.xId[:], Ko, 64)] + [(B[6][:, 0:64], T.Id[:], T.CL[:, 64 * j:64 * j + 64], 64) for j in range(8)],
           ["xId", "Id", "CL0"] + oR("K"), ["b6"], 6, True, False, ext=oE, after=oA)
        mm("ps1", [(B[6][:, 0:64], T.Id[:], T.CL[:, 64 * j:64 * j + 64], 64) for j in range(8, 16)], ["CL1"], ["b6"], 6, False, True)
        vtt(T.k1[:], B[6][:, 0:64], o[:, own:own + 64], A.mult, 64, ["b6"] + oR("M"), ["k1"], (6,), ext=oE, after=oA)
        op("V", 64 * par["sc"] + 50, lambda: V.tensor_tensor(T.KB[:, ko:ko + 320].indirect(T.spU[:]), T.k1[:], Ko, A.add),
           ["spU", "k1"] + oR("K"), ["K%d" % tk, "Kd%d" % tk], (), kE, kA, nm="scK")

    for t in range(ST):
        last = t == ST - 1
        cur[0] = t
        ko = KBW * t
        own = PKW * t
        K = T.KB[:, ko:ko + 256]
        z = T.zb[:, 256 * t:256 * t + 256]
        aF = T.aF[:, 16 * t:16 * t + 16]
        aR, zR = (["a0"], ["z0"]) if t == 0 else ([], [])
        aE, aA = ([], []) if t == 0 else ([("ra%d" % t, NE)], [snd["a", t - 1]])
        zE, zA = ([], []) if t == 0 else ([("rz%d" % t, NE)], [snd["z", t - 1]])
        vts(T.aU[:], aF, AS, None, A.mult, None, 16, aR, ["aU"], ext=aE, after=aA)
        gath("V", T.ra[:], T.P[:, 0:1024 * (t + 1)], T.aU[:], 256, ["P%d" % j for j in range(t + 1)] + ["aU"], ["ra"])
        act(T.a5[:], aF, AF.Copy, 16, aR, ["a5"], scale=4.0 * AS, ext=aE, after=aA)
        phrases("x", "ra", 0, par["xs"] if t else par["xs0"])
        if t > 0:
            patch(t - 1, t, False)
        Kt, Bt = "K%d" % t, "Bd%d" % t
        if not last:
            snd["K", t] = send("toK", [(1, T.KB[:, ko:ko + 576], T.KB[:, ko + KBW:ko + KBW + 576], "rK%d" % (t + 1))], [Kt, Bt, "Kd%d" % t], par["lat"] + 2500)
        gath("S", T.rb[:], T.P[:, 0:1024], T.bU[:], 256, ["P0", "bU"], ["rb"])
        mm("pw", [(B[6][:, 256:512], T.Id[:], T.wc[:], 256), (B[6][:, 256:512], T.Id[:], K, 256)], ["Id", "wc", Kt], ["b6c"], 6, True, True)
        vcp(T.wo[:], B[6][:, 256:512], 256, ["b6c"], ["wo"], (6,))
        vts(T.rb16[:], T.rb[:], -2048.0, None, A.add, None, 256, ["rb"], ["rb16"], half=True)
        phrases("y", "rb", 4096, par["ys"])
        terms = []
        mm("pz", [(B[2][:, 0:256], T.Id[:], z, 256)], ["Id"] + zR, ["b2"], 2, True, True, zE, zA)
        mm("kz", [(B[1][:, 128 * h:128 * h + 128], T.zb[:, 256 * t + 128 * h:256 * t + 128 * h + 128], T.ZC[:], 128) for h in range(2)],
           ["ZC"] + zR, ["b1", "b1s"], 1, True, False, zE, zA)
        for k in range(0, KV, 2):
            mm("kx%d" % k, [(B[1][:, 128 * h + j:128 * h + 128:16], T.XY[:, 2048 * h + j:2048 * h + 2048:16], T.Un32[:, 15:143:16], 8) for j in (k, k + 1) for h in range(2)],
               ["Un32", "b1s"] + allx, ["kx%d" % k], None, False, False)
            terms.append("kx%d" % k)
        for k in range(0, 16, 2):
            if k < KV:
                for j in (k, k + 1):
                    vtt(T.MX[:, 256 * j:256 * j + 256], T.XY[:, j:4096:16], B[2][:, 0:256], A.max, 256, allx + ["b2"], ["mx%d" % j], (2,))
            else:
                bk = par["rows"][(k - KV) // 2 % len(par["rows"])]
                mm("pm%d" % k, [(B[bk][:, 256 * j:256 * j + 256], w, r, 256) for j in (0, 1) for w, r in ((T.nId[:], z), (T.Id[:], T.XY[:, k + j:4096:16]))],
                   zR + allx + ["Id", "nId"], ["b%d" % bk, "b%db" % bk, "b%du" % bk], bk, True, True, zE, zA)
                act(T.MX[:, 256 * k:256 * k + 512], B[bk][:], AF.Abs, 512, ["b%d" % bk, "b%db" % bk], ["mx%d" % k, "mx%d" % (k + 1)], (bk,), scale=0.5)
            mm("km%d" % k, [(B[1][:, 128 * h + j:128 * h + 128:16], T.MX[:, 256 * j + 128 * h:256 * j + 128 * h + 128], T.U64[:, 15:143:16], 8) for j in (k, k + 1) for h in range(2)],
               ["U64", "b1s", "mx%d" % k, "mx%d" % (k + 1)], ["km%d" % k], None, False, False)
            terms.append("km%d" % k)
        mm("kB", [(B[1][:, 128 * h:128 * h + 128], T.KB[:, ko + 128 * h:ko + 128 * h + 128], T.sId[:], 128) for h in range(2)], ["sId", Kt] + terms, ["b1"], 1, False, True)
        vscan(T.kS[:], T.R1[:], B[1][:, 0:256], A.add, A.min, 256, ["R1", "b1"], ["kS"], (1,))
        if not last:
            dma("Y", T.P[:, 1024 * (t + 1):1024 * (t + 2)], T.P[:, 0:1024], ["P0", "mx14"], ["P%d" % (t + 1)], "cp%d" % t, 3000, "cp")
        k16 = T.kS[:, 15:256:16]
        vts(T.r16[:], k16, M32, M32, A.add, A.subtract, 16, ["kS"], ["r16"])
        vts(T.low[:], k16, M1, M1 + 1, A.add, A.subtract, 16, ["kS"], ["low"])
        vtt(T.ZT[:, 0:16], T.low[:], T.r16[:], A.subtract, 16, ["low", "r16"], ["ZT0"])
        vtt(T.ZT[:, 16:48:2], k16, T.low[:], A.subtract, 16, ["kS", "low"], ["ZT1"])
        gtt(T.SK[:], T.ZT[:], T.skU[:, 0:2], T.skW[:], A.mult, 32, ["ZT0", "ZT1", "ZT2", "skU", "skW0", "skW1"], ["SK"])
        mm("pv", [(B[5][:, 256:288], T.tId[:], T.vD[:], 32)] + [(B[5][:, 256 + j:288:8], T.Id2[:, 128 - 16 * j:256 - 16 * j], T.SK[:, j:32:8], 4) for j in range(8)],
           ["SK", "Id2a", "Id2b", "tId", "vD"], ["b5v"], 5, True, True)
        vcp(T.vF[:], B[5][:, 256:288], 32, ["b5v"], ["vF"], (5,))
        gath("V", T.vU[:], T.vF[:], T.skU[:, 2:4], 32, ["vF", "skU"], ["vU"])
        mm("pZ", [(B[3][0:16, 256 + 128 * h:384 + 128 * h], T.ZT[:, 16 + 16 * h:32 + 16 * h], T.Id[:], 128) for h in range(2)], ["ZT1", "ZT2", "Id"], ["b3u"], 3, True, True)
        vcp(T.ZB[0:16], B[3][0:16, 256:512], 256, ["b3u"], ["ZB"], (3,))
        mm("pt", [(B[3][:, 0:256], T.I16[:], T.rb16[:], 256), (B[3][:, 0:256], T.WT[0:16, :], T.ZB[0:16], 256)], ["I16", "rb16", "WT", "ZB"], ["b3"], 3, True, True)
        vts(T.T16[:], B[3][:, 0:256], -2048.0, 2048.0, A.max, A.min, 256, ["b3"], ["T16"], (3,))

        def both(w, src, p):
            return [m for w0, w1 in spans for m in ((B[4][:, 48 * w0:16 * w0 + 32 * w1], w, src[0:p, w0:w1, :], 32 * (w1 - w0)),
                                                    (B[4][:, 16 * w0 + 32 * w1:48 * w1], w, src[0:p, w0:w1, 0:16], 16 * (w1 - w0)))]
        mm("pA", [(B[4][:, 48 * w0:16 * w0 + 32 * w1], T.Id[:], T.tri[:, 0:32 * (w1 - w0)], 32 * (w1 - w0)) for w0, w1 in spans] + both(T.WC[0:16, :], T.ZB, 16),
           ["Id", "tri", "WC", "ZB"], ["b4"], 4, True, False)
        mm("pc", both(T.BO16[:], T.T16, 128), ["BO16", "T16"], ["b4"], 4, False, True)
        for pi, (w0, w1) in enumerate(spans):
            e0, n = 48 * w0, 32 * (w1 - w0)
            vscan(T.cS[:, e0:e0 + n], T.R2[:, 0:n], B[4][:, e0:e0 + n], A.add, A.min, n, ["R2", "b4"], ["cS%d" % pi], (4,))
        act(T.cR[:], B[4][:, 0:384], AF.Copy, 384, ["b4"], ["cR"], (4,))
        gtt(T.eq[:], T.cS[:], T.bcU[:, 32:56], T.cR[:], A.not_equal, 384, ["cS0", "cS1", "cSx0", "cSx1", "cR", "bcU"], ["eq"])
        gath("S", T.xw[:, 0:256], T.XY[:, 0:4096], T.vU[:, 0:16], 256, ["vU"] + allx, ["xk"])
        for pi, (w0, w1) in enumerate(spans):
            a0, a1 = 32 * w0, 32 * w1
            gath("S", T.xw[:, 256 + a0:256 + a1], T.XY[:, 4096 + 16 * a0:4096 + 16 * a1], T.vU[:, 16 + 2 * w0:16 + 2 * w1], a1 - a0,
                 ["vU"] + ally[2 * w0:2 * w1], ["wk%d" % pi])
            mm("ph%d" % pi, [(B[6][:, a0:a1], T.hId[:], T.xw[:, a0:a1], a1 - a0), (B[6][:, a0:a1], T.hId[:], T.xw[:, 256 + a0:256 + a1], a1 - a0)],
               ["hId", "xk", "wk%d" % pi], ["b6"], 6, True, True)
            vts(T.half[:, a0:a1], B[6][:, a0:a1], M1, M1, A.add, A.subtract, a1 - a0, ["b6"], ["half%d" % pi], (6,))
        mm("pn", [(B[5][:, 0:256], T.Id[:], z, 256), (B[5][:, 0:256], T.nId[:], T.xw[:, 256:512], 256)], ["Id", "nId", "wk0", "wk1"] + zR, ["b5"], 5, True, True)
        act(T.ZW[:, 0:512:2], B[5][:, 0:256], AF.Abs, 256, ["b5"], ["zm"], (5,))
        mm("pe", [(B[3][:, 256:512], T.tId[:], T.tri[:], 256)], ["tId", "tri"], ["b3u"], 3, True, False)
        mm("pu", [(B[3][:, 256:512], T.Wu[:], T.ZW[:, 0:512:2], 256)], ["Wu", "zm"], ["b3u"], 3, False, True)
        vscan(T.kS[:], T.R2[:], B[3][:, 256:512], A.add, A.min, 256, ["R2", "b3u"], ["kS"], (3,), nm="uS")
        vtt(T.amI[:], T.kS[:, 15:256:16], T.a5[:], A.add, 16, ["kS", "a5"], ["amI"])
        vts(T.amJ[:], T.amI[:], 1023, None, A.bitwise_and, None, 16, ["amI"], ["amJ"])
        vts(T.da[:], T.amJ[:], 1.0 / AS, None, A.mult, None, 16, ["amJ"], ["da"])

        for pi, cs in enumerate(par["parts"]):
            bk, off, key = ((0, 0, "b0"), (2, 256, "b2b"))[pi]
            nb, s0, nk = ((7, 0, "b7"), (1, 256, "b1q"))[pi]
            w0, w1 = spans[pi]
            a0, a1, q0, q1, e0, e1 = 32 * w0, 32 * w1, 2 * w0, 2 * w1, 48 * w0, 48 * w1
            n, n3, s = a1 - a0, e1 - e0, "_%d" % pi
            for c in cs:
                lo, hi, ns = 16 * CH * c, 16 * CH * (c + 1), par["subs"][c]
                for j in range(ns):
                    l0, l1 = CH * c + CH // ns * j, CH * c + CH // ns * (j + 1)
                    gtt(T.DF[:, 16 * l0:16 * l1], T.XY[:, 4096 + lo:4096 + hi], T.wo[:, l0:l1], T.XY[:, 16 * l0:16 * l1], A.subtract, 16 * CH // ns,
                        allx[l0 // 16:l1 // 16] + ally[4 * c:4 * c + 4] + ["wo"], ["df%d_%d" % (c, j)])
                dfs = ["df%d_%d" % (c, j) for j in range(ns)]
                out = B[bk][:, off + CH * c:off + CH * (c + 1)]
                relu = c in par["rv"]
                if relu:
                    for h in range(2):
                        mm("dl%d_%d" % (c, h), [(out, DG("Un32", k), T.DF[:, lo + k:hi:16], CH) for k in range(8 * h, 8 * h + 8)], ["Un32"] + dfs, [key], bk,
                           c == cs[0] and h == 0, False)
                    vts(T.AB[:, lo:hi], T.DF[:, lo:hi], 0.0, None, A.max, None, 16 * CH, dfs, ["ab%d" % c], half=True)
                else:
                    act(T.AB[:, lo:hi], T.DF[:, lo:hi], AF.Abs, 16 * CH, dfs, ["ab%d" % c], scale=0.5)
                for h in range(2):
                    mm("da%d_%d" % (c, h), [(out, DG("U64", k), T.AB[:, lo + k:hi:16], CH) for k in range(8 * h, 8 * h + 8)], ["U64", "ab%d" % c], [key], bk,
                       c == cs[0] and h == 0 and not relu, c == cs[-1] and h == 1)
            mm("n0" + s, [(B[nb][:, s0:s0 + n3], T.Id[:], T.cmk[:, e0:e1], n3)], ["Id", "cmk" + s, "cmj" + s], [nk], nb, True, False)
            act(T.mis[:, a0:a1], B[bk][:, off + a0:off + a1], AF.Sign, n, [key, "nth"], ["mis%d" % pi], (bk,), bias=T.nth[:, 0:1], scale=1.0 / 32)
            mm("n1" + s, [(B[nb][:, s0:s0 + n], T.BOs[:], T.mis[:, a0:a1], n)] +
               [(B[nb][:, s0 + n + 16 * j:s0 + n + 16 * j + 16], T.BOs[:], T.mis[:, a0 + 32 * j:a0 + 32 * j + 16], 16) for j in range(w1 - w0)],
               ["BOs", "mis%d" % pi], [nk], nb, False, True)
            vscan(T.nS[:, a0:a1], T.t01[:, a0:a1], B[nb][:, s0:s0 + n], A.mult, A.max, n, ["t01", nk], ["nS%d" % pi], (nb,))
            if pi == 1:
                vts(T.dl[:], T.nS[:, 15:256:16], 0.0, None, A.is_le, None, 16, ["nS0", "nS1"], ["dl"])
                vtt(T.t2[:], T.nS[:, 15:256:16], T.da[:], A.min, 16, ["nS0", "nS1", "da"], ["t2"])
                aS = T.aS[:, 16 * t:16 * t + 16]
                vtt(aS, T.t2[:], aF, A.add, 16, ["t2", "aU"], ["aS%d" % t], nm="aS")
                if not last:
                    snd["a", t] = send("toa", [(1, aS, T.aF[:, 16 * t + 16:16 * t + 32], "ra%d" % (t + 1))], ["aS%d" % t], par["lat"])
                else:
                    cur[0] = ST
                    vts(T.amI[:], aS, AS, None, A.mult, None, 16, ["aS%d" % t], ["amI"], nm="aI")
                    vts(T.amJ[:], T.amI[:], 1023, None, A.bitwise_and, None, 16, ["amI"], ["amJ"], nm="aJ")
                    vcp(T.a5[:], T.amJ[:], 16, ["amJ"], ["a5"], nm="aK")
                    dma("Y", T.ya[:], T.a5[:], ["a5"], [], "out", 2500, "oa")
                    cur[0] = t
            vtt(T.cm[:, e0:e1], T.eq[:, e0:e1], B[nb][:, s0:s0 + n3], A.is_lt, n3, ["eq", nk], ["cm" + s], (nb,))
            vscan(T.bS[:, e0:e1], T.R3[:, 0:n3], T.cm[:, e0:e1], A.mult, A.add, n3, ["R3", "cm" + s], ["bS" + s])
            vts(T.f1[:, q0:q1:2], T.bS[:, e0 + 15:e0 + n:32], T.pw[:, 15:16], col[:, 12:13], A.not_equal, A.mult, 8, ["bS" + s, "pw", "c12"], ["f0" + s])
            vts(T.f3[:, w0:w1], T.bS[:, e0 + 31:e0 + n:32], T.pw[:, 15:16], col[:, 13:14], A.not_equal, A.mult, 8, ["bS" + s, "pw", "c13"], ["f3" + s])
            vts(T.f3[:, 8 + w0:8 + w1], T.bS[:, e0 + n + 15:e1:16], 0.0, col[:, 13:14], A.is_gt, A.mult, 8, ["bS" + s, "c13"], ["f4" + s])
            vtt(T.f1[:, q0 + 1:q1:2], T.f3[:, w0:w1], T.f3[:, 8 + w0:8 + w1], A.max, 8, ["f3" + s, "f4" + s], ["f1" + s])
            vtt(T.f2[:, q0:q1], T.f1[:, q0:q1], T.cS[:, e0 + 15:e0 + n:16], A.max, 16, ["f0" + s, "f1" + s, "cS%d" % pi], ["f2" + s])
            vcp(T.offU[:, q0:q1], T.f2[:, q0:q1], 16, ["f2" + s], ["offU" + s])
            for w in range(w1 - 1, w0 - 1, -1):
                scat(T.X[:], T.offU[:, 2 * w:2 * w + 2], T.half[:, 32 * w:32 * w + 32], 32, ["offU" + s, "half%d" % pi], Xr, nm="sx%d" % w)
        miss = ["mis0", "mis1"]
        mm("pq", [(B[0][:, 256:512], T.BOs[:], T.mis[:, 0:256], 256)], ["BOs"] + miss, ["b0b"], 0, True, True)
        act(T.dvS[:], B[0][:, 256:512], AF.Sign, 256, ["b0b", "c14"], ["dvS"], (0,), bias=col[:, 14:15], scale=-1.0)
        vscan(T.pref[:], T.ones[:], T.dvS[:], A.add, A.add, 256, ["ones", "dvS"], ["pref"], half=True)
        for j in range(4):
            act(T.junk[:, 256 * j:256 * j + 256], T.pref[:], AF.Sign, 256, ["pref", "jC1"], ["junk%d" % j, "acc%d" % j], bias=T.jC[:, 4 + j:5 + j], accum=T.acc[:, j:j + 1])
        mm("pd", [(B[2][:, 0:256], T.hId[:], z, 256), (B[2][:, 0:256], T.hId[:], T.XY[:, 0:4096:16], 256)], ["hId"] + allx + zR, ["b2"], 2, True, True, zE, zA)
        act(T.kT[:], B[2][:, 0:256], AF.Copy, 256, ["b2"], ["kT"], (2,), bias=M1, nm="zc")
        act(T.ZW[:, 1:512:2], T.kT[:], AF.Copy, 256, ["kT"], ["zd"], bias=-M1)
        src = T.pkS[:, own + 136:own + 144]
        act(src, T.pref[:, 248:256], AF.Copy, 8, ["pref"], ["pkA%d" % t], nm="pkA")
        if not last:
            snd["A", t] = send("toA", [(2, src, T.pkA[:, 32 * t:32 * t + 8], "rA%d" % t)], ["pkA%d" % t], par["lat"])
        else:
            snd["A", t] = send("toA", [(1, src, T.pkA[:, 32 * t:32 * t + 8], "rA%d" % t), (3, src, T.pkA[:, 32 * t + 8:32 * t + 16], "rO%d" % t)], ["pkA%d" % t], par["lat"] + 600)
        accs = ["acc%d" % j for j in range(4)]
        vts(T.posU[:], T.acc[:], -0.5, 128.0, A.mult, A.add, 4, accs, ["posU"])
        act(T.pkS[:, own + 128:own + 132], T.acc[:], AF.Copy, 4, accs, ["pkp%d" % t], bias=128.0, scale=-0.5, nm="pkp")
        gath(par["pk"][0], T.pkS[:, own + 64:own + 128], T.KB[:, ko:ko + 320], T.posU[:], 64, ["posU", Kt, "Kd%d" % t], ["pkK%d" % t], nm="pkK")
        gath(par["pk"][1], T.pkS[:, own + 144:own + 208], T.KB[:, ko + 320:ko + 640], T.posU[:], 64, ["posU", Bt, "Be%d" % t], ["pkB%d" % t], nm="pkB")
        act(T.pkS[:, own + 208:own + 272], T.KB[:, ko:ko + 320].indirect(T.posU[:]), AF.Identity, 64, ["posU", Kt, "Kd%d" % t, "c15"], ["pkL%d" % t],
            bias=col[:, 15:16], gather=True, nm="pkL")
        act(T.pkS[:, own:own + 64], T.mis[:].indirect(T.posU[:]), AF.Copy, 64, ["posU", "misd"] + miss, ["pkM%d" % t], bias=0.5, scale=0.5, gather=True, nm="pkM")
        sO, sM = T.pkS[:, own:own + 144], T.pkS[:, own + 128:own + 272]
        pkR = ["pk%s%d" % (a, t) for a in ("BLpA" if last else "KMBLpA")]
        if not last:
            snd["P", t] = send("toP", [(1, sO, T.pkO[:, own:own + 144], "rO%d" % t), (3, sM, T.pkM[:, own + 128:own + 272], "rM%d" % t)], pkR, par["lat"] + 800)
        else:
            snd["P", t] = send("toP", [(2, sM, T.pkM[:, own + 128:own + 272], "rM%d" % t)], pkR, par["lat"] + 300)
        vtt(T.s2[:], T.s1[:], T.dl[:], A.add, 16, ["s1", "dl"], ["s2"])
        vcp(T.slU[:], T.s2[:], 16, ["s2"], ["slU"])
        zS = T.zS[:, 256 * t:256 * t + 256]
        gath("S", zS, T.ZW[:], T.slU[:], 256, ["slU", "zm", "zd"], ["zS%d" % t], nm="zS")
        if not last:
            snd["z", t] = send("toz", [(1, zS, T.zb[:, 256 * t + 256:256 * t + 512], "rz%d" % (t + 1))], ["zS%d" % t], par["lat"] + 600)
            vts(T.AI[:, 0:1], T.pref[:, 255:256], 0.5, None, A.mult, None, 1, ["pref"], ["AI"])
            vts(T.AI[:, 1:2], T.AI[:, 0:1], 31, None, A.bitwise_and, None, 1, ["AI"], ["AJ"])
            vtt(T.nth[:, 0:1], T.thF[:, 0:1], T.AI[:, 1:2], A.subtract, 1, ["thF", "AJ"], ["nth"])
        else:
            dma("Y", T.yz[:], zS, ["zS%d" % t], [], "out", 2500, "oz")
            dma("Y", T.yx[:], T.X[:, 0:4096], Xr, [], "out", 7500, "ox")
            cur[0] = ST
            patch(t, t, True)
            dma("S", T.yk[:], K, [Kt], [], "out", 2500, "ok")
            dma("S", T.yb[:], T.bF[:], ["bF"], [], "out", 2500, "ob")
    return ops, nsent[0]


def first_calls(ops, par):
    n, hop = len(ops), par["hop"]
    eng = [o["e"] for o in ops]
    cost = [o["alts"][o["e"]][0] for o in ops]
    succ = [[] for _ in range(n)]
    for i, o in enumerate(ops):
        for d in o["deps"]:
            succ[d].append(i)
    place = {nm.lstrip("+"): 900.0 * j / len(q) + (1000 if nm[0] == "+" else 0) for q in par["queues"].values() for j, nm in enumerate(q)}
    pr = [0.0] * n
    for i in range(n - 1, -1, -1):
        o = ops[i]
        if o["t"] == 0 and o["nm"] in par["first"]:
            pr[i] = 5000.0 - par["first"].index(o["nm"])
        elif o["t"] >= 0 and o["nm"] in place:
            pr[i] = -1000.0 * o["t"] - place[o["nm"]]
        elif o["nm"] == "dma":
            pr[i] = 1e9 - i
        else:
            pr[i] = max([pr[s] + (2000.0 if ops[s]["t"] >= 0 and o["t"] < 0 else 0) for s in succ[i]] + [-1e9]) + 1e-7 * (cost[i] + o["lat"] + hop)
    left = [len(o["deps"]) for o in ops]
    rd, en = [0.0] * n, [0.0] * n
    cand = {e: [i for i in range(n) if left[i] == 0 and eng[i] == e] for e in "VSPGY"}
    free = dict.fromkeys(cand, 0.0)
    order = []
    while len(order) < n:
        now, e = min((max(free[e], min(rd[i] for i in q)), j, e) for j, (e, q) in enumerate(cand.items()) if q)[::2]
        b = max((i for i in cand[e] if rd[i] <= now + par["near"]), key=lambda i: pr[i])
        if rd[b] > now:
            short = [i for i in cand[e] if rd[i] <= now and cost[i] <= rd[b] - now + par["slack"]]
            if short:
                b = max(short, key=lambda i: pr[i])
        free[e] = max(now, rd[b]) + cost[b]
        en[b] = free[e] + ops[b]["lat"]
        cand[e].remove(b)
        order.append(b)
        for j in succ[b]:
            left[j] -= 1
            if left[j] == 0:
                rd[j] = max(en[d] + (0 if eng[d] == eng[j] and ops[d]["lat"] == 0 and (k == "bank" or eng[j] == "P") else hop) for d, k in ops[j]["deps"].items())
                cand[eng[j]].append(j)
    later = set(x[1:] for q in par["queues"].values() for x in q if x[0] == "+")
    return {e: [i for i in order if eng[i] == e and (ops[i]["t"] < 0 or ops[i]["t"] == 0 and ops[i]["nm"] not in later)] for e in "VSPGY"}, eng


def schedule(ops, par):
    seq, eng = first_calls(ops, par)
    at = {}
    for i, o in enumerate(ops):
        at.setdefault((o["nm"], o["t"], eng[i]), []).append(i)
    for e in seq:
        for t in range(1, ST + 1):
            for x in par["queues"][e]:
                k = (x[1:], t - 1, e) if x[0] == "+" else (x, t, e)
                if k[1] < ST - 1 or k[1] == ST - 1 and ("+" + k[0]) not in par["last"][e]:
                    seq[e] += at.get(k, [])
        for x in par["last"][e]:
            seq[e] += at[(x[1:], ST - 1, e) if x[0] == "+" else (x, ST, e)]
    done, order, pos = set(), [], dict.fromkeys(seq, 0)
    while len(order) < len(ops):
        before = len(order)
        for e, s in seq.items():
            while pos[e] < len(s) and all(d in done for d in ops[s[pos[e]]]["deps"]):
                done.add(s[pos[e]])
                order.append(s[pos[e]])
                pos[e] += 1
        assert len(order) > before
    return order, eng


def rank_program(g, core, T, topo):
    if T.rank_of(core) is None:
        return
    ops, nsent = build(g, core, T, topo, PAR)
    order, eng = schedule(ops, PAR)
    Q = {"V": g.vector, "S": g.scalar, "P": g.tensor, "G": g, "Y": g.sync}
    cnt = {"out": 0}
    mark = {}
    seen = {e: {} for e in Q}
    allw = {}
    need = set()
    for i, o in enumerate(ops):
        for d, kind in o["deps"].items():
            if kind == "far" or ops[d]["sem"] == "none":
                continue
            if eng[d] == eng[i] and ops[d]["sem"] is None and (kind == "bank" or eng[i] == "P"):
                continue
            need.add((d, i))
    raises = set(d for d, i in need)
    for i in order:
        o, e = ops[i], eng[i]
        waits = {}
        for d in o["deps"]:
            if (d, i) in need:
                s, v = mark[d]
                waits[s] = max(waits.get(s, 0), v)
        for s, v in o["ext"]:
            waits[s] = max(waits.get(s, 0), v)
        for s, v in waits.items():
            if seen[e].get(s, 0) < v:
                Q[e].wait_ge(T.sem[s], v)
                seen[e][s] = v
                allw[s] = max(allw.get(s, 0), v)
        r = o["alts"][e][1]()
        if o["sem"] == "none":
            continue
        if o["sem"] is not None:
            s = o["sem"]
        elif i in raises:
            s = "s" + e
        else:
            continue
        r.then_inc(T.sem[s], o["semn"])
        cnt[s] = cnt.get(s, 0) + o["semn"]
        mark[i] = (s, cnt[s])
    g.wait_ge(T.sem.sent, nsent)
    for s, v in cnt.items():
        if allw.get(s, 0) < v:
            g.wait_ge(T.sem[s], v)
